import numpy as np
import ml_dtypes


def mxq(x, axis, fmt="e4m3"):
    dtype, down = {"e4m3": (ml_dtypes.float8_e4m3fn, 7), "e5m2": (ml_dtypes.float8_e5m2, 14)}[fmt]
    v = np.moveaxis(np.asarray(x, np.float32).astype(ml_dtypes.bfloat16).astype(np.float64), axis, -1)
    blocks = v.reshape(v.shape[:-1] + (-1, 32))
    amax = np.abs(blocks).max(-1, keepdims=True)
    byte = np.maximum(np.where(amax > 0, np.frexp(amax)[1] - 1 + 127, 0) - down, 1)
    scale = np.exp2(byte - 127.0)
    codes = (blocks / scale).astype(np.float32).astype(dtype).astype(np.float64)
    return np.moveaxis((codes * scale).reshape(v.shape), -1, axis)


WIDE = False


def mx_kscale(k):
    if not WIDE:
        return np.ones(k)
    levels = np.array([10, -10, 5, -5, 0])
    if k % 512:
        return np.exp2(np.random.permutation(np.resize(levels, k // 32))).repeat(32)
    a = np.empty((k // 512, 16))
    for p in range(k // 512):
        a[p, :8] = np.random.permutation(np.resize(levels, 8))
        for g in range(8):
            far = levels[np.abs(levels - a[p, g]) >= 10]
            a[p, g + 8] = far[np.random.randint(len(far))]
    return np.exp2(a.ravel()).repeat(32)


def f64(x):
    return np.asarray(x).astype(np.float64)


def striped(idx):
    return np.tile(idx.reshape(-1, 16).T, (8, 1)).astype(np.uint16)


def unstriped(offs):
    return offs[:16].T.reshape(-1).astype(np.int64)


E2M1 = np.array([0.0, 0.5, 1.0, 1.5, 2.0, 3.0, 4.0, 6.0, -0.0, -0.5, -1.0, -1.5, -2.0, -3.0, -4.0, -6.0])


def pack_weight(w, fmt):
    k, n = w.shape
    w = f64(np.asarray(w, np.float32).astype(ml_dtypes.bfloat16)).reshape(k // 32, 32, n)
    amax = np.abs(w).max(1)
    if fmt == "e4m3":
        byte = np.frexp(amax)[1] - 1 + 127 - 7
    else:
        mant, ex = np.frexp(amax / 6.0)
        byte = np.where(mant > 0.5, ex, ex - 1) + 127
    byte = np.clip(np.where(amax > 0, byte, 1), 1, 254)
    scaled = (w * np.exp2(127.0 - byte)[:, None, :]).reshape(k, n).astype(np.float32)
    by_word = np.ascontiguousarray(scaled.reshape(k // 512, 128, 4, n).transpose(0, 1, 3, 2))
    if fmt == "e4m3":
        words = by_word.astype(ml_dtypes.float8_e4m3fn).view(np.uint8)
    else:
        c = by_word.astype(ml_dtypes.float4_e2m1fn).view(np.uint8) & 0xF
        words = (c[..., 0::2] | (c[..., 1::2] << 4)).reshape(k // 512, 128, 2 * n)
    return np.ascontiguousarray(words), np.ascontiguousarray(byte.astype(np.uint8).reshape(k // 512, 16, n))


def unpack_weight(words, scales, fmt):
    g, _, n = scales.shape
    words = np.ascontiguousarray(words).reshape(g, 128, n, -1)
    if fmt == "e4m3":
        vals = words.view(ml_dtypes.float8_e4m3fn).astype(np.float64)
    else:
        nib = np.empty((g, 128, n, 4), np.uint8)
        nib[..., 0::2] = words & 0xF
        nib[..., 1::2] = words >> 4
        vals = E2M1[nib]
    vals = vals * np.repeat(np.exp2(scales.astype(np.float64) - 127.0), 8, axis=1)[..., None]
    return vals.transpose(0, 1, 3, 2).reshape(g * 512, n)


def gelu(v):
    return 0.5 * v * (1.0 + np.tanh(np.sqrt(2.0 / np.pi) * (v + 0.044715 * v**3)))


K, T, S, H, N = 1024, 2048, 1024, 512, 512


def setup_inputs():
    n = np.random.standard_normal
    s = mx_kscale(K)[:, None]
    u = mx_kscale(H)[:, None]
    tab_words, tab_scales = pack_weight(n((K, T)) * s, "e4m3")
    w1 = n((K, H)) / np.sqrt(K) / s * u.T
    w4_words, w4_scales = pack_weight(n((K, H)) / np.sqrt(K) / s * u.T, "e2m1")
    w8_words, w8_scales = pack_weight(n((K, H)) / np.sqrt(K) / s * u.T, "e4m3")
    wd = n((H, N)) / np.sqrt(H) / u
    return {
        "tab_words": tab_words, "tab_scales": tab_scales,
        "offs": striped(np.random.permutation(T)[:S]),
        "offs2": striped(np.random.permutation(T)[:S]),
        "offs3": striped(np.random.permutation(T)[:S]),
        "w1": w1.astype(np.float32),
        "w4_words": w4_words, "w4_scales": w4_scales,
        "w8_words": w8_words, "w8_scales": w8_scales,
        "wd": wd.astype(np.float32),
    }


def reference(tab_words, tab_scales, offs, offs2, offs3, w1, w4_words, w4_scales, w8_words, w8_scales, wd):
    past = unpack_weight(tab_words, tab_scales, "e4m3")[:, unstriped(offs)]
    now = unpack_weight(tab_words, tab_scales, "e4m3")[:, unstriped(offs2)]
    future = unpack_weight(tab_words, tab_scales, "e4m3")[:, unstriped(offs3)]
    a = mxq(f64(w1), 0, "e4m3").T @ past
    b = unpack_weight(w4_words, w4_scales, "e2m1").T @ now
    c = unpack_weight(w8_words, w8_scales, "e4m3").T @ future
    h = np.abs(a - b) - np.abs(b - c)
    return mxq(f64(wd), 0, "e4m3").T @ mxq(h, 0, "e4m3")

@@ -1,0 +1,239 @@
+from contextlib import ExitStack
+
+import concourse.mybir as mybir
+from concourse.masks import make_identity
+
+K, T, S, H, N = 1024, 2048, 1024, 512, 512
+FLOPS = 2 * S * (3 * K * H + H * N)
+
+F32 = mybir.dt.float32
+BF16 = mybir.dt.bfloat16
+I32 = mybir.dt.int32
+U32 = mybir.dt.uint32
+U16 = mybir.dt.uint16
+U8 = mybir.dt.uint8
+FP8X4 = mybir.dt.float8_e4m3fn_x4
+FP4X4 = mybir.dt.float4_e2m1fn_x4
+ACT = mybir.ActivationFunctionType
+ALU = mybir.AluOpType
+
+P = 128
+PASSES = K // 512
+TILES = S // P
+PAIR = 2 * P
+
+
+def tile_list_patch_motion_acceleration_kernel(
+    tc, tab_words, tab_scales, offs, offs2, offs3, w1, w4_words, w4_scales, w8_words, w8_scales, wd, out
+):
+    nc = tc.nc
+    with ExitStack() as ctx:
+        keep = ctx.enter_context(tc.tile_pool(name="keep", bufs=1))
+        ring = ctx.enter_context(tc.tile_pool(name="ring", bufs=3))
+        psum = ctx.enter_context(tc.psum_pool(name="psum", bufs=1))
+
+        list_past = keep.tile([P, S // 16], U16, name="list_past")
+        list_now = keep.tile([P, S // 16], U16, name="list_now")
+        list_future = keep.tile([P, S // 16], U16, name="list_future")
+        tab_w = keep.tile([P, PASSES, T], I32, name="tab_w", align_bytes=64)
+        tab_s = keep.tile([P, T], U8, name="tab_s", align_bytes=64)
+        now_s1 = keep.tile([P, S], U8, name="now_s1", align_bytes=64)
+        w4_w = keep.tile([P, PASSES, 2 * H], U8, name="w4_w", align_bytes=64)
+        w8_w = keep.tile([P, PASSES, H], I32, name="w8_w", align_bytes=64)
+        w4_s = keep.tile([P, PASSES, H], U8, name="w4_s", align_bytes=64)
+        w8_s = keep.tile([P, H], U8, name="w8_s", align_bytes=64)
+        ident = keep.tile([P, P], F32, name="ident", align_bytes=64)
+
+        nc.gpsimd.memset(tab_s[:].bitcast(I32), 0)
+        nc.vector.memset(w8_s[:].bitcast(I32), 0)
+        nc.vector.memset(w4_s[:].bitcast(I32), 0)
+        nc.vector.memset(now_s1[:].bitcast(I32), 0)
+
+        nc.sync.dma_start(list_now[:], offs2)
+        nc.sync.dma_start(list_future[:], offs3)
+        for q in range(4):
+            nc.sync.dma_start(
+                tab_s[32 * q : 32 * q + 4 * PASSES, :].bitcast(I32), tab_scales[:, 4 * q : 4 * q + 4, :].bitcast(I32)
+            )
+        nc.sync.dma_start(tab_w[:], tab_words.rearrange("a p t i -> p a (t i)").bitcast(I32))
+        nc.sync.dma_start(w8_w[:], w8_words.rearrange("a p e i -> p a (e i)").bitcast(I32))
+        for q in range(4):
+            nc.gpsimd.dma_start(
+                w8_s[32 * q : 32 * q + 4 * PASSES, :].bitcast(I32), w8_scales[:, 4 * q : 4 * q + 4, :].bitcast(I32)
+            )
+        for q in range(4):
+            nc.sync.dma_start(
+                w4_s[32 * q : 32 * q + 4, :, :].bitcast(I32),
+                w4_scales[:, 4 * q : 4 * q + 4, :].rearrange("a r e -> r a e").bitcast(I32),
+            )
+        nc.sync.dma_start(w4_w[:].bitcast(I32), w4_words.rearrange("a p e -> p a e").bitcast(I32))
+        make_identity(nc, ident[:])
+
+        def gather_scales(lst, name):
+            picked = keep.tile([P, S], U8, name=name, align_bytes=64)
+            nc.vector.tensor_copy(picked[:], tab_s[:].indirect(lst[:]))
+            return picked
+
+        def gather_words(lst, first, count, name):
+            picked = []
+            for a in range(PASSES):
+                words = keep.tile([P, count], U32, name="%s_%d_%d" % (name, first, a), align_bytes=64)
+                window = tab_w[:, a, :].bitcast(U32)
+                nc.vector.tensor_copy(words[:], window.indirect(lst[:, first // 16 : (first + count) // 16]))
+                picked.append(words)
+            return [[w[:, j : j + P] for w in picked] for j in range(0, count, P)]
+
+        now_s = gather_scales(list_now, "now_s")
+        for r in range(4):
+            nc.sync.dma_start(now_s1[r:P:32, :].bitcast(I32), now_s[4 + r : P : 32, :].bitcast(I32))
+        future_s = gather_scales(list_future, "future_s")
+
+        w1_raw = []
+        for a in range(PASSES):
+            for c in range(2):
+                raw = keep.tile([P, 4, H // 2], F32, name="w1_raw_%d_%d" % (a, c))
+                rows = w1[512 * a : 512 * (a + 1), (H // 2) * c : (H // 2) * (c + 1)]
+                nc.sync.dma_start(raw[:], rows.rearrange("(p j) c -> p j c", j=4))
+                w1_raw.append(raw)
+        nc.sync.dma_start(list_past[:], offs)
+        wd_raw = keep.tile([P, 4, N], F32, name="wd_raw")
+        nc.sync.dma_start(wd_raw[:], wd.rearrange("(p j) c -> p j c", j=4))
+
+        def round_and_quantize(copy, raw, codes, scales, name):
+            width = raw.shape[2]
+            grouped = keep.tile([P, width, 4], BF16, name=name, align_bytes=64)
+            copy(
+                grouped[:].rearrange("p (c i) j -> p c j i", i=4),
+                raw[:].rearrange("p j (c i) -> p c j i", i=4),
+            )
+            nc.vector.quantize_mx(
+                out=codes.bitcast(FP8X4), scales=scales, in_=grouped[:].rearrange("p c j -> p (c j)")
+            )
+
+        def project(bank, words, word_scales, weights, weight_scales):
+            for a in range(PASSES):
+                nc.tensor.matmul_mx(
+                    out=bank[:],
+                    lhsT=words[a].bitcast(FP8X4),
+                    lhsT_scale=word_scales[a],
+                    rhs=weights[a],
+                    rhs_scale=weight_scales[a],
+                    start=(a == 0),
+                    stop=(a == PASSES - 1),
+                )
+
+        def dealt(bank):
+            return bank[:].rearrange("j (p t) -> j t p", t=4)
+
+        def turn_and_add(bank, terms):
+            for t in range(4):
+                for n, term in enumerate(terms):
+                    nc.tensor.matmul(
+                        bank[:, t, :],
+                        lhsT=term[:, t, :],
+                        rhs=ident[:],
+                        is_transpose=True,
+                        start=(n == 0),
+                        stop=(n == len(terms) - 1),
+                    )
+
+        w1_codes = keep.tile([P, PASSES, H], U32, name="w1_codes", align_bytes=64)
+        w1_s = keep.tile([P, PASSES, H], U8, name="w1_s", align_bytes=64)
+        w4_ops = [w4_w[:, a, :].bitcast(FP4X4) for a in range(PASSES)]
+        w8_ops = [w8_w[:, a, :].bitcast(FP8X4) for a in range(PASSES)]
+        w1_ops = [w1_codes[:, a, :].bitcast(FP8X4) for a in range(PASSES)]
+
+        now_w, future_w = [], []
+        for first, count in ((0, 256), (256, 256), (512, 512)):
+            future_w.extend(gather_words(list_future, first, count, "future_w"))
+            now_w.extend(gather_words(list_now, first, count, "now_w"))
+
+        minus_b, second = [], []
+        for i in range(TILES):
+            cols = slice(P * i, P * (i + 1))
+            c_bank = psum.tile([P, H], F32, name="c_bank", tag="proj%d" % (2 * (i % 3)))
+            project(
+                c_bank,
+                future_w[i],
+                [future_s[4 * a :, cols] for a in range(PASSES)],
+                w8_ops,
+                [w8_s[4 * a :, :] for a in range(PASSES)],
+            )
+            c_sb = ring.tile([P, 4, P], F32, name="c_sb")
+            nc.scalar.copy(c_sb[:], dealt(c_bank))
+
+            b_bank = psum.tile([P, H], F32, name="b_bank", tag="proj%d" % (2 * (i % 3) + 1))
+            project(b_bank, now_w[i], [now_s[:, cols], now_s1[:, cols]], w4_ops, [w4_s[:, a, :] for a in range(PASSES)])
+            nb = keep.tile([P, 4, P], F32, name="minus_b_%d" % i)
+            nc.scalar.activation(nb[:], dealt(b_bank), ACT.Copy, scale=-1.0)
+            minus_b.append(nb)
+
+            v_bank = psum.tile([P, 4, P], F32, name="v_bank", tag="turn%d" % (i % 2))
+            turn_and_add(v_bank, [c_sb, nb])
+            size = keep.tile([P, P, 4], F32, name="second_%d" % i)
+            nc.scalar.activation(size[:], v_bank[:].rearrange("p t j -> p j t"), ACT.Abs)
+            second.append(size)
+
+            if i in (1, 2):
+                a = i - 1
+                for c in range(2):
+                    half = slice((H // 2) * c, (H // 2) * (c + 1))
+                    round_and_quantize(
+                        nc.scalar.copy, w1_raw[2 * a + c], w1_codes[:, a, half], w1_s[:, a, half], "w1_bf_%d_%d" % (a, c)
+                    )
+
+        past_s = gather_scales(list_past, "past_s")
+        past_w = gather_words(list_past, 0, S // 2, "past_w") + gather_words(list_past, S // 2, S // 2, "past_w")
+        wd_codes = keep.tile([P, N], U32, name="wd_codes", align_bytes=64)
+        wd_s = keep.tile([P, N], U8, name="wd_s", align_bytes=64)
+        round_and_quantize(nc.vector.tensor_copy, wd_raw, wd_codes[:], wd_s[:], "wd_bf")
+
+        first_sizes = []
+        for i in range(TILES):
+            cols = slice(P * i, P * (i + 1))
+            a_bank = psum.tile([P, H], F32, name="a_bank", tag="proj%d" % (4, 5, 0, 1)[i % 4])
+            project(
+                a_bank,
+                past_w[i],
+                [past_s[4 * a :, cols] for a in range(PASSES)],
+                w1_ops,
+                [w1_s[:, a, :] for a in range(PASSES)],
+            )
+            u_sb = keep.tile([P, 4, P], F32, name="u_sb_%d" % i)
+            nc.vector.tensor_tensor(u_sb[:], dealt(a_bank), minus_b[i][:], ALU.add)
+            u_bank = psum.tile([P, 4, P], F32, name="u_bank", tag="turn%d" % (i % 2))
+            turn_and_add(u_bank, [u_sb])
+            size = keep.tile([P, P, 4], F32, name="first_%d" % i)
+            nc.scalar.activation(size[:], u_bank[:].rearrange("p t j -> p j t"), ACT.Abs)
+            first_sizes.append(size)
+
+        out_rows = out.rearrange("(g m p) j -> p g m j", g=2, p=P)
+        for pair in range(TILES // 2):
+            h = keep.tile([P, 2, P, 4], BF16, name="h_%d" % pair, align_bytes=64)
+            for half in range(2):
+                i = 2 * pair + half
+                nc.vector.tensor_tensor(h[:, half, :, :], first_sizes[i][:], second[i][:], ALU.subtract)
+            h_codes = keep.tile([P, PAIR], U32, name="h_codes_%d" % pair, align_bytes=64)
+            h_s = keep.tile([P, PAIR], U8, name="h_s_%d" % pair, align_bytes=64)
+            nc.vector.quantize_mx(
+                out=h_codes[:].bitcast(FP8X4), scales=h_s[:], in_=h[:].rearrange("p f j t -> p (f j t)")
+            )
+            for g in range(2):
+                o_bank = psum.tile([P, 2, PAIR], F32, name="o_bank", tag="proj%d" % (2 + g))
+                for m in range(2):
+                    rows = slice(P * (2 * g + m), P * (2 * g + m + 1))
+                    nc.tensor.matmul_mx(
+                        out=o_bank[:, m, :],
+                        lhsT=wd_codes[:, rows].bitcast(FP8X4),
+                        lhsT_scale=wd_s[:, rows],
+                        rhs=h_codes[:].bitcast(FP8X4),
+                        rhs_scale=h_s[:],
+                        start=True,
+                        stop=True,
+                    )
+                o_sb = keep.tile([P, 2, PAIR], F32, name="o_sb_%d_%d" % (pair, g))
+                if pair == TILES // 2 - 1 and g == 1:
+                    nc.vector.tensor_copy(o_sb[:], o_bank[:])
+                else:
+                    nc.scalar.copy(o_sb[:], o_bank[:])
+                nc.sync.dma_start(out_rows[:, g, :, PAIR * pair : PAIR * (pair + 1)], o_sb[:])

@@ -1,7 +1,6 @@
 from contextlib import ExitStack
 
 import concourse.mybir as mybir
-from concourse.masks import make_identity
 
 K, T, S, H, N = 1024, 2048, 1024, 512, 512
 FLOPS = 2 * S * (3 * K * H + H * N)
@@ -38,188 +37,191 @@ def tile_list_patch_motion_acceleration_kernel(
         tab_w = keep.tile([P, PASSES, T], I32, name="tab_w", align_bytes=64)
         tab_s = keep.tile([P, T], U8, name="tab_s", align_bytes=64)
         now_s1 = keep.tile([P, S], U8, name="now_s1", align_bytes=64)
-        w4_w = keep.tile([P, PASSES, 2 * H], U8, name="w4_w", align_bytes=64)
-        w8_w = keep.tile([P, PASSES, H], I32, name="w8_w", align_bytes=64)
-        w4_s = keep.tile([P, PASSES, H], U8, name="w4_s", align_bytes=64)
-        w8_s = keep.tile([P, H], U8, name="w8_s", align_bytes=64)
-        ident = keep.tile([P, P], F32, name="ident", align_bytes=64)
+        w4_in = keep.tile([P, PASSES, H // 2], I32, name="w4_in", tag="now_w_0_1", align_bytes=64)
+        w8_in = keep.tile([P, PASSES, H], I32, name="w8_in", align_bytes=64)
+        w4s_in = keep.tile([P, PASSES, H // 4], I32, name="w4s_in", tag="now_w_0_0", align_bytes=64)
+        w8s_in = keep.tile([P, 1, H // 4], I32, name="w8s_in", align_bytes=64)
 
         nc.gpsimd.memset(tab_s[:].bitcast(I32), 0)
-        nc.vector.memset(w8_s[:].bitcast(I32), 0)
-        nc.vector.memset(w4_s[:].bitcast(I32), 0)
+        nc.vector.memset(w8s_in[:], 0)
+        nc.vector.memset(w4s_in[:], 0)
         nc.vector.memset(now_s1[:].bitcast(I32), 0)
 
         nc.sync.dma_start(list_now[:], offs2)
-        nc.sync.dma_start(list_future[:], offs3)
         for q in range(4):
             nc.sync.dma_start(
                 tab_s[32 * q : 32 * q + 4 * PASSES, :].bitcast(I32), tab_scales[:, 4 * q : 4 * q + 4, :].bitcast(I32)
             )
-        nc.sync.dma_start(tab_w[:], tab_words.rearrange("a p t i -> p a (t i)").bitcast(I32))
-        nc.sync.dma_start(w8_w[:], w8_words.rearrange("a p e i -> p a (e i)").bitcast(I32))
-        for q in range(4):
-            nc.gpsimd.dma_start(
-                w8_s[32 * q : 32 * q + 4 * PASSES, :].bitcast(I32), w8_scales[:, 4 * q : 4 * q + 4, :].bitcast(I32)
-            )
+        nc.sync.dma_start(list_future[:], offs3)
+        nc.sync.dma_start(w8_in[:], w8_words.rearrange("a p e i -> p a (e i)").bitcast(I32))
         for q in range(4):
             nc.sync.dma_start(
-                w4_s[32 * q : 32 * q + 4, :, :].bitcast(I32),
+                w8s_in[32 * q : 32 * q + 4 * PASSES, 0, :], w8_scales[:, 4 * q : 4 * q + 4, :].bitcast(I32)
+            )
+        nc.sync.dma_start(tab_w[:], tab_words.rearrange("a p t i -> p a (t i)").bitcast(I32))
+        nc.sync.dma_start(w4_in[:], w4_words.rearrange("a p e -> p a e").bitcast(I32))
+        for q in range(4):
+            nc.sync.dma_start(
+                w4s_in[32 * q : 32 * q + 4, :, :],
                 w4_scales[:, 4 * q : 4 * q + 4, :].rearrange("a r e -> r a e").bitcast(I32),
             )
-        nc.sync.dma_start(w4_w[:].bitcast(I32), w4_words.rearrange("a p e -> p a e").bitcast(I32))
-        make_identity(nc, ident[:])
+
+        def deal(source, name):
+            rows, width = source.shape[1], source.shape[2]
+            dealt = keep.tile([P, rows, width], I32, name=name, align_bytes=64)
+            nc.vector.tensor_copy(
+                dealt[:].rearrange("p a (t g i) -> p a t g i", t=4, g=16),
+                source[:].rearrange("p a (g t i) -> p a t g i", t=4, g=16),
+            )
+            return dealt
 
         def gather_scales(lst, name):
             picked = keep.tile([P, S], U8, name=name, align_bytes=64)
             nc.vector.tensor_copy(picked[:], tab_s[:].indirect(lst[:]))
             return picked
 
-        def gather_words(lst, first, count, name):
+        def gather_words(lst, name):
             picked = []
-            for a in range(PASSES):
-                words = keep.tile([P, count], U32, name="%s_%d_%d" % (name, first, a), align_bytes=64)
-                window = tab_w[:, a, :].bitcast(U32)
-                nc.vector.tensor_copy(words[:], window.indirect(lst[:, first // 16 : (first + count) // 16]))
-                picked.append(words)
-            return [[w[:, j : j + P] for w in picked] for j in range(0, count, P)]
+            for half in range(2):
+                offsets = lst[:, (S // 32) * half : (S // 32) * (half + 1)]
+                passes = []
+                for a in range(PASSES):
+                    label = "%s_%d_%d" % (name, half, a)
+                    words = keep.tile([P, S // 2], U32, name=label, tag=label, align_bytes=64)
+                    nc.vector.tensor_copy(words[:], tab_w[:, a, :].bitcast(U32).indirect(offsets))
+                    passes.append(words)
+                picked.extend([w[:, j : j + P] for w in passes] for j in range(0, S // 2, P))
+            return picked
 
         now_s = gather_scales(list_now, "now_s")
         for r in range(4):
             nc.sync.dma_start(now_s1[r:P:32, :].bitcast(I32), now_s[4 + r : P : 32, :].bitcast(I32))
         future_s = gather_scales(list_future, "future_s")
 
-        w1_raw = []
+        w1_raw = keep.tile([P, PASSES, 4, H], F32, name="w1_raw", tag="w1_then_v")
         for a in range(PASSES):
-            for c in range(2):
-                raw = keep.tile([P, 4, H // 2], F32, name="w1_raw_%d_%d" % (a, c))
-                rows = w1[512 * a : 512 * (a + 1), (H // 2) * c : (H // 2) * (c + 1)]
-                nc.sync.dma_start(raw[:], rows.rearrange("(p j) c -> p j c", j=4))
-                w1_raw.append(raw)
+            nc.sync.dma_start(w1_raw[:, a], w1[512 * a : 512 * (a + 1), :].rearrange("(p j) c -> p j c", j=4))
         nc.sync.dma_start(list_past[:], offs)
         wd_raw = keep.tile([P, 4, N], F32, name="wd_raw")
-        nc.sync.dma_start(wd_raw[:], wd.rearrange("(p j) c -> p j c", j=4))
+        wd_rows = wd.rearrange("(g t i) n -> t g i n", t=4, i=8)
+        for t in range(4):
+            nc.sync.dma_start(wd_raw[:, t, :], wd_rows[t])
 
-        def round_and_quantize(copy, raw, codes, scales, name):
-            width = raw.shape[2]
-            grouped = keep.tile([P, width, 4], BF16, name=name, align_bytes=64)
-            copy(
-                grouped[:].rearrange("p (c i) j -> p c j i", i=4),
-                raw[:].rearrange("p j (c i) -> p c j i", i=4),
-            )
-            nc.vector.quantize_mx(
-                out=codes.bitcast(FP8X4), scales=scales, in_=grouped[:].rearrange("p c j -> p (c j)")
-            )
+        w8_w = deal(w8_in, "w8_w")
+        w8_s = deal(w8s_in, "w8_s")[:].bitcast(U8)
+        future_w = gather_words(list_future, "future_w")
+        w4_w = deal(w4_in, "w4_w")
+        w4_s = deal(w4s_in, "w4_s")[:].bitcast(U8)
+        now_w = gather_words(list_now, "now_w")
+        past_s = gather_scales(list_past, "past_s")
+        past_w = gather_words(list_past, "past_w")
 
-        def project(bank, words, word_scales, weights, weight_scales):
-            for a in range(PASSES):
-                nc.tensor.matmul_mx(
-                    out=bank[:],
-                    lhsT=words[a].bitcast(FP8X4),
-                    lhsT_scale=word_scales[a],
-                    rhs=weights[a],
-                    rhs_scale=weight_scales[a],
-                    start=(a == 0),
-                    stop=(a == PASSES - 1),
-                )
+        def quantize(codes, scales, values):
+            nc.vector.quantize_mx(out=codes.bitcast(FP8X4), scales=scales, in_=values)
 
-        def dealt(bank):
-            return bank[:].rearrange("j (p t) -> j t p", t=4)
-
-        def turn_and_add(bank, terms):
+        def project(bank, weights, weight_scales, words, word_scales):
             for t in range(4):
-                for n, term in enumerate(terms):
-                    nc.tensor.matmul(
-                        bank[:, t, :],
-                        lhsT=term[:, t, :],
-                        rhs=ident[:],
-                        is_transpose=True,
-                        start=(n == 0),
-                        stop=(n == len(terms) - 1),
+                for a in range(PASSES):
+                    nc.tensor.matmul_mx(
+                        out=bank[:, t, :],
+                        lhsT=weights(a, t),
+                        lhsT_scale=weight_scales(a, t),
+                        rhs=words[a].bitcast(FP8X4),
+                        rhs_scale=word_scales[a],
+                        start=(a == 0),
+                        stop=(a == PASSES - 1),
                     )
+
+        def woven(bank):
+            return bank[:].rearrange("p t j -> p j t")
+
+        def project_future(i):
+            cols = slice(P * i, P * (i + 1))
+            c_bank = psum.tile([P, 4, P], F32, name="c_bank", tag="bank%d" % (2 + i % 4))
+            project(
+                c_bank,
+                lambda a, t: w8_w[:, a, P * t : P * (t + 1)].bitcast(FP8X4),
+                lambda a, t: w8_s[4 * a :, 0, P * t : P * (t + 1)],
+                future_w[i],
+                [future_s[4 * a :, cols] for a in range(PASSES)],
+            )
+            c = keep.tile([P, P, 4], F32, name="c_%d" % i)
+            nc.scalar.copy(c[:], woven(c_bank))
+            return c
+
+        c_sb = [project_future(i) for i in range(TILES)]
+
+        minus_b = []
+        for i in range(TILES):
+            cols = slice(P * i, P * (i + 1))
+            b_bank = psum.tile([P, 4, P], F32, name="b_bank", tag="bank%d" % (i % 2))
+            project(
+                b_bank,
+                lambda a, t: w4_w[:, a, 64 * t : 64 * (t + 1)].bitcast(FP4X4),
+                lambda a, t: w4_s[:, a, P * t : P * (t + 1)],
+                now_w[i],
+                [now_s[:, cols], now_s1[:, cols]],
+            )
+            nb = keep.tile([P, P, 4], F32, name="minus_b_%d" % i)
+            nc.scalar.activation(nb[:], woven(b_bank), ACT.Copy, scale=-1.0)
+            minus_b.append(nb)
 
         w1_codes = keep.tile([P, PASSES, H], U32, name="w1_codes", align_bytes=64)
         w1_s = keep.tile([P, PASSES, H], U8, name="w1_s", align_bytes=64)
-        w4_ops = [w4_w[:, a, :].bitcast(FP4X4) for a in range(PASSES)]
-        w8_ops = [w8_w[:, a, :].bitcast(FP8X4) for a in range(PASSES)]
-        w1_ops = [w1_codes[:, a, :].bitcast(FP8X4) for a in range(PASSES)]
+        for a in range(PASSES):
+            w1_bf = keep.tile([P, 4 * H], BF16, name="w1_bf_%d" % a, align_bytes=64)
+            rounded = w1_bf[:].rearrange("p (t g i j) -> p t g i j", t=4, g=16, i=8)
+            source = w1_raw[:, a].rearrange("p j (g t i) -> p t g i j", t=4, g=16)
+            for t in range(4):
+                nc.gpsimd.tensor_scalar(rounded[:, t], source[:, t], 1.0, 0.0, ALU.mult, ALU.add)
+            quantize(w1_codes[:, a, :], w1_s[:, a, :], w1_bf[:])
 
-        now_w, future_w = [], []
-        for first, count in ((0, 256), (256, 256), (512, 512)):
-            future_w.extend(gather_words(list_future, first, count, "future_w"))
-            now_w.extend(gather_words(list_now, first, count, "now_w"))
-
-        minus_b, second = [], []
+        second = []
+        v = keep.tile([P, TILES, P, 4], F32, name="v", tag="w1_then_v")
         for i in range(TILES):
-            cols = slice(P * i, P * (i + 1))
-            c_bank = psum.tile([P, H], F32, name="c_bank", tag="proj%d" % (2 * (i % 3)))
-            project(
-                c_bank,
-                future_w[i],
-                [future_s[4 * a :, cols] for a in range(PASSES)],
-                w8_ops,
-                [w8_s[4 * a :, :] for a in range(PASSES)],
-            )
-            c_sb = ring.tile([P, 4, P], F32, name="c_sb")
-            nc.scalar.copy(c_sb[:], dealt(c_bank))
-
-            b_bank = psum.tile([P, H], F32, name="b_bank", tag="proj%d" % (2 * (i % 3) + 1))
-            project(b_bank, now_w[i], [now_s[:, cols], now_s1[:, cols]], w4_ops, [w4_s[:, a, :] for a in range(PASSES)])
-            nb = keep.tile([P, 4, P], F32, name="minus_b_%d" % i)
-            nc.scalar.activation(nb[:], dealt(b_bank), ACT.Copy, scale=-1.0)
-            minus_b.append(nb)
-
-            v_bank = psum.tile([P, 4, P], F32, name="v_bank", tag="turn%d" % (i % 2))
-            turn_and_add(v_bank, [c_sb, nb])
+            nc.gpsimd.tensor_tensor(v[:, i], c_sb[i][:], minus_b[i][:], ALU.add)
             size = keep.tile([P, P, 4], F32, name="second_%d" % i)
-            nc.scalar.activation(size[:], v_bank[:].rearrange("p t j -> p j t"), ACT.Abs)
+            nc.scalar.activation(size[:], v[:, i], ACT.Abs)
             second.append(size)
 
-            if i in (1, 2):
-                a = i - 1
-                for c in range(2):
-                    half = slice((H // 2) * c, (H // 2) * (c + 1))
-                    round_and_quantize(
-                        nc.scalar.copy, w1_raw[2 * a + c], w1_codes[:, a, half], w1_s[:, a, half], "w1_bf_%d_%d" % (a, c)
-                    )
-
-        past_s = gather_scales(list_past, "past_s")
-        past_w = gather_words(list_past, 0, S // 2, "past_w") + gather_words(list_past, S // 2, S // 2, "past_w")
+        wd_bf = keep.tile([P, N, 4], BF16, name="wd_bf", align_bytes=64)
+        nc.scalar.copy(
+            wd_bf[:].rearrange("p (c i) t -> p c t i", i=4), wd_raw[:].rearrange("p t (c i) -> p c t i", i=4)
+        )
         wd_codes = keep.tile([P, N], U32, name="wd_codes", align_bytes=64)
         wd_s = keep.tile([P, N], U8, name="wd_s", align_bytes=64)
-        round_and_quantize(nc.vector.tensor_copy, wd_raw, wd_codes[:], wd_s[:], "wd_bf")
+        quantize(wd_codes[:], wd_s[:], wd_bf[:].rearrange("p c t -> p (c t)"))
 
-        first_sizes = []
-        for i in range(TILES):
+        first = []
+
+        def first_size(i):
             cols = slice(P * i, P * (i + 1))
-            a_bank = psum.tile([P, H], F32, name="a_bank", tag="proj%d" % (4, 5, 0, 1)[i % 4])
+            a_bank = psum.tile([P, 4, P], F32, name="a_bank", tag="bank%d" % (2 + i % 4))
             project(
                 a_bank,
+                lambda a, t: w1_codes[:, a, P * t : P * (t + 1)].bitcast(FP8X4),
+                lambda a, t: w1_s[:, a, P * t : P * (t + 1)],
                 past_w[i],
                 [past_s[4 * a :, cols] for a in range(PASSES)],
-                w1_ops,
-                [w1_s[:, a, :] for a in range(PASSES)],
             )
-            u_sb = keep.tile([P, 4, P], F32, name="u_sb_%d" % i)
-            nc.vector.tensor_tensor(u_sb[:], dealt(a_bank), minus_b[i][:], ALU.add)
-            u_bank = psum.tile([P, 4, P], F32, name="u_bank", tag="turn%d" % (i % 2))
-            turn_and_add(u_bank, [u_sb])
+            u = ring.tile([P, P, 4], F32, name="u")
+            nc.vector.tensor_tensor(u[:], woven(a_bank), minus_b[i][:], ALU.add)
             size = keep.tile([P, P, 4], F32, name="first_%d" % i)
-            nc.scalar.activation(size[:], u_bank[:].rearrange("p t j -> p j t"), ACT.Abs)
-            first_sizes.append(size)
+            nc.scalar.activation(size[:], u[:], ACT.Abs)
+            first.append(size)
 
         out_rows = out.rearrange("(g m p) j -> p g m j", g=2, p=P)
-        for pair in range(TILES // 2):
+
+        def decode(pair):
             h = keep.tile([P, 2, P, 4], BF16, name="h_%d" % pair, align_bytes=64)
             for half in range(2):
                 i = 2 * pair + half
-                nc.vector.tensor_tensor(h[:, half, :, :], first_sizes[i][:], second[i][:], ALU.subtract)
+                nc.vector.tensor_tensor(h[:, half, :, :], first[i][:], second[i][:], ALU.subtract)
             h_codes = keep.tile([P, PAIR], U32, name="h_codes_%d" % pair, align_bytes=64)
             h_s = keep.tile([P, PAIR], U8, name="h_s_%d" % pair, align_bytes=64)
-            nc.vector.quantize_mx(
-                out=h_codes[:].bitcast(FP8X4), scales=h_s[:], in_=h[:].rearrange("p f j t -> p (f j t)")
-            )
+            quantize(h_codes[:], h_s[:], h[:].rearrange("p f j t -> p (f j t)"))
             for g in range(2):
-                o_bank = psum.tile([P, 2, PAIR], F32, name="o_bank", tag="proj%d" % (2 + g))
+                o_bank = psum.tile([P, 2, PAIR], F32, name="o_bank", tag="bank%d" % (6 + g))
                 for m in range(2):
                     rows = slice(P * (2 * g + m), P * (2 * g + m + 1))
                     nc.tensor.matmul_mx(
@@ -237,3 +239,10 @@ def tile_list_patch_motion_acceleration_kernel(
                 else:
                     nc.scalar.copy(o_sb[:], o_bank[:])
                 nc.sync.dma_start(out_rows[:, g, :, PAIR * pair : PAIR * (pair + 1)], o_sb[:])
+
+        for pair in range(TILES // 2):
+            first_size(2 * pair)
+            first_size(2 * pair + 1)
+            if pair > 0:
+                decode(pair - 1)
+        decode(TILES // 2 - 1)

@@ -37,14 +37,12 @@ def tile_list_patch_motion_acceleration_kernel(
         tab_w = keep.tile([P, PASSES, T], I32, name="tab_w", align_bytes=64)
         tab_s = keep.tile([P, T], U8, name="tab_s", align_bytes=64)
         now_s1 = keep.tile([P, S], U8, name="now_s1", align_bytes=64)
-        w4_in = keep.tile([P, PASSES, H // 2], I32, name="w4_in", tag="now_w_0_1", align_bytes=64)
+        w4_in = keep.tile([P, PASSES, H // 2], I32, name="w4_in", tag="now_w_1", align_bytes=64)
         w8_in = keep.tile([P, PASSES, H], I32, name="w8_in", align_bytes=64)
-        w4s_in = keep.tile([P, PASSES, H // 4], I32, name="w4s_in", tag="now_w_0_0", align_bytes=64)
-        w8s_in = keep.tile([P, 1, H // 4], I32, name="w8s_in", align_bytes=64)
+        ws_in = keep.tile([P, PASSES + 1, H // 4], I32, name="ws_in", tag="now_w_0", align_bytes=64)
 
         nc.gpsimd.memset(tab_s[:].bitcast(I32), 0)
-        nc.vector.memset(w8s_in[:], 0)
-        nc.vector.memset(w4s_in[:], 0)
+        nc.vector.memset(ws_in[:], 0)
         nc.vector.memset(now_s1[:].bitcast(I32), 0)
 
         nc.sync.dma_start(list_now[:], offs2)
@@ -54,17 +52,20 @@ def tile_list_patch_motion_acceleration_kernel(
             )
         nc.sync.dma_start(list_future[:], offs3)
         nc.sync.dma_start(w8_in[:], w8_words.rearrange("a p e i -> p a (e i)").bitcast(I32))
-        for q in range(4):
-            nc.sync.dma_start(
-                w8s_in[32 * q : 32 * q + 4 * PASSES, 0, :], w8_scales[:, 4 * q : 4 * q + 4, :].bitcast(I32)
-            )
         nc.sync.dma_start(tab_w[:], tab_words.rearrange("a p t i -> p a (t i)").bitcast(I32))
-        nc.sync.dma_start(w4_in[:], w4_words.rearrange("a p e -> p a e").bitcast(I32))
+        raw = keep.tile([P, PASSES + 1, 4, H], F32, name="raw", tag="raw_then_b")
+        w1_rows = w1.rearrange("(a p j) c -> a p j c", p=P, j=4)
+        nc.sync.dma_start(raw[:, 0], w1_rows[0])
         for q in range(4):
             nc.sync.dma_start(
-                w4s_in[32 * q : 32 * q + 4, :, :],
+                ws_in[32 * q : 32 * q + 4 * PASSES, PASSES, :], w8_scales[:, 4 * q : 4 * q + 4, :].bitcast(I32)
+            )
+        for q in range(4):
+            nc.sync.dma_start(
+                ws_in[32 * q : 32 * q + 4, 0:PASSES, :],
                 w4_scales[:, 4 * q : 4 * q + 4, :].rearrange("a r e -> r a e").bitcast(I32),
             )
+        nc.sync.dma_start(w4_in[:], w4_words.rearrange("a p e -> p a e").bitcast(I32))
 
         def deal(source, name):
             rows, width = source.shape[1], source.shape[2]
@@ -80,148 +81,128 @@ def tile_list_patch_motion_acceleration_kernel(
             nc.vector.tensor_copy(picked[:], tab_s[:].indirect(lst[:]))
             return picked
 
-        def gather_words(lst, name):
-            picked = []
-            for half in range(2):
-                offsets = lst[:, (S // 32) * half : (S // 32) * (half + 1)]
-                passes = []
-                for a in range(PASSES):
-                    label = "%s_%d_%d" % (name, half, a)
-                    words = keep.tile([P, S // 2], U32, name=label, tag=label, align_bytes=64)
-                    nc.vector.tensor_copy(words[:], tab_w[:, a, :].bitcast(U32).indirect(offsets))
-                    passes.append(words)
-                picked.extend([w[:, j : j + P] for w in passes] for j in range(0, S // 2, P))
-            return picked
+        def gather_words(lst, a, first, count, name, tag):
+            words = keep.tile([P, count], U32, name=name, tag=tag, align_bytes=64)
+            offsets = lst[:, first // 16 : (first + count) // 16]
+            nc.vector.tensor_copy(words[:], tab_w[:, a, :].bitcast(U32).indirect(offsets))
+            return [words[:, j : j + P] for j in range(0, count, P)]
 
         now_s = gather_scales(list_now, "now_s")
         for r in range(4):
             nc.sync.dma_start(now_s1[r:P:32, :].bitcast(I32), now_s[4 + r : P : 32, :].bitcast(I32))
         future_s = gather_scales(list_future, "future_s")
 
-        w1_raw = keep.tile([P, PASSES, 4, H], F32, name="w1_raw", tag="w1_then_v")
-        for a in range(PASSES):
-            nc.sync.dma_start(w1_raw[:, a], w1[512 * a : 512 * (a + 1), :].rearrange("(p j) c -> p j c", j=4))
+        nc.sync.dma_start(raw[:, 1], w1_rows[1])
         nc.sync.dma_start(list_past[:], offs)
-        wd_raw = keep.tile([P, 4, N], F32, name="wd_raw")
         wd_rows = wd.rearrange("(g t i) n -> t g i n", t=4, i=8)
         for t in range(4):
-            nc.sync.dma_start(wd_raw[:, t, :], wd_rows[t])
+            nc.sync.dma_start(raw[:, PASSES, t, :], wd_rows[t])
 
         w8_w = deal(w8_in, "w8_w")
-        w8_s = deal(w8s_in, "w8_s")[:].bitcast(U8)
-        future_w = gather_words(list_future, "future_w")
+        future_w = [gather_words(list_future, a, 0, S, "future_w_%d" % a, "future_w_%d" % a) for a in range(PASSES)]
+        w_s = deal(ws_in, "w_s")[:].bitcast(U8)
         w4_w = deal(w4_in, "w4_w")
-        w4_s = deal(w4s_in, "w4_s")[:].bitcast(U8)
-        now_w = gather_words(list_now, "now_w")
+        now_w = [gather_words(list_now, a, 0, S, "now_w_%d" % a, "now_w_%d" % a) for a in range(PASSES)]
         past_s = gather_scales(list_past, "past_s")
-        past_w = gather_words(list_past, "past_w")
+        past_w = [gather_words(list_past, 0, 0, S, "past_w_0", "past_w_0")]
 
         def quantize(codes, scales, values):
             nc.vector.quantize_mx(out=codes.bitcast(FP8X4), scales=scales, in_=values)
 
-        def project(bank, weights, weight_scales, words, word_scales):
+        def w4_pass(a, t, i):
+            rows, cols = slice(P * t, P * (t + 1)), slice(P * i, P * (i + 1))
+            plane = now_s if a == 0 else now_s1
+            return w4_w[:, a, 64 * t : 64 * (t + 1)].bitcast(FP4X4), w_s[:, a, rows], now_w[a][i], plane[:, cols]
+
+        def w8_pass(a, t, i):
+            rows, cols = slice(P * t, P * (t + 1)), slice(P * i, P * (i + 1))
+            return w8_w[:, a, rows].bitcast(FP8X4), w_s[4 * a :, PASSES, rows], future_w[a][i], future_s[4 * a :, cols]
+
+        def w1_pass(a, t, i):
+            rows, cols = slice(P * t, P * (t + 1)), slice(P * i, P * (i + 1))
+            return w1_codes[:, a, rows].bitcast(FP8X4), w1_s[:, a, rows], past_w[a][i], past_s[4 * a :, cols]
+
+        def project(i, bank_number, products):
+            bank = psum.tile([P, 4, P], F32, name="bank", tag="bank%d" % bank_number)
             for t in range(4):
-                for a in range(PASSES):
+                passes = [product(a, t, i) for product in products for a in range(PASSES)]
+                for n, (weights, weight_scales, words, word_scales) in enumerate(passes):
                     nc.tensor.matmul_mx(
                         out=bank[:, t, :],
-                        lhsT=weights(a, t),
-                        lhsT_scale=weight_scales(a, t),
-                        rhs=words[a].bitcast(FP8X4),
-                        rhs_scale=word_scales[a],
-                        start=(a == 0),
-                        stop=(a == PASSES - 1),
+                        lhsT=weights,
+                        lhsT_scale=weight_scales,
+                        rhs=words.bitcast(FP8X4),
+                        rhs_scale=word_scales,
+                        start=(n == 0),
+                        stop=(n == len(passes) - 1),
                     )
+            return bank
 
-        def woven(bank):
-            return bank[:].rearrange("p t j -> p j t")
-
-        def project_future(i):
-            cols = slice(P * i, P * (i + 1))
-            c_bank = psum.tile([P, 4, P], F32, name="c_bank", tag="bank%d" % (2 + i % 4))
-            project(
-                c_bank,
-                lambda a, t: w8_w[:, a, P * t : P * (t + 1)].bitcast(FP8X4),
-                lambda a, t: w8_s[4 * a :, 0, P * t : P * (t + 1)],
-                future_w[i],
-                [future_s[4 * a :, cols] for a in range(PASSES)],
-            )
-            c = keep.tile([P, P, 4], F32, name="c_%d" % i)
-            nc.scalar.copy(c[:], woven(c_bank))
-            return c
-
-        c_sb = [project_future(i) for i in range(TILES)]
-
-        minus_b = []
-        for i in range(TILES):
-            cols = slice(P * i, P * (i + 1))
-            b_bank = psum.tile([P, 4, P], F32, name="b_bank", tag="bank%d" % (i % 2))
-            project(
-                b_bank,
-                lambda a, t: w4_w[:, a, 64 * t : 64 * (t + 1)].bitcast(FP4X4),
-                lambda a, t: w4_s[:, a, P * t : P * (t + 1)],
-                now_w[i],
-                [now_s[:, cols], now_s1[:, cols]],
-            )
-            nb = keep.tile([P, P, 4], F32, name="minus_b_%d" % i)
-            nc.scalar.activation(nb[:], woven(b_bank), ACT.Copy, scale=-1.0)
-            minus_b.append(nb)
+        def size_of(difference, name):
+            size = keep.tile([P, P, 4], F32, name=name)
+            nc.scalar.activation(size[:], difference[:].rearrange("p t j -> p j t"), ACT.Abs)
+            return size
 
         w1_codes = keep.tile([P, PASSES, H], U32, name="w1_codes", align_bytes=64)
         w1_s = keep.tile([P, PASSES, H], U8, name="w1_s", align_bytes=64)
         for a in range(PASSES):
             w1_bf = keep.tile([P, 4 * H], BF16, name="w1_bf_%d" % a, align_bytes=64)
             rounded = w1_bf[:].rearrange("p (t g i j) -> p t g i j", t=4, g=16, i=8)
-            source = w1_raw[:, a].rearrange("p j (g t i) -> p t g i j", t=4, g=16)
+            source = raw[:, a].rearrange("p j (g t i) -> p t g i j", t=4, g=16)
             for t in range(4):
-                nc.gpsimd.tensor_scalar(rounded[:, t], source[:, t], 1.0, 0.0, ALU.mult, ALU.add)
+                nc.scalar.activation(rounded[:, t], source[:, t], ACT.Copy, scale=-1.0)
             quantize(w1_codes[:, a, :], w1_s[:, a, :], w1_bf[:])
-
-        second = []
-        v = keep.tile([P, TILES, P, 4], F32, name="v", tag="w1_then_v")
-        for i in range(TILES):
-            nc.gpsimd.tensor_tensor(v[:, i], c_sb[i][:], minus_b[i][:], ALU.add)
-            size = keep.tile([P, P, 4], F32, name="second_%d" % i)
-            nc.scalar.activation(size[:], v[:, i], ACT.Abs)
-            second.append(size)
 
         wd_bf = keep.tile([P, N, 4], BF16, name="wd_bf", align_bytes=64)
         nc.scalar.copy(
-            wd_bf[:].rearrange("p (c i) t -> p c t i", i=4), wd_raw[:].rearrange("p t (c i) -> p c t i", i=4)
+            wd_bf[:].rearrange("p (c i) t -> p c t i", i=4), raw[:, PASSES].rearrange("p t (c i) -> p c t i", i=4)
         )
         wd_codes = keep.tile([P, N], U32, name="wd_codes", align_bytes=64)
         wd_s = keep.tile([P, N], U8, name="wd_s", align_bytes=64)
         quantize(wd_codes[:], wd_s[:], wd_bf[:].rearrange("p c t -> p (c t)"))
 
+        c_banks = [project(i, 2 + i, [w8_pass]) for i in range(TILES - 2)]
+        b_sb = keep.tile([P, TILES, 4, P], F32, name="b_sb", tag="raw_then_b")
+        for i in range(TILES):
+            b_bank = project(i, i % 2, [w4_pass])
+            nc.scalar.copy(b_sb[:, i], b_bank[:])
+        c_banks.extend(project(i, i % 2, [w8_pass]) for i in range(TILES - 2, TILES))
+
+        second = []
+        for i in range(TILES):
+            v = ring.tile([P, 4, P], F32, name="v")
+            nc.vector.tensor_tensor(v[:], c_banks[i][:], b_sb[:, i], ALU.subtract)
+            second.append(size_of(v, "second_%d" % i))
+
+        past_w.append([])
+        for half in range(2):
+            name = "past_w_1_%d" % half
+            past_w[1].extend(gather_words(list_past, 1, (S // 2) * half, S // 2, name, "future_w_%d" % half))
+
         first = []
 
         def first_size(i):
-            cols = slice(P * i, P * (i + 1))
-            a_bank = psum.tile([P, 4, P], F32, name="a_bank", tag="bank%d" % (2 + i % 4))
-            project(
-                a_bank,
-                lambda a, t: w1_codes[:, a, P * t : P * (t + 1)].bitcast(FP8X4),
-                lambda a, t: w1_s[:, a, P * t : P * (t + 1)],
-                past_w[i],
-                [past_s[4 * a :, cols] for a in range(PASSES)],
-            )
-            u = ring.tile([P, P, 4], F32, name="u")
-            nc.vector.tensor_tensor(u[:], woven(a_bank), minus_b[i][:], ALU.add)
-            size = keep.tile([P, P, 4], F32, name="first_%d" % i)
-            nc.scalar.activation(size[:], u[:], ACT.Abs)
-            first.append(size)
+            if i < TILES - 2:
+                a_bank = project(i, 2 + i % 4, [w1_pass])
+                u = ring.tile([P, 4, P], F32, name="u")
+                nc.vector.tensor_tensor(u[:], a_bank[:], b_sb[:, i], ALU.add)
+            else:
+                u = project(i, i % 2, [w4_pass, w1_pass])
+            first.append(size_of(u, "first_%d" % i))
 
         out_rows = out.rearrange("(g m p) j -> p g m j", g=2, p=P)
 
-        def decode(pair):
-            h = keep.tile([P, 2, P, 4], BF16, name="h_%d" % pair, align_bytes=64)
-            for half in range(2):
-                i = 2 * pair + half
-                nc.vector.tensor_tensor(h[:, half, :, :], first[i][:], second[i][:], ALU.subtract)
-            h_codes = keep.tile([P, PAIR], U32, name="h_codes_%d" % pair, align_bytes=64)
-            h_s = keep.tile([P, PAIR], U8, name="h_s_%d" % pair, align_bytes=64)
+        def decode(tiles):
+            width = P * len(tiles)
+            cols = slice(P * tiles[0], P * tiles[0] + width)
+            h = keep.tile([P, len(tiles), P, 4], BF16, name="h_%d" % tiles[0], align_bytes=64)
+            for n, i in enumerate(tiles):
+                nc.vector.tensor_tensor(h[:, n], first[i][:], second[i][:], ALU.subtract)
+            h_codes = keep.tile([P, width], U32, name="h_codes_%d" % tiles[0], align_bytes=64)
+            h_s = keep.tile([P, width], U8, name="h_s_%d" % tiles[0], align_bytes=64)
             quantize(h_codes[:], h_s[:], h[:].rearrange("p f j t -> p (f j t)"))
             for g in range(2):
-                o_bank = psum.tile([P, 2, PAIR], F32, name="o_bank", tag="bank%d" % (6 + g))
+                o_bank = psum.tile([P, 2, width], F32, name="o_bank", tag="bank%d" % (6 + g))
                 for m in range(2):
                     rows = slice(P * (2 * g + m), P * (2 * g + m + 1))
                     nc.tensor.matmul_mx(
@@ -233,16 +214,17 @@ def tile_list_patch_motion_acceleration_kernel(
                         start=True,
                         stop=True,
                     )
-                o_sb = keep.tile([P, 2, PAIR], F32, name="o_sb_%d_%d" % (pair, g))
-                if pair == TILES // 2 - 1 and g == 1:
+                o_sb = keep.tile([P, 2, width], F32, name="o_sb_%d_%d" % (tiles[0], g))
+                if tiles[0] >= TILES // 2 and g == 1:
                     nc.vector.tensor_copy(o_sb[:], o_bank[:])
                 else:
                     nc.scalar.copy(o_sb[:], o_bank[:])
-                nc.sync.dma_start(out_rows[:, g, :, PAIR * pair : PAIR * (pair + 1)], o_sb[:])
+                nc.sync.dma_start(out_rows[:, g, :, cols], o_sb[:])
 
         for pair in range(TILES // 2):
             first_size(2 * pair)
             first_size(2 * pair + 1)
             if pair > 0:
-                decode(pair - 1)
-        decode(TILES // 2 - 1)
+                decode([2 * pair - 2, 2 * pair - 1])
+        decode([TILES - 2])
+        decode([TILES - 1])

@@ -1,6 +1,7 @@
 from contextlib import ExitStack
 
 import concourse.mybir as mybir
+from concourse.masks import make_identity
 
 K, T, S, H, N = 1024, 2048, 1024, 512, 512
 FLOPS = 2 * S * (3 * K * H + H * N)
@@ -19,7 +20,7 @@ ALU = mybir.AluOpType
 P = 128
 PASSES = K // 512
 TILES = S // P
-PAIR = 2 * P
+HALF = TILES // 2
 
 
 def tile_list_patch_motion_acceleration_kernel(
@@ -28,7 +29,6 @@ def tile_list_patch_motion_acceleration_kernel(
     nc = tc.nc
     with ExitStack() as ctx:
         keep = ctx.enter_context(tc.tile_pool(name="keep", bufs=1))
-        ring = ctx.enter_context(tc.tile_pool(name="ring", bufs=3))
         psum = ctx.enter_context(tc.psum_pool(name="psum", bufs=1))
 
         list_past = keep.tile([P, S // 16], U16, name="list_past")
@@ -37,12 +37,16 @@ def tile_list_patch_motion_acceleration_kernel(
         tab_w = keep.tile([P, PASSES, T], I32, name="tab_w", align_bytes=64)
         tab_s = keep.tile([P, T], U8, name="tab_s", align_bytes=64)
         now_s1 = keep.tile([P, S], U8, name="now_s1", align_bytes=64)
-        w4_in = keep.tile([P, PASSES, H // 2], I32, name="w4_in", tag="now_w_1", align_bytes=64)
-        w8_in = keep.tile([P, PASSES, H], I32, name="w8_in", align_bytes=64)
-        ws_in = keep.tile([P, PASSES + 1, H // 4], I32, name="ws_in", tag="now_w_0", align_bytes=64)
+        w4_w = keep.tile([P, PASSES, 2 * H], U8, name="w4_w", align_bytes=64)
+        w8_w = keep.tile([P, PASSES, H], I32, name="w8_w", align_bytes=64)
+        w4_s = keep.tile([P, PASSES, H], U8, name="w4_s", align_bytes=64)
+        w8_s = keep.tile([P, H], U8, name="w8_s", align_bytes=64)
+        ident = keep.tile([P, P], F32, name="ident", align_bytes=64)
 
         nc.gpsimd.memset(tab_s[:].bitcast(I32), 0)
-        nc.vector.memset(ws_in[:], 0)
+        make_identity(nc, ident[:])
+        nc.vector.memset(w8_s[:].bitcast(I32), 0)
+        nc.vector.memset(w4_s[:].bitcast(I32), 0)
         nc.vector.memset(now_s1[:].bitcast(I32), 0)
 
         nc.sync.dma_start(list_now[:], offs2)
@@ -51,144 +55,156 @@ def tile_list_patch_motion_acceleration_kernel(
                 tab_s[32 * q : 32 * q + 4 * PASSES, :].bitcast(I32), tab_scales[:, 4 * q : 4 * q + 4, :].bitcast(I32)
             )
         nc.sync.dma_start(list_future[:], offs3)
-        nc.sync.dma_start(w8_in[:], w8_words.rearrange("a p e i -> p a (e i)").bitcast(I32))
         nc.sync.dma_start(tab_w[:], tab_words.rearrange("a p t i -> p a (t i)").bitcast(I32))
-        raw = keep.tile([P, PASSES + 1, 4, H], F32, name="raw", tag="raw_then_b")
-        w1_rows = w1.rearrange("(a p j) c -> a p j c", p=P, j=4)
-        nc.sync.dma_start(raw[:, 0], w1_rows[0])
+        nc.sync.dma_start(w8_w[:], w8_words.rearrange("a p e i -> p a (e i)").bitcast(I32))
         for q in range(4):
             nc.sync.dma_start(
-                ws_in[32 * q : 32 * q + 4 * PASSES, PASSES, :], w8_scales[:, 4 * q : 4 * q + 4, :].bitcast(I32)
+                w8_s[32 * q : 32 * q + 4 * PASSES, :].bitcast(I32), w8_scales[:, 4 * q : 4 * q + 4, :].bitcast(I32)
             )
+        nc.sync.dma_start(w4_w[:].bitcast(I32), w4_words.rearrange("a p e -> p a e").bitcast(I32))
+        w1_rows = w1.rearrange("(a p j) c -> a p j c", p=P, j=4)
+        w1_raw = [keep.tile([P, 4, H], F32, name="w1_raw_%d" % a) for a in range(PASSES)]
+        nc.sync.dma_start(w1_raw[0][:], w1_rows[0])
         for q in range(4):
             nc.sync.dma_start(
-                ws_in[32 * q : 32 * q + 4, 0:PASSES, :],
+                w4_s[32 * q : 32 * q + 4, :, :].bitcast(I32),
                 w4_scales[:, 4 * q : 4 * q + 4, :].rearrange("a r e -> r a e").bitcast(I32),
             )
-        nc.sync.dma_start(w4_in[:], w4_words.rearrange("a p e -> p a e").bitcast(I32))
-
-        def deal(source, name):
-            rows, width = source.shape[1], source.shape[2]
-            dealt = keep.tile([P, rows, width], I32, name=name, align_bytes=64)
-            nc.vector.tensor_copy(
-                dealt[:].rearrange("p a (t g i) -> p a t g i", t=4, g=16),
-                source[:].rearrange("p a (g t i) -> p a t g i", t=4, g=16),
-            )
-            return dealt
 
         def gather_scales(lst, name):
             picked = keep.tile([P, S], U8, name=name, align_bytes=64)
             nc.vector.tensor_copy(picked[:], tab_s[:].indirect(lst[:]))
             return picked
 
-        def gather_words(lst, a, first, count, name, tag):
-            words = keep.tile([P, count], U32, name=name, tag=tag, align_bytes=64)
-            offsets = lst[:, first // 16 : (first + count) // 16]
-            nc.vector.tensor_copy(words[:], tab_w[:, a, :].bitcast(U32).indirect(offsets))
-            return [words[:, j : j + P] for j in range(0, count, P)]
+        def gather_words(lst, half, names):
+            offsets = lst[:, (S // 32) * half : (S // 32) * (half + 1)]
+            picked = []
+            for a in range(PASSES):
+                words = keep.tile([P, S // 2], U32, name="words", tag=names % (2 * half + a), align_bytes=64)
+                nc.vector.tensor_copy(words[:], tab_w[:, a, :].bitcast(U32).indirect(offsets))
+                picked.append(words)
+            return [[w[:, j : j + P] for w in picked] for j in range(0, S // 2, P)]
 
         now_s = gather_scales(list_now, "now_s")
         for r in range(4):
             nc.sync.dma_start(now_s1[r:P:32, :].bitcast(I32), now_s[4 + r : P : 32, :].bitcast(I32))
         future_s = gather_scales(list_future, "future_s")
 
-        nc.sync.dma_start(raw[:, 1], w1_rows[1])
+        nc.sync.dma_start(w1_raw[1][:], w1_rows[1])
         nc.sync.dma_start(list_past[:], offs)
+        wd_raw = keep.tile([P, 4, N], F32, name="wd_raw")
         wd_rows = wd.rearrange("(g t i) n -> t g i n", t=4, i=8)
         for t in range(4):
-            nc.sync.dma_start(raw[:, PASSES, t, :], wd_rows[t])
+            nc.sync.dma_start(wd_raw[:, t, :], wd_rows[t])
 
-        w8_w = deal(w8_in, "w8_w")
-        future_w = [gather_words(list_future, a, 0, S, "future_w_%d" % a, "future_w_%d" % a) for a in range(PASSES)]
-        w_s = deal(ws_in, "w_s")[:].bitcast(U8)
-        w4_w = deal(w4_in, "w4_w")
-        now_w = [gather_words(list_now, a, 0, S, "now_w_%d" % a, "now_w_%d" % a) for a in range(PASSES)]
-        past_s = gather_scales(list_past, "past_s")
-        past_w = [gather_words(list_past, 0, 0, S, "past_w_0", "past_w_0")]
+        future_w, now_w = [], []
+        for half in range(2):
+            future_w.extend(gather_words(list_future, half, "future_w_%d"))
+            now_w.extend(gather_words(list_now, half, "now_w_%d"))
+
+        def round_on_gpsimd(grouped, raw):
+            width = grouped.shape[1]
+            for c in range(0, width, P):
+                nc.gpsimd.tensor_scalar(
+                    grouped[:, c : c + P, :], raw[:, :, c : c + P].rearrange("p j c -> p c j"), 1.0, 0.0, ALU.mult, ALU.add
+                )
 
         def quantize(codes, scales, values):
             nc.vector.quantize_mx(out=codes.bitcast(FP8X4), scales=scales, in_=values)
 
-        def w4_pass(a, t, i):
-            rows, cols = slice(P * t, P * (t + 1)), slice(P * i, P * (i + 1))
-            plane = now_s if a == 0 else now_s1
-            return w4_w[:, a, 64 * t : 64 * (t + 1)].bitcast(FP4X4), w_s[:, a, rows], now_w[a][i], plane[:, cols]
-
-        def w8_pass(a, t, i):
-            rows, cols = slice(P * t, P * (t + 1)), slice(P * i, P * (i + 1))
-            return w8_w[:, a, rows].bitcast(FP8X4), w_s[4 * a :, PASSES, rows], future_w[a][i], future_s[4 * a :, cols]
-
-        def w1_pass(a, t, i):
-            rows, cols = slice(P * t, P * (t + 1)), slice(P * i, P * (i + 1))
-            return w1_codes[:, a, rows].bitcast(FP8X4), w1_s[:, a, rows], past_w[a][i], past_s[4 * a :, cols]
-
-        def project(i, bank_number, products):
-            bank = psum.tile([P, 4, P], F32, name="bank", tag="bank%d" % bank_number)
-            for t in range(4):
-                passes = [product(a, t, i) for product in products for a in range(PASSES)]
-                for n, (weights, weight_scales, words, word_scales) in enumerate(passes):
-                    nc.tensor.matmul_mx(
-                        out=bank[:, t, :],
-                        lhsT=weights,
-                        lhsT_scale=weight_scales,
-                        rhs=words.bitcast(FP8X4),
-                        rhs_scale=word_scales,
-                        start=(n == 0),
-                        stop=(n == len(passes) - 1),
-                    )
-            return bank
-
-        def size_of(difference, name):
-            size = keep.tile([P, P, 4], F32, name=name)
-            nc.scalar.activation(size[:], difference[:].rearrange("p t j -> p j t"), ACT.Abs)
-            return size
-
         w1_codes = keep.tile([P, PASSES, H], U32, name="w1_codes", align_bytes=64)
         w1_s = keep.tile([P, PASSES, H], U8, name="w1_s", align_bytes=64)
         for a in range(PASSES):
-            w1_bf = keep.tile([P, 4 * H], BF16, name="w1_bf_%d" % a, align_bytes=64)
-            rounded = w1_bf[:].rearrange("p (t g i j) -> p t g i j", t=4, g=16, i=8)
-            source = raw[:, a].rearrange("p j (g t i) -> p t g i j", t=4, g=16)
-            for t in range(4):
-                nc.scalar.activation(rounded[:, t], source[:, t], ACT.Copy, scale=-1.0)
-            quantize(w1_codes[:, a, :], w1_s[:, a, :], w1_bf[:])
-
+            for c in range(2):
+                cols = slice((H // 2) * c, (H // 2) * (c + 1))
+                grouped = keep.tile([P, H // 2, 4], BF16, name="w1_bf", tag="past_w_%d" % (2 * c + a), align_bytes=64)
+                round_on_gpsimd(grouped, w1_raw[a][:, :, cols])
+                quantize(w1_codes[:, a, cols], w1_s[:, a, cols], grouped[:].rearrange("p c j -> p (c j)"))
         wd_bf = keep.tile([P, N, 4], BF16, name="wd_bf", align_bytes=64)
-        nc.scalar.copy(
-            wd_bf[:].rearrange("p (c i) t -> p c t i", i=4), raw[:, PASSES].rearrange("p t (c i) -> p c t i", i=4)
-        )
+        round_on_gpsimd(wd_bf, wd_raw[:])
         wd_codes = keep.tile([P, N], U32, name="wd_codes", align_bytes=64)
         wd_s = keep.tile([P, N], U8, name="wd_s", align_bytes=64)
         quantize(wd_codes[:], wd_s[:], wd_bf[:].rearrange("p c t -> p (c t)"))
 
-        c_banks = [project(i, 2 + i, [w8_pass]) for i in range(TILES - 2)]
-        b_sb = keep.tile([P, TILES, 4, P], F32, name="b_sb", tag="raw_then_b")
-        for i in range(TILES):
-            b_bank = project(i, i % 2, [w4_pass])
-            nc.scalar.copy(b_sb[:, i], b_bank[:])
-        c_banks.extend(project(i, i % 2, [w8_pass]) for i in range(TILES - 2, TILES))
+        past_s = gather_scales(list_past, "past_s")
+        past_w = gather_words(list_past, 0, "past_w_%d") + gather_words(list_past, 1, "past_w_%d")
 
-        second = []
-        for i in range(TILES):
-            v = ring.tile([P, 4, P], F32, name="v")
-            nc.vector.tensor_tensor(v[:], c_banks[i][:], b_sb[:, i], ALU.subtract)
-            second.append(size_of(v, "second_%d" % i))
+        def project(i, words, word_scales, weights, weight_scales):
+            bank = psum.tile([P, H], F32, name="bank", tag="product%d" % (i % HALF))
+            for a in range(PASSES):
+                nc.tensor.matmul_mx(
+                    out=bank[:],
+                    lhsT=words[i][a].bitcast(FP8X4),
+                    lhsT_scale=word_scales[a][:, P * i : P * (i + 1)],
+                    rhs=weights[a],
+                    rhs_scale=weight_scales[a],
+                    start=(a == 0),
+                    stop=(a == PASSES - 1),
+                )
+            return bank[:].rearrange("j (g t i) -> j t g i", t=4, i=8)
 
-        past_w.append([])
+        def size_of_sum(i, terms, name):
+            bank = psum.tile([P, 4, P], F32, name="bank", tag="turned%d" % (i % 2))
+            for t in range(4):
+                for n, term in enumerate(terms):
+                    nc.tensor.matmul(
+                        bank[:, t, :],
+                        lhsT=term[:, t].rearrange("j g i -> j (g i)"),
+                        rhs=ident[:],
+                        is_transpose=True,
+                        start=(n == 0),
+                        stop=(n == len(terms) - 1),
+                    )
+            size = keep.tile([P, P, 4], F32, name="%s_%d" % (name, i))
+            nc.scalar.activation(size[:], bank[:].rearrange("p t j -> p j t"), ACT.Abs)
+            return size
+
+        def dealt_tile(name, i):
+            return keep.tile([P, 4, 16, 8], F32, name="%s_%d" % (name, i))
+
+        minus_b, second = [], []
         for half in range(2):
-            name = "past_w_1_%d" % half
-            past_w[1].extend(gather_words(list_past, 1, (S // 2) * half, S // 2, name, "future_w_%d" % half))
+            tiles = range(HALF * half, HALF * (half + 1))
+            c_sb = {}
+            for i in tiles:
+                c = project(
+                    i,
+                    future_w,
+                    [future_s[4 * a :, :] for a in range(PASSES)],
+                    [w8_w[:, a, :].bitcast(FP8X4) for a in range(PASSES)],
+                    [w8_s[4 * a :, :] for a in range(PASSES)],
+                )
+                c_sb[i] = dealt_tile("c", i)
+                nc.scalar.copy(c_sb[i][:], c)
+            for i in tiles:
+                b = project(
+                    i,
+                    now_w,
+                    [now_s[:], now_s1[:]],
+                    [w4_w[:, a, :].bitcast(FP4X4) for a in range(PASSES)],
+                    [w4_s[:, a, :] for a in range(PASSES)],
+                )
+                minus_b.append(dealt_tile("minus_b", i))
+                nc.scalar.activation(minus_b[i][:], b, ACT.Copy, scale=-1.0)
+                second.append(size_of_sum(i, [minus_b[i], c_sb[i]], "second"))
 
         first = []
 
         def first_size(i):
-            if i < TILES - 2:
-                a_bank = project(i, 2 + i % 4, [w1_pass])
-                u = ring.tile([P, 4, P], F32, name="u")
-                nc.vector.tensor_tensor(u[:], a_bank[:], b_sb[:, i], ALU.add)
+            a_sum = project(
+                i,
+                past_w,
+                [past_s[4 * a :, :] for a in range(PASSES)],
+                [w1_codes[:, a, :].bitcast(FP8X4) for a in range(PASSES)],
+                [w1_s[:, a, :] for a in range(PASSES)],
+            )
+            a_sb = dealt_tile("a", i)
+            if i < HALF:
+                nc.scalar.copy(a_sb[:], a_sum)
+                first.append(size_of_sum(i, [a_sb, minus_b[i]], "first"))
             else:
-                u = project(i, i % 2, [w4_pass, w1_pass])
-            first.append(size_of(u, "first_%d" % i))
+                nc.vector.tensor_tensor(a_sb[:], a_sum, minus_b[i][:], ALU.add)
+                first.append(size_of_sum(i, [a_sb], "first"))
 
         out_rows = out.rearrange("(g m p) j -> p g m j", g=2, p=P)
 
@@ -202,7 +218,7 @@ def tile_list_patch_motion_acceleration_kernel(
             h_s = keep.tile([P, width], U8, name="h_s_%d" % tiles[0], align_bytes=64)
             quantize(h_codes[:], h_s[:], h[:].rearrange("p f j t -> p (f j t)"))
             for g in range(2):
-                o_bank = psum.tile([P, 2, width], F32, name="o_bank", tag="bank%d" % (6 + g))
+                o_bank = psum.tile([P, 2, width], F32, name="o_bank", tag="decoded%d" % g)
                 for m in range(2):
                     rows = slice(P * (2 * g + m), P * (2 * g + m + 1))
                     nc.tensor.matmul_mx(
@@ -215,7 +231,7 @@ def tile_list_patch_motion_acceleration_kernel(
                         stop=True,
                     )
                 o_sb = keep.tile([P, 2, width], F32, name="o_sb_%d_%d" % (tiles[0], g))
-                if tiles[0] >= TILES // 2 and g == 1:
+                if tiles[0] >= HALF and g == 1:
                     nc.vector.tensor_copy(o_sb[:], o_bank[:])
                 else:
                     nc.scalar.copy(o_sb[:], o_bank[:])

@@ -21,6 +21,7 @@ P = 128
 PASSES = K // 512
 TILES = S // P
 HALF = TILES // 2
+CHUNKS = ((0, 256), (256, 512), (512, 1024))
 
 
 def tile_list_patch_motion_acceleration_kernel(
@@ -42,12 +43,14 @@ def tile_list_patch_motion_acceleration_kernel(
         w4_s = keep.tile([P, PASSES, H], U8, name="w4_s", align_bytes=64)
         w8_s = keep.tile([P, H], U8, name="w8_s", align_bytes=64)
         ident = keep.tile([P, P], F32, name="ident", align_bytes=64)
+        w1_raw = [keep.tile([P, 4, H], F32, name="w1_raw_%d" % a) for a in range(PASSES)]
+        wd_raw = keep.tile([P, 4, N], F32, name="wd_raw")
 
         nc.gpsimd.memset(tab_s[:].bitcast(I32), 0)
         make_identity(nc, ident[:])
         nc.vector.memset(w8_s[:].bitcast(I32), 0)
         nc.vector.memset(w4_s[:].bitcast(I32), 0)
-        nc.vector.memset(now_s1[:].bitcast(I32), 0)
+        nc.vector.memset(now_s1[96:P, :].bitcast(I32), 0)
 
         nc.sync.dma_start(list_now[:], offs2)
         for q in range(4):
@@ -62,75 +65,65 @@ def tile_list_patch_motion_acceleration_kernel(
                 w8_s[32 * q : 32 * q + 4 * PASSES, :].bitcast(I32), w8_scales[:, 4 * q : 4 * q + 4, :].bitcast(I32)
             )
         nc.sync.dma_start(w4_w[:].bitcast(I32), w4_words.rearrange("a p e -> p a e").bitcast(I32))
-        w1_rows = w1.rearrange("(a p j) c -> a p j c", p=P, j=4)
-        w1_raw = [keep.tile([P, 4, H], F32, name="w1_raw_%d" % a) for a in range(PASSES)]
-        nc.sync.dma_start(w1_raw[0][:], w1_rows[0])
-        for q in range(4):
-            nc.sync.dma_start(
-                w4_s[32 * q : 32 * q + 4, :, :].bitcast(I32),
-                w4_scales[:, 4 * q : 4 * q + 4, :].rearrange("a r e -> r a e").bitcast(I32),
-            )
 
         def gather_scales(lst, name):
             picked = keep.tile([P, S], U8, name=name, align_bytes=64)
             nc.vector.tensor_copy(picked[:], tab_s[:].indirect(lst[:]))
             return picked
 
-        def gather_words(lst, half, names):
-            offsets = lst[:, (S // 32) * half : (S // 32) * (half + 1)]
-            picked = []
-            for a in range(PASSES):
-                words = keep.tile([P, S // 2], U32, name="words", tag=names % (2 * half + a), align_bytes=64)
-                nc.vector.tensor_copy(words[:], tab_w[:, a, :].bitcast(U32).indirect(offsets))
-                picked.append(words)
-            return [[w[:, j : j + P] for w in picked] for j in range(0, S // 2, P)]
-
         now_s = gather_scales(list_now, "now_s")
-        for r in range(4):
-            nc.sync.dma_start(now_s1[r:P:32, :].bitcast(I32), now_s[4 + r : P : 32, :].bitcast(I32))
+        nc.sync.dma_start(now_s1[0 : P - 4, :].bitcast(I32), now_s[4:P, :].bitcast(I32))
         future_s = gather_scales(list_future, "future_s")
 
-        nc.sync.dma_start(w1_raw[1][:], w1_rows[1])
+        for q in range(4):
+            nc.sync.dma_start(
+                w4_s[32 * q : 32 * q + 4, :, :].bitcast(I32),
+                w4_scales[:, 4 * q : 4 * q + 4, :].rearrange("a r e -> r a e").bitcast(I32),
+            )
+        w1_rows = w1.rearrange("(a p j) c -> a p j c", p=P, j=4)
+        nc.sync.dma_start(w1_raw[0][:], w1_rows[0])
         nc.sync.dma_start(list_past[:], offs)
-        wd_raw = keep.tile([P, 4, N], F32, name="wd_raw")
+        nc.sync.dma_start(w1_raw[1][:], w1_rows[1])
         wd_rows = wd.rearrange("(g t i) n -> t g i n", t=4, i=8)
         for t in range(4):
             nc.sync.dma_start(wd_raw[:, t, :], wd_rows[t])
 
-        future_w, now_w = [], []
-        for half in range(2):
-            future_w.extend(gather_words(list_future, half, "future_w_%d"))
-            now_w.extend(gather_words(list_now, half, "now_w_%d"))
+        def gather_words(lst, chunk, tags):
+            start, end = CHUNKS[chunk]
+            picked = []
+            for a in range(PASSES):
+                words = keep.tile([P, end - start], U32, name="words", tag=tags[a], align_bytes=64)
+                nc.vector.tensor_copy(words[:], tab_w[:, a, :].bitcast(U32).indirect(lst[:, start // 16 : end // 16]))
+                picked.append(words)
+            return [[w[:, j : j + P] for w in picked] for j in range(0, end - start, P)]
 
-        def round_on_gpsimd(grouped, raw):
-            width = grouped.shape[1]
-            for c in range(0, width, P):
-                nc.gpsimd.tensor_scalar(
-                    grouped[:, c : c + P, :], raw[:, :, c : c + P].rearrange("p j c -> p c j"), 1.0, 0.0, ALU.mult, ALU.add
-                )
+        future_w, now_w = [], []
+        for chunk in range(len(CHUNKS)):
+            future_w.extend(gather_words(list_future, chunk, ["future_w_%d_%d" % (chunk, a) for a in range(PASSES)]))
+            now_w.extend(gather_words(list_now, chunk, ["now_w_%d_%d" % (chunk, a) for a in range(PASSES)]))
+        past_s = gather_scales(list_past, "past_s")
 
         def quantize(codes, scales, values):
             nc.vector.quantize_mx(out=codes.bitcast(FP8X4), scales=scales, in_=values)
 
+        def woven(grouped, raw):
+            return grouped.rearrange("p (c i) t -> p c t i", i=4), raw.rearrange("p t (c i) -> p c t i", i=4)
+
         w1_codes = keep.tile([P, PASSES, H], U32, name="w1_codes", align_bytes=64)
         w1_s = keep.tile([P, PASSES, H], U8, name="w1_s", align_bytes=64)
-        for a in range(PASSES):
-            for c in range(2):
-                cols = slice((H // 2) * c, (H // 2) * (c + 1))
-                grouped = keep.tile([P, H // 2, 4], BF16, name="w1_bf", tag="past_w_%d" % (2 * c + a), align_bytes=64)
-                round_on_gpsimd(grouped, w1_raw[a][:, :, cols])
-                quantize(w1_codes[:, a, cols], w1_s[:, a, cols], grouped[:].rearrange("p c j -> p (c j)"))
-        wd_bf = keep.tile([P, N, 4], BF16, name="wd_bf", align_bytes=64)
-        round_on_gpsimd(wd_bf, wd_raw[:])
-        wd_codes = keep.tile([P, N], U32, name="wd_codes", align_bytes=64)
-        wd_s = keep.tile([P, N], U8, name="wd_s", align_bytes=64)
-        quantize(wd_codes[:], wd_s[:], wd_bf[:].rearrange("p c t -> p (c t)"))
+        halves = [(a, c) for a in range(PASSES) for c in range(2)]
+        w1_bf = []
+        for n, (a, c) in enumerate(halves):
+            w1_bf.append(keep.tile([P, H // 2, 4], BF16, name="w1_bf", tag="stage_%d" % n, align_bytes=64))
+            nc.vector.tensor_copy(*woven(w1_bf[n][:], w1_raw[a][:, :, (H // 2) * c : (H // 2) * (c + 1)]))
+        for n, (a, c) in enumerate(halves):
+            cols = slice((H // 2) * c, (H // 2) * (c + 1))
+            quantize(w1_codes[:, a, cols], w1_s[:, a, cols], w1_bf[n][:].rearrange("p c j -> p (c j)"))
 
-        past_s = gather_scales(list_past, "past_s")
-        past_w = gather_words(list_past, 0, "past_w_%d") + gather_words(list_past, 1, "past_w_%d")
+        past_w = gather_words(list_past, 0, ["stage_2", "stage_3"]) + gather_words(list_past, 1, ["stage_0", "stage_1"])
 
-        def project(i, words, word_scales, weights, weight_scales):
-            bank = psum.tile([P, H], F32, name="bank", tag="product%d" % (i % HALF))
+        def project(bank_tag, i, words, word_scales, weights, weight_scales):
+            bank = psum.tile([P, H], F32, name="bank", tag="product%d" % bank_tag)
             for a in range(PASSES):
                 nc.tensor.matmul_mx(
                     out=bank[:],
@@ -163,11 +156,12 @@ def tile_list_patch_motion_acceleration_kernel(
             return keep.tile([P, 4, 16, 8], F32, name="%s_%d" % (name, i))
 
         minus_b, second = [], []
-        for half in range(2):
-            tiles = range(HALF * half, HALF * (half + 1))
+        for pair in range(TILES // 2):
+            tiles = (2 * pair, 2 * pair + 1)
             c_sb = {}
             for i in tiles:
                 c = project(
+                    i % 2,
                     i,
                     future_w,
                     [future_s[4 * a :, :] for a in range(PASSES)],
@@ -178,6 +172,7 @@ def tile_list_patch_motion_acceleration_kernel(
                 nc.scalar.copy(c_sb[i][:], c)
             for i in tiles:
                 b = project(
+                    2 + i % 2,
                     i,
                     now_w,
                     [now_s[:], now_s1[:]],
@@ -186,27 +181,44 @@ def tile_list_patch_motion_acceleration_kernel(
                 )
                 minus_b.append(dealt_tile("minus_b", i))
                 nc.scalar.activation(minus_b[i][:], b, ACT.Copy, scale=-1.0)
+            for i in tiles:
                 second.append(size_of_sum(i, [minus_b[i], c_sb[i]], "second"))
+
+        wd_codes = keep.tile([P, N], U32, name="wd_codes", align_bytes=64)
+        wd_s = keep.tile([P, N], U8, name="wd_s", align_bytes=64)
+        for c in range(2):
+            wd_bf = keep.tile([P, N // 2, 4], BF16, name="wd_bf", tag="wd_stage_%d" % c, align_bytes=64)
+            for piece in range(2):
+                start = (N // 2) * c + P * piece
+                nc.scalar.copy(*woven(wd_bf[:, P * piece : P * (piece + 1), :], wd_raw[:, :, start : start + P]))
+            cols = slice((N // 2) * c, (N // 2) * (c + 1))
+            quantize(wd_codes[:, cols], wd_s[:, cols], wd_bf[:].rearrange("p c t -> p (c t)"))
+        past_w.extend(gather_words(list_past, 2, ["wd_stage_0", "wd_stage_1"]))
 
         first = []
 
-        def first_size(i):
-            a_sum = project(
-                i,
-                past_w,
-                [past_s[4 * a :, :] for a in range(PASSES)],
-                [w1_codes[:, a, :].bitcast(FP8X4) for a in range(PASSES)],
-                [w1_s[:, a, :] for a in range(PASSES)],
-            )
-            a_sb = dealt_tile("a", i)
-            if i < HALF:
-                nc.scalar.copy(a_sb[:], a_sum)
-                first.append(size_of_sum(i, [a_sb, minus_b[i]], "first"))
-            else:
-                nc.vector.tensor_tensor(a_sb[:], a_sum, minus_b[i][:], ALU.add)
-                first.append(size_of_sum(i, [a_sb], "first"))
+        def first_sizes(tiles):
+            terms = {}
+            for i in tiles:
+                a_sum = project(
+                    i % 4,
+                    i,
+                    past_w,
+                    [past_s[4 * a :, :] for a in range(PASSES)],
+                    [w1_codes[:, a, :].bitcast(FP8X4) for a in range(PASSES)],
+                    [w1_s[:, a, :] for a in range(PASSES)],
+                )
+                a_sb = dealt_tile("a", i)
+                if i < HALF:
+                    nc.scalar.copy(a_sb[:], a_sum)
+                    terms[i] = [a_sb, minus_b[i]]
+                else:
+                    nc.vector.tensor_tensor(a_sb[:], a_sum, minus_b[i][:], ALU.add)
+                    terms[i] = [a_sb]
+            for i in tiles:
+                first.append(size_of_sum(i, terms[i], "first"))
 
-        out_rows = out.rearrange("(g m p) j -> p g m j", g=2, p=P)
+        out_rows = out.rearrange("(m p) j -> p m j", p=P)
 
         def decode(tiles):
             width = P * len(tiles)
@@ -217,10 +229,11 @@ def tile_list_patch_motion_acceleration_kernel(
             h_codes = keep.tile([P, width], U32, name="h_codes_%d" % tiles[0], align_bytes=64)
             h_s = keep.tile([P, width], U8, name="h_s_%d" % tiles[0], align_bytes=64)
             quantize(h_codes[:], h_s[:], h[:].rearrange("p f j t -> p (f j t)"))
-            for g in range(2):
-                o_bank = psum.tile([P, 2, width], F32, name="o_bank", tag="decoded%d" % g)
-                for m in range(2):
-                    rows = slice(P * (2 * g + m), P * (2 * g + m + 1))
+            per_bank = 4 // len(tiles)
+            for g in range(len(tiles)):
+                o_bank = psum.tile([P, per_bank, width], F32, name="o_bank", tag="decoded%d" % ((tiles[0] + g) % 2))
+                for m in range(per_bank):
+                    rows = slice(P * (per_bank * g + m), P * (per_bank * g + m + 1))
                     nc.tensor.matmul_mx(
                         out=o_bank[:, m, :],
                         lhsT=wd_codes[:, rows].bitcast(FP8X4),
@@ -230,16 +243,12 @@ def tile_list_patch_motion_acceleration_kernel(
                         start=True,
                         stop=True,
                     )
-                o_sb = keep.tile([P, 2, width], F32, name="o_sb_%d_%d" % (tiles[0], g))
-                if tiles[0] >= HALF and g == 1:
-                    nc.vector.tensor_copy(o_sb[:], o_bank[:])
-                else:
-                    nc.scalar.copy(o_sb[:], o_bank[:])
-                nc.sync.dma_start(out_rows[:, g, :, cols], o_sb[:])
+                o_sb = keep.tile([P, per_bank, width], F32, name="o_sb_%d_%d" % (tiles[0], g))
+                nc.scalar.copy(o_sb[:], o_bank[:])
+                nc.sync.dma_start(out_rows[:, per_bank * g : per_bank * (g + 1), cols], o_sb[:])
 
         for pair in range(TILES // 2):
-            first_size(2 * pair)
-            first_size(2 * pair + 1)
+            first_sizes((2 * pair, 2 * pair + 1))
             if pair > 0:
                 decode([2 * pair - 2, 2 * pair - 1])
         decode([TILES - 2])

@@ -46,7 +46,7 @@ def tile_list_patch_motion_acceleration_kernel(
         w1_raw = [keep.tile([P, 4, H], F32, name="w1_raw_%d" % a) for a in range(PASSES)]
         wd_raw = keep.tile([P, 4, N], F32, name="wd_raw")
 
-        nc.gpsimd.memset(tab_s[:].bitcast(I32), 0)
+        nc.vector.memset(tab_s[:].bitcast(I32), 0)
         make_identity(nc, ident[:])
         nc.vector.memset(w8_s[:].bitcast(I32), 0)
         nc.vector.memset(w4_s[:].bitcast(I32), 0)
@@ -72,7 +72,7 @@ def tile_list_patch_motion_acceleration_kernel(
             return picked
 
         now_s = gather_scales(list_now, "now_s")
-        nc.sync.dma_start(now_s1[0 : P - 4, :].bitcast(I32), now_s[4:P, :].bitcast(I32))
+        nc.sync.dma_start(now_s1[0:100, :].bitcast(I32), now_s[4:104, :].bitcast(I32))
         future_s = gather_scales(list_future, "future_s")
 
         for q in range(4):

@@ -21,7 +21,7 @@ P = 128
 PASSES = K // 512
 TILES = S // P
 HALF = TILES // 2
-CHUNKS = ((0, 256), (256, 512), (512, 1024))
+REPEATED = (6, 7)
 
 
 def tile_list_patch_motion_acceleration_kernel(
@@ -32,112 +32,126 @@ def tile_list_patch_motion_acceleration_kernel(
         keep = ctx.enter_context(tc.tile_pool(name="keep", bufs=1))
         psum = ctx.enter_context(tc.psum_pool(name="psum", bufs=1))
 
+        def sb(shape, dtype, name, tag=None):
+            return keep.tile(shape, dtype, name=name, tag=tag or name, align_bytes=64)
+
         list_past = keep.tile([P, S // 16], U16, name="list_past")
         list_now = keep.tile([P, S // 16], U16, name="list_now")
         list_future = keep.tile([P, S // 16], U16, name="list_future")
-        tab_w = keep.tile([P, PASSES, T], I32, name="tab_w", align_bytes=64)
-        tab_s = keep.tile([P, T], U8, name="tab_s", align_bytes=64)
-        now_s1 = keep.tile([P, S], U8, name="now_s1", align_bytes=64)
-        w4_w = keep.tile([P, PASSES, 2 * H], U8, name="w4_w", align_bytes=64)
-        w8_w = keep.tile([P, PASSES, H], I32, name="w8_w", align_bytes=64)
-        w4_s = keep.tile([P, PASSES, H], U8, name="w4_s", align_bytes=64)
-        w8_s = keep.tile([P, H], U8, name="w8_s", align_bytes=64)
-        ident = keep.tile([P, P], F32, name="ident", align_bytes=64)
-        w1_raw = [keep.tile([P, 4, H], F32, name="w1_raw_%d" % a) for a in range(PASSES)]
-        wd_raw = keep.tile([P, 4, N], F32, name="wd_raw")
+        tab_w = [sb([P, T], I32, "tab_w_%d" % a) for a in range(PASSES)]
+        tab_s = sb([P, T], U8, "tab_s")
+        now_s1 = [sb([P, S // 2], U8, "now_s1_%d" % u) for u in range(2)]
+        w4_w = sb([P, PASSES, 2 * H], U8, "w4_w")
+        w8_w = [sb([P, H], I32, "w8_w_%d" % a) for a in range(PASSES)]
+        w4_s = sb([P, PASSES, H], U8, "w4_s")
+        w8_s = sb([P, H], U8, "w8_s")
+        ident = sb([P, P], F32, "ident")
+        w1_raw = [sb([P, 4, H], F32, "w1_raw_%d" % a) for a in range(PASSES)]
+        wd_raw = sb([P, 4, N], F32, "wd_raw")
 
         nc.vector.memset(tab_s[:].bitcast(I32), 0)
         make_identity(nc, ident[:])
         nc.vector.memset(w8_s[:].bitcast(I32), 0)
         nc.vector.memset(w4_s[:].bitcast(I32), 0)
-        nc.vector.memset(now_s1[96:P, :].bitcast(I32), 0)
+        for u in range(2):
+            nc.vector.memset(now_s1[u][96:P, :].bitcast(I32), 0)
 
+        tab_rows = tab_words.rearrange("a p t i -> a p (t i)").bitcast(I32)
+        w8_rows = w8_words.rearrange("a p e i -> a p (e i)").bitcast(I32)
         nc.sync.dma_start(list_now[:], offs2)
         for q in range(4):
             nc.sync.dma_start(
                 tab_s[32 * q : 32 * q + 4 * PASSES, :].bitcast(I32), tab_scales[:, 4 * q : 4 * q + 4, :].bitcast(I32)
             )
         nc.sync.dma_start(list_future[:], offs3)
-        nc.sync.dma_start(tab_w[:], tab_words.rearrange("a p t i -> p a (t i)").bitcast(I32))
-        nc.sync.dma_start(w8_w[:], w8_words.rearrange("a p e i -> p a (e i)").bitcast(I32))
+        nc.sync.dma_start(tab_w[0][:], tab_rows[0])
+        nc.sync.dma_start(w8_w[0][:], w8_rows[0])
         for q in range(4):
             nc.sync.dma_start(
                 w8_s[32 * q : 32 * q + 4 * PASSES, :].bitcast(I32), w8_scales[:, 4 * q : 4 * q + 4, :].bitcast(I32)
             )
-        nc.sync.dma_start(w4_w[:].bitcast(I32), w4_words.rearrange("a p e -> p a e").bitcast(I32))
+        nc.sync.dma_start(tab_w[1][:], tab_rows[1])
+        nc.sync.dma_start(w8_w[1][:], w8_rows[1])
 
-        def gather_scales(lst, name):
-            picked = keep.tile([P, S], U8, name=name, align_bytes=64)
-            nc.vector.tensor_copy(picked[:], tab_s[:].indirect(lst[:]))
+        def gather(window, dtype, lst, start, end, picked):
+            nc.vector.tensor_copy(picked, window[:].bitcast(dtype).indirect(lst[:, start // 16 : end // 16]))
+
+        def gather_scales(lst, u, name, tag=None):
+            picked = sb([P, S // 2], U8, name, tag)
+            gather(tab_s, U8, lst, (S // 2) * u, (S // 2) * (u + 1), picked[:])
             return picked
 
-        now_s = gather_scales(list_now, "now_s")
-        nc.sync.dma_start(now_s1[0:100, :].bitcast(I32), now_s[4:104, :].bitcast(I32))
-        future_s = gather_scales(list_future, "future_s")
+        def gather_words(lst, a, start, end, name, tag=None):
+            picked = sb([P, end - start], U32, name, tag)
+            gather(tab_w[a], U32, lst, start, end, picked[:])
+            return [picked[:, j : j + P] for j in range(0, end - start, P)]
 
+        def move_up(u):
+            nc.sync.dma_start(now_s1[u][0:100, :].bitcast(I32), now_s[u][4:104, :].bitcast(I32))
+
+        now_s = [gather_scales(list_now, 0, "now_s_0")]
+        move_up(0)
+        nc.sync.dma_start(w4_w[:].bitcast(I32), w4_words.rearrange("a p e -> p a e").bitcast(I32))
         for q in range(4):
             nc.sync.dma_start(
                 w4_s[32 * q : 32 * q + 4, :, :].bitcast(I32),
                 w4_scales[:, 4 * q : 4 * q + 4, :].rearrange("a r e -> r a e").bitcast(I32),
             )
         w1_rows = w1.rearrange("(a p j) c -> a p j c", p=P, j=4)
-        nc.sync.dma_start(w1_raw[0][:], w1_rows[0])
+        for a in range(PASSES):
+            nc.sync.dma_start(w1_raw[a][:], w1_rows[a])
         nc.sync.dma_start(list_past[:], offs)
-        nc.sync.dma_start(w1_raw[1][:], w1_rows[1])
         wd_rows = wd.rearrange("(g t i) n -> t g i n", t=4, i=8)
         for t in range(4):
             nc.sync.dma_start(wd_raw[:, t, :], wd_rows[t])
 
-        def gather_words(lst, chunk, tags):
-            start, end = CHUNKS[chunk]
-            picked = []
-            for a in range(PASSES):
-                words = keep.tile([P, end - start], U32, name="words", tag=tags[a], align_bytes=64)
-                nc.vector.tensor_copy(words[:], tab_w[:, a, :].bitcast(U32).indirect(lst[:, start // 16 : end // 16]))
-                picked.append(words)
-            return [[w[:, j : j + P] for w in picked] for j in range(0, end - start, P)]
+        future_s = [gather_scales(list_future, 0, "future_s_0")]
+        future_w = [gather_words(list_future, 0, 0, 512, "future_w_0")]
+        now_w = [gather_words(list_now, 0, 0, 512, "now_w_0")]
+        future_w.append(
+            gather_words(list_future, 1, 0, 256, "future_w_1a") + gather_words(list_future, 1, 256, 512, "future_w_1b")
+        )
+        now_w.append(gather_words(list_now, 1, 0, 512, "now_w_1"))
 
-        future_w, now_w = [], []
-        for chunk in range(len(CHUNKS)):
-            future_w.extend(gather_words(list_future, chunk, ["future_w_%d_%d" % (chunk, a) for a in range(PASSES)]))
-            now_w.extend(gather_words(list_now, chunk, ["now_w_%d_%d" % (chunk, a) for a in range(PASSES)]))
-        past_s = gather_scales(list_past, "past_s")
+        def mx_pass(bank, i, words, word_scales, weights, weight_scales, start, stop):
+            cols = slice(P * (i % HALF), P * (i % HALF + 1))
+            nc.tensor.matmul_mx(
+                out=bank[:],
+                lhsT=words.bitcast(FP8X4),
+                lhsT_scale=word_scales[:, cols],
+                rhs=weights,
+                rhs_scale=weight_scales,
+                start=start,
+                stop=stop,
+            )
 
-        def quantize(codes, scales, values):
-            nc.vector.quantize_mx(out=codes.bitcast(FP8X4), scales=scales, in_=values)
+        def c_pass(bank, i, a):
+            mx_pass(
+                bank, i, future_w[a][i], future_s[i // HALF][4 * a :, :], w8_w[a][:].bitcast(FP8X4), w8_s[4 * a :, :],
+                a == 0, a == PASSES - 1,
+            )
 
-        def woven(grouped, raw):
-            return grouped.rearrange("p (c i) t -> p c t i", i=4), raw.rearrange("p t (c i) -> p c t i", i=4)
+        def b_pass(bank, i, a, start, stop):
+            plane = [now_s, now_s1][a][i // HALF]
+            mx_pass(bank, i, now_w[a][i], plane[:], w4_w[:, a, :].bitcast(FP4X4), w4_s[:, a, :], start, stop)
 
-        w1_codes = keep.tile([P, PASSES, H], U32, name="w1_codes", align_bytes=64)
-        w1_s = keep.tile([P, PASSES, H], U8, name="w1_s", align_bytes=64)
-        halves = [(a, c) for a in range(PASSES) for c in range(2)]
-        w1_bf = []
-        for n, (a, c) in enumerate(halves):
-            w1_bf.append(keep.tile([P, H // 2, 4], BF16, name="w1_bf", tag="stage_%d" % n, align_bytes=64))
-            nc.vector.tensor_copy(*woven(w1_bf[n][:], w1_raw[a][:, :, (H // 2) * c : (H // 2) * (c + 1)]))
-        for n, (a, c) in enumerate(halves):
-            cols = slice((H // 2) * c, (H // 2) * (c + 1))
-            quantize(w1_codes[:, a, cols], w1_s[:, a, cols], w1_bf[n][:].rearrange("p c j -> p (c j)"))
+        def a_pass(bank, i, a, stop):
+            mx_pass(
+                bank, i, past_w[a][i], past_s[i // HALF][4 * a :, :], w1_codes[:, a, :].bitcast(FP8X4), w1_s[:, a, :],
+                a == 0, stop,
+            )
 
-        past_w = gather_words(list_past, 0, ["stage_2", "stage_3"]) + gather_words(list_past, 1, ["stage_0", "stage_1"])
+        def product_bank(i):
+            return psum.tile([P, H], F32, name="bank", tag="product%d" % (i % 4))
 
-        def project(bank_tag, i, words, word_scales, weights, weight_scales):
-            bank = psum.tile([P, H], F32, name="bank", tag="product%d" % bank_tag)
-            for a in range(PASSES):
-                nc.tensor.matmul_mx(
-                    out=bank[:],
-                    lhsT=words[i][a].bitcast(FP8X4),
-                    lhsT_scale=word_scales[a][:, P * i : P * (i + 1)],
-                    rhs=weights[a],
-                    rhs_scale=weight_scales[a],
-                    start=(a == 0),
-                    stop=(a == PASSES - 1),
-                )
+        def dealt(bank):
             return bank[:].rearrange("j (g t i) -> j t g i", t=4, i=8)
 
-        def size_of_sum(i, terms, name):
-            bank = psum.tile([P, 4, P], F32, name="bank", tag="turned%d" % (i % 2))
+        def dealt_tile(name, i):
+            return sb([P, 4, 16, 8], F32, "%s_%d" % (name, i))
+
+        def turned_sum(tag, terms):
+            bank = psum.tile([P, 4, P], F32, name="bank", tag="turned%d" % tag)
             for t in range(4):
                 for n, term in enumerate(terms):
                     nc.tensor.matmul(
@@ -148,90 +162,124 @@ def tile_list_patch_motion_acceleration_kernel(
                         start=(n == 0),
                         stop=(n == len(terms) - 1),
                     )
-            size = keep.tile([P, P, 4], F32, name="%s_%d" % (name, i))
-            nc.scalar.activation(size[:], bank[:].rearrange("p t j -> p j t"), ACT.Abs)
-            return size
+            return bank[:].rearrange("p t j -> p j t")
 
-        def dealt_tile(name, i):
-            return keep.tile([P, 4, 16, 8], F32, name="%s_%d" % (name, i))
+        c_sb, minus_b = [], []
+        second = [sb([P, 2, P, 4], F32, "second_%d" % pair) for pair in range(HALF)]
 
-        minus_b, second = [], []
-        for pair in range(TILES // 2):
-            tiles = (2 * pair, 2 * pair + 1)
-            c_sb = {}
+        def second_sizes(tiles):
+            banks = [product_bank(i) for i in tiles]
+            order = [(n, a) for a in range(PASSES) for n in range(HALF)]
+            if tiles[0] > 0:
+                order = sorted(order)
+            for n, a in order:
+                c_pass(banks[n], tiles[n], a)
+                if a == PASSES - 1:
+                    c_sb.append(dealt_tile("c", tiles[n]))
+                    nc.scalar.copy(c_sb[tiles[n]][:], dealt(banks[n]))
             for i in tiles:
-                c = project(
-                    i % 2,
-                    i,
-                    future_w,
-                    [future_s[4 * a :, :] for a in range(PASSES)],
-                    [w8_w[:, a, :].bitcast(FP8X4) for a in range(PASSES)],
-                    [w8_s[4 * a :, :] for a in range(PASSES)],
-                )
-                c_sb[i] = dealt_tile("c", i)
-                nc.scalar.copy(c_sb[i][:], c)
-            for i in tiles:
-                b = project(
-                    2 + i % 2,
-                    i,
-                    now_w,
-                    [now_s[:], now_s1[:]],
-                    [w4_w[:, a, :].bitcast(FP4X4) for a in range(PASSES)],
-                    [w4_s[:, a, :] for a in range(PASSES)],
-                )
+                bank = product_bank(i)
+                for a in range(PASSES):
+                    b_pass(bank, i, a, a == 0, a == PASSES - 1)
                 minus_b.append(dealt_tile("minus_b", i))
-                nc.scalar.activation(minus_b[i][:], b, ACT.Copy, scale=-1.0)
+                nc.scalar.activation(minus_b[i][:], dealt(bank), ACT.Copy, scale=-1.0)
             for i in tiles:
-                second.append(size_of_sum(i, [minus_b[i], c_sb[i]], "second"))
+                nc.scalar.activation(second[i // 2][:, i % 2], turned_sum(i % 4, [minus_b[i], c_sb[i]]), ACT.Abs)
 
-        wd_codes = keep.tile([P, N], U32, name="wd_codes", align_bytes=64)
-        wd_s = keep.tile([P, N], U8, name="wd_s", align_bytes=64)
-        for c in range(2):
-            wd_bf = keep.tile([P, N // 2, 4], BF16, name="wd_bf", tag="wd_stage_%d" % c, align_bytes=64)
-            for piece in range(2):
-                start = (N // 2) * c + P * piece
-                nc.scalar.copy(*woven(wd_bf[:, P * piece : P * (piece + 1), :], wd_raw[:, :, start : start + P]))
-            cols = slice((N // 2) * c, (N // 2) * (c + 1))
-            quantize(wd_codes[:, cols], wd_s[:, cols], wd_bf[:].rearrange("p c t -> p (c t)"))
-        past_w.extend(gather_words(list_past, 2, ["wd_stage_0", "wd_stage_1"]))
+        second_sizes(range(HALF))
 
-        first = []
+        now_s.append(gather_scales(list_now, 1, "now_s_1", "future_w_1a"))
+        move_up(1)
+        future_s.append(gather_scales(list_future, 1, "future_s_1", "future_w_1b"))
+        future_w[0].extend(gather_words(list_future, 0, 512, S, "future_w_0b", "future_s_0"))
+        future_w[1].extend(gather_words(list_future, 1, 512, S, "future_w_1c"))
+        now_w[0].extend(gather_words(list_now, 0, 512, S, "now_w_0b", "now_w_0"))
+        now_w[1].extend(gather_words(list_now, 1, 512, S, "now_w_1b"))
+
+        second_sizes(range(HALF, TILES))
+
+        def quantize(codes, scales, values):
+            nc.vector.quantize_mx(out=codes.bitcast(FP8X4), scales=scales, in_=values)
+
+        def woven(grouped, raw):
+            return grouped.rearrange("p (c i) t -> p c t i", i=4), raw.rearrange("p t (c i) -> p c t i", i=4)
+
+        w1_codes = sb([P, PASSES, H], U32, "w1_codes")
+        w1_s = sb([P, PASSES, H], U8, "w1_s")
+        w1_bf = []
+        for a in range(PASSES):
+            w1_bf.append(sb([P, H, 4], BF16, "w1_bf_%d" % a, "c_%d" % (2 + a)))
+            nc.vector.tensor_scalar_mul(*woven(w1_bf[a][:], w1_raw[a][:]), -1.0)
+        for a in range(PASSES):
+            quantize(w1_codes[:, a, :], w1_s[:, a, :], w1_bf[a][:].rearrange("p c j -> p (c j)"))
+
+        past_s = [gather_scales(list_past, 0, "past_s_0")]
+        early = sb([P, PASSES, S // 2], U32, "past_w_early", "c_2")
+        for start in (0, 256):
+            for a in range(PASSES):
+                gather(tab_w[a], U32, list_past, start, start + 256, early[:, a, start : start + 256])
+        past_s.append(gather_scales(list_past, 1, "past_s_1", "c_4"))
+        late = sb([P, PASSES, S // 2], U32, "past_w_late", "c_3")
+        for a in range(PASSES):
+            gather(tab_w[a], U32, list_past, S // 2, S, late[:, a, :])
+        past_w = [
+            [[early, late][i // HALF][:, a, P * (i % HALF) : P * (i % HALF + 1)] for i in range(TILES)]
+            for a in range(PASSES)
+        ]
+
+        wd_codes = sb([P, N], U32, "wd_codes")
+        wd_s = sb([P, N], U8, "wd_s")
+        wd_bf = sb([P, N, 4], BF16, "wd_bf", "c_6")
+        nc.vector.tensor_copy(*woven(wd_bf[:], wd_raw[:]))
+        quantize(wd_codes[:], wd_s[:], wd_bf[:].rearrange("p c t -> p (c t)"))
+
+        terms = {}
+
+        def first_products(tiles):
+            for i in tiles:
+                bank = product_bank(i)
+                for a in range(PASSES):
+                    a_pass(bank, i, a, a == PASSES - 1 and i not in REPEATED)
+                a_sb = dealt_tile("a", i)
+                if i in REPEATED:
+                    for a in range(PASSES):
+                        b_pass(bank, i, a, False, a == PASSES - 1)
+                    nc.scalar.activation(a_sb[:], dealt(bank), ACT.Abs)
+                    terms[i] = [a_sb]
+                else:
+                    nc.scalar.activation(a_sb[:], dealt(bank), ACT.Copy, scale=-1.0)
+                    terms[i] = [a_sb, minus_b[i]]
+
+        first = {}
 
         def first_sizes(tiles):
-            terms = {}
-            for i in tiles:
-                a_sum = project(
-                    i % 4,
-                    i,
-                    past_w,
-                    [past_s[4 * a :, :] for a in range(PASSES)],
-                    [w1_codes[:, a, :].bitcast(FP8X4) for a in range(PASSES)],
-                    [w1_s[:, a, :] for a in range(PASSES)],
-                )
-                a_sb = dealt_tile("a", i)
-                if i < HALF:
-                    nc.scalar.copy(a_sb[:], a_sum)
-                    terms[i] = [a_sb, minus_b[i]]
+            size = None
+            for n, i in enumerate(tiles):
+                turned = turned_sum(i % 2, terms[i])
+                if i in REPEATED:
+                    first[i] = turned
                 else:
-                    nc.vector.tensor_tensor(a_sb[:], a_sum, minus_b[i][:], ALU.add)
-                    terms[i] = [a_sb]
-            for i in tiles:
-                first.append(size_of_sum(i, terms[i], "first"))
+                    if n == 0:
+                        size = sb([P, 2, P, 4], F32, "first_%d" % i)
+                    nc.scalar.activation(size[:, n], turned, ACT.Abs)
+                    first[tiles[0]] = size[:]
 
         out_rows = out.rearrange("(m p) j -> p m j", p=P)
 
-        def decode(tiles):
+        def decode(tiles, tags, copies):
             width = P * len(tiles)
             cols = slice(P * tiles[0], P * tiles[0] + width)
-            h = keep.tile([P, len(tiles), P, 4], BF16, name="h_%d" % tiles[0], align_bytes=64)
-            for n, i in enumerate(tiles):
-                nc.vector.tensor_tensor(h[:, n], first[i][:], second[i][:], ALU.subtract)
-            h_codes = keep.tile([P, width], U32, name="h_codes_%d" % tiles[0], align_bytes=64)
-            h_s = keep.tile([P, width], U8, name="h_s_%d" % tiles[0], align_bytes=64)
+            h = sb([P, len(tiles), P, 4], BF16, "h_%d" % tiles[0])
+            if len(tiles) == 2:
+                nc.vector.tensor_tensor(h[:], first[tiles[0]], second[tiles[0] // 2][:], ALU.subtract)
+            else:
+                nc.vector.tensor_tensor(h[:, 0], first[tiles[0]], second[tiles[0] // 2][:, tiles[0] % 2], ALU.subtract)
+            h_codes = sb([P, width], U32, "h_codes_%d" % tiles[0])
+            h_s = sb([P, width], U8, "h_s_%d" % tiles[0])
             quantize(h_codes[:], h_s[:], h[:].rearrange("p f j t -> p (f j t)"))
             per_bank = 4 // len(tiles)
             for g in range(len(tiles)):
-                o_bank = psum.tile([P, per_bank, width], F32, name="o_bank", tag="decoded%d" % ((tiles[0] + g) % 2))
+                o_bank = psum.tile([P, per_bank, width], F32, name="bank", tag=tags[g])
                 for m in range(per_bank):
                     rows = slice(P * (per_bank * g + m), P * (per_bank * g + m + 1))
                     nc.tensor.matmul_mx(
@@ -243,13 +291,21 @@ def tile_list_patch_motion_acceleration_kernel(
                         start=True,
                         stop=True,
                     )
-                o_sb = keep.tile([P, per_bank, width], F32, name="o_sb_%d_%d" % (tiles[0], g))
-                nc.scalar.copy(o_sb[:], o_bank[:])
+                o_sb = sb([P, per_bank, width], F32, "o_sb_%d_%d" % (tiles[0], g))
+                copies[g](o_sb[:], o_bank[:])
                 nc.sync.dma_start(out_rows[:, per_bank * g : per_bank * (g + 1), cols], o_sb[:])
 
-        for pair in range(TILES // 2):
-            first_sizes((2 * pair, 2 * pair + 1))
-            if pair > 0:
-                decode([2 * pair - 2, 2 * pair - 1])
-        decode([TILES - 2])
-        decode([TILES - 1])
+        first_products((0, 1, 2, 3))
+        first_sizes((0, 1))
+        first_sizes((2, 3))
+        first_products((4, 5))
+        ring = ("turned2", "turned3")
+        on_scalar = (nc.scalar.copy, nc.scalar.copy)
+        decode((0, 1), ring, on_scalar)
+        first_sizes((4, 5))
+        first_products((6, 7))
+        decode((2, 3), ring, on_scalar)
+        first_sizes((6, 7))
+        decode((4, 5), ("product0", "product1"), on_scalar)
+        decode((6,), ("product2",), (nc.scalar.copy,))
+        decode((7,), ("product3",), (nc.vector.tensor_copy,))

@@ -22,6 +22,7 @@ PASSES = K // 512
 TILES = S // P
 HALF = TILES // 2
 REPEATED = (6, 7)
+ON_VECTOR = (4, 5)
 
 
 def tile_list_patch_motion_acceleration_kernel(
@@ -164,7 +165,7 @@ def tile_list_patch_motion_acceleration_kernel(
                     )
             return bank[:].rearrange("p t j -> p j t")
 
-        c_sb, minus_b = [], []
+        c_sb, b_sb = [], []
         second = [sb([P, 2, P, 4], F32, "second_%d" % pair) for pair in range(HALF)]
 
         def second_sizes(tiles):
@@ -176,15 +177,15 @@ def tile_list_patch_motion_acceleration_kernel(
                 c_pass(banks[n], tiles[n], a)
                 if a == PASSES - 1:
                     c_sb.append(dealt_tile("c", tiles[n]))
-                    nc.scalar.copy(c_sb[tiles[n]][:], dealt(banks[n]))
+                    nc.scalar.activation(c_sb[tiles[n]][:], dealt(banks[n]), ACT.Copy, scale=-1.0)
             for i in tiles:
                 bank = product_bank(i)
                 for a in range(PASSES):
                     b_pass(bank, i, a, a == 0, a == PASSES - 1)
-                minus_b.append(dealt_tile("minus_b", i))
-                nc.scalar.activation(minus_b[i][:], dealt(bank), ACT.Copy, scale=-1.0)
+                b_sb.append(dealt_tile("b_sb", i))
+                nc.scalar.copy(b_sb[i][:], dealt(bank))
             for i in tiles:
-                nc.scalar.activation(second[i // 2][:, i % 2], turned_sum(i % 4, [minus_b[i], c_sb[i]]), ACT.Abs)
+                nc.scalar.activation(second[i // 2][:, i % 2], turned_sum(i % 4, [b_sb[i], c_sb[i]]), ACT.Abs)
 
         second_sizes(range(HALF))
 
@@ -246,9 +247,12 @@ def tile_list_patch_motion_acceleration_kernel(
                         b_pass(bank, i, a, False, a == PASSES - 1)
                     nc.scalar.activation(a_sb[:], dealt(bank), ACT.Abs)
                     terms[i] = [a_sb]
+                elif i in ON_VECTOR:
+                    nc.vector.tensor_tensor(a_sb[:], dealt(bank), b_sb[i][:], ALU.add)
+                    terms[i] = [a_sb]
                 else:
-                    nc.scalar.activation(a_sb[:], dealt(bank), ACT.Copy, scale=-1.0)
-                    terms[i] = [a_sb, minus_b[i]]
+                    nc.scalar.copy(a_sb[:], dealt(bank))
+                    terms[i] = [a_sb, b_sb[i]]
 
         first = {}
 

@@ -21,8 +21,7 @@ P = 128
 PASSES = K // 512
 TILES = S // P
 HALF = TILES // 2
-REPEATED = (6, 7)
-ON_VECTOR = (4, 5)
+ON_VECTOR = (6, 7)
 
 
 def tile_list_patch_motion_acceleration_kernel(
@@ -220,18 +219,14 @@ def tile_list_patch_motion_acceleration_kernel(
             for a in range(PASSES):
                 gather(tab_w[a], U32, list_past, start, start + 256, early[:, a, start : start + 256])
         past_s.append(gather_scales(list_past, 1, "past_s_1", "c_4"))
-        late = sb([P, PASSES, S // 2], U32, "past_w_late", "c_3")
-        for a in range(PASSES):
-            gather(tab_w[a], U32, list_past, S // 2, S, late[:, a, :])
-        past_w = [
-            [[early, late][i // HALF][:, a, P * (i % HALF) : P * (i % HALF + 1)] for i in range(TILES)]
-            for a in range(PASSES)
-        ]
+        past_w = [[early[:, a, P * i : P * (i + 1)] for i in range(HALF)] for a in range(PASSES)]
+        past_w[0].extend(gather_words(list_past, 0, S // 2, S, "past_w_late_0", "c_3"))
 
         wd_codes = sb([P, N], U32, "wd_codes")
         wd_s = sb([P, N], U8, "wd_s")
-        wd_bf = sb([P, N, 4], BF16, "wd_bf", "c_6")
+        wd_bf = sb([P, N, 4], BF16, "wd_bf", "c_5")
         nc.vector.tensor_copy(*woven(wd_bf[:], wd_raw[:]))
+        past_w[1].extend(gather_words(list_past, 1, S // 2, S, "past_w_late_1", "c_6"))
         quantize(wd_codes[:], wd_s[:], wd_bf[:].rearrange("p c t -> p (c t)"))
 
         terms = {}
@@ -240,14 +235,9 @@ def tile_list_patch_motion_acceleration_kernel(
             for i in tiles:
                 bank = product_bank(i)
                 for a in range(PASSES):
-                    a_pass(bank, i, a, a == PASSES - 1 and i not in REPEATED)
+                    a_pass(bank, i, a, a == PASSES - 1)
                 a_sb = dealt_tile("a", i)
-                if i in REPEATED:
-                    for a in range(PASSES):
-                        b_pass(bank, i, a, False, a == PASSES - 1)
-                    nc.scalar.activation(a_sb[:], dealt(bank), ACT.Abs)
-                    terms[i] = [a_sb]
-                elif i in ON_VECTOR:
+                if i in ON_VECTOR:
                     nc.vector.tensor_tensor(a_sb[:], dealt(bank), b_sb[i][:], ALU.add)
                     terms[i] = [a_sb]
                 else:
@@ -257,32 +247,26 @@ def tile_list_patch_motion_acceleration_kernel(
         first = {}
 
         def first_sizes(tiles):
-            size = None
-            for n, i in enumerate(tiles):
-                turned = turned_sum(i % 2, terms[i])
-                if i in REPEATED:
-                    first[i] = turned
-                else:
-                    if n == 0:
-                        size = sb([P, 2, P, 4], F32, "first_%d" % i)
-                    nc.scalar.activation(size[:, n], turned, ACT.Abs)
-                    first[tiles[0]] = size[:]
+            first[tiles[0] // 2] = sb([P, 2, P, 4], F32, "first_%d" % tiles[0])
+            for i in tiles:
+                nc.scalar.activation(first[i // 2][:, i % 2], turned_sum(i % 2, terms[i]), ACT.Abs)
 
         out_rows = out.rearrange("(m p) j -> p m j", p=P)
 
-        def decode(tiles, tags, copies):
+        def difference(tiles):
+            h = sb([P, len(tiles), P, 4], BF16, "h_%d" % tiles[0])
+            part = slice(tiles[0] % 2, tiles[-1] % 2 + 1)
+            nc.vector.tensor_tensor(h[:], first[tiles[0] // 2][:, part], second[tiles[0] // 2][:, part], ALU.subtract)
+            return h
+
+        def decode(tiles, h, tags, copies):
             width = P * len(tiles)
             cols = slice(P * tiles[0], P * tiles[0] + width)
-            h = sb([P, len(tiles), P, 4], BF16, "h_%d" % tiles[0])
-            if len(tiles) == 2:
-                nc.vector.tensor_tensor(h[:], first[tiles[0]], second[tiles[0] // 2][:], ALU.subtract)
-            else:
-                nc.vector.tensor_tensor(h[:, 0], first[tiles[0]], second[tiles[0] // 2][:, tiles[0] % 2], ALU.subtract)
             h_codes = sb([P, width], U32, "h_codes_%d" % tiles[0])
             h_s = sb([P, width], U8, "h_s_%d" % tiles[0])
             quantize(h_codes[:], h_s[:], h[:].rearrange("p f j t -> p (f j t)"))
-            per_bank = 4 // len(tiles)
-            for g in range(len(tiles)):
+            per_bank = 4 // len(tags)
+            for g in range(len(tags)):
                 o_bank = psum.tile([P, per_bank, width], F32, name="bank", tag=tags[g])
                 for m in range(per_bank):
                     rows = slice(P * (per_bank * g + m), P * (per_bank * g + m + 1))
@@ -302,14 +286,16 @@ def tile_list_patch_motion_acceleration_kernel(
         first_products((0, 1, 2, 3))
         first_sizes((0, 1))
         first_sizes((2, 3))
-        first_products((4, 5))
+        first_products((4, 5, 6, 7))
         ring = ("turned2", "turned3")
         on_scalar = (nc.scalar.copy, nc.scalar.copy)
-        decode((0, 1), ring, on_scalar)
+        decode((0, 1), difference((0, 1)), ring, on_scalar)
         first_sizes((4, 5))
-        first_products((6, 7))
-        decode((2, 3), ring, on_scalar)
+        decode((2, 3), difference((2, 3)), ring, on_scalar)
         first_sizes((6, 7))
-        decode((4, 5), ("product0", "product1"), on_scalar)
-        decode((6,), ("product2",), (nc.scalar.copy,))
-        decode((7,), ("product3",), (nc.vector.tensor_copy,))
+        h_45 = difference((4, 5))
+        h_6 = difference((6,))
+        decode((4, 5), h_45, ("product0", "product1"), on_scalar)
+        h_7 = difference((7,))
+        decode((6,), h_6, ("product2",), (nc.scalar.copy,))
+        decode((7,), h_7, ("product3", "turned2"), (nc.vector.tensor_copy, nc.scalar.copy))

@@ -22,6 +22,7 @@ PASSES = K // 512
 TILES = S // P
 HALF = TILES // 2
 ON_VECTOR = (6, 7)
+REPEATED = (0, 1)
 
 
 def tile_list_patch_motion_acceleration_kernel(
@@ -107,11 +108,12 @@ def tile_list_patch_motion_acceleration_kernel(
 
         future_s = [gather_scales(list_future, 0, "future_s_0")]
         future_w = [gather_words(list_future, 0, 0, 512, "future_w_0")]
-        now_w = [gather_words(list_now, 0, 0, 512, "now_w_0")]
-        future_w.append(
-            gather_words(list_future, 1, 0, 256, "future_w_1a") + gather_words(list_future, 1, 256, 512, "future_w_1b")
-        )
-        now_w.append(gather_words(list_now, 1, 0, 512, "now_w_1"))
+        now_w = [gather_words(list_now, 0, 0, 256, "now_w_0a")]
+        now_w[0].extend(gather_words(list_now, 0, 256, 512, "now_w_0b"))
+        future_w.append(gather_words(list_future, 1, 0, 256, "future_w_1a"))
+        future_w[1].extend(gather_words(list_future, 1, 256, 512, "future_w_1b"))
+        now_w.append(gather_words(list_now, 1, 0, 256, "now_w_1a"))
+        now_w[1].extend(gather_words(list_now, 1, 256, 512, "now_w_1b"))
 
         def mx_pass(bank, i, words, word_scales, weights, weight_scales, start, stop):
             cols = slice(P * (i % HALF), P * (i % HALF + 1))
@@ -135,14 +137,14 @@ def tile_list_patch_motion_acceleration_kernel(
             plane = [now_s, now_s1][a][i // HALF]
             mx_pass(bank, i, now_w[a][i], plane[:], w4_w[:, a, :].bitcast(FP4X4), w4_s[:, a, :], start, stop)
 
-        def a_pass(bank, i, a, stop):
+        def a_pass(bank, i, a, start):
             mx_pass(
                 bank, i, past_w[a][i], past_s[i // HALF][4 * a :, :], w1_codes[:, a, :].bitcast(FP8X4), w1_s[:, a, :],
-                a == 0, stop,
+                start, a == PASSES - 1,
             )
 
-        def product_bank(i):
-            return psum.tile([P, H], F32, name="bank", tag="product%d" % (i % 4))
+        def new_bank(tag):
+            return psum.tile([P, H], F32, name="bank", tag=tag)
 
         def dealt(bank):
             return bank[:].rearrange("j (g t i) -> j t g i", t=4, i=8)
@@ -151,7 +153,7 @@ def tile_list_patch_motion_acceleration_kernel(
             return sb([P, 4, 16, 8], F32, "%s_%d" % (name, i))
 
         def turned_sum(tag, terms):
-            bank = psum.tile([P, 4, P], F32, name="bank", tag="turned%d" % tag)
+            bank = psum.tile([P, 4, P], F32, name="bank", tag=tag)
             for t in range(4):
                 for n, term in enumerate(terms):
                     nc.tensor.matmul(
@@ -164,39 +166,67 @@ def tile_list_patch_motion_acceleration_kernel(
                     )
             return bank[:].rearrange("p t j -> p j t")
 
-        c_sb, b_sb = [], []
+        c_sb, b_sb = {}, {}
         second = [sb([P, 2, P, 4], F32, "second_%d" % pair) for pair in range(HALF)]
 
-        def second_sizes(tiles):
-            banks = [product_bank(i) for i in tiles]
-            order = [(n, a) for a in range(PASSES) for n in range(HALF)]
-            if tiles[0] > 0:
-                order = sorted(order)
-            for n, a in order:
-                c_pass(banks[n], tiles[n], a)
+        def c_products(order, tags):
+            banks = {}
+            for i, a in order:
+                if a == 0:
+                    banks[i] = new_bank(tags[i % len(tags)])
+                c_pass(banks[i], i, a)
                 if a == PASSES - 1:
-                    c_sb.append(dealt_tile("c", tiles[n]))
-                    nc.scalar.activation(c_sb[tiles[n]][:], dealt(banks[n]), ACT.Copy, scale=-1.0)
-            for i in tiles:
-                bank = product_bank(i)
+                    c_sb[i] = dealt_tile("c", i)
+                    nc.scalar.activation(c_sb[i][:], dealt(banks[i]), ACT.Copy, scale=-1.0)
+
+        def b_products(tiles, tags):
+            for i, tag in zip(tiles, tags):
+                bank = new_bank(tag)
                 for a in range(PASSES):
                     b_pass(bank, i, a, a == 0, a == PASSES - 1)
-                b_sb.append(dealt_tile("b_sb", i))
+                b_sb[i] = dealt_tile("b_sb", i)
                 nc.scalar.copy(b_sb[i][:], dealt(bank))
-            for i in tiles:
-                nc.scalar.activation(second[i // 2][:, i % 2], turned_sum(i % 4, [b_sb[i], c_sb[i]]), ACT.Abs)
 
-        second_sizes(range(HALF))
+        def second_sizes(tiles, tags):
+            for i, tag in zip(tiles, tags):
+                nc.scalar.activation(second[i // 2][:, i % 2], turned_sum(tag, [b_sb[i], c_sb[i]]), ACT.Abs)
+
+        def both_passes(tiles):
+            return [(i, a) for i in tiles for a in range(PASSES)]
+
+        low, high = ("product0", "product1"), ("product2", "product3")
+        turned, spare = ("turned0", "turned1"), ("spare0", "spare1")
+
+        c_products([(0, 0), (1, 0), (2, 0), (0, 1), (1, 1), (2, 1), (3, 0), (3, 1)], low + high)
+        b_products((0, 1), low)
+        b_products((2, 3), high)
 
         now_s.append(gather_scales(list_now, 1, "now_s_1", "future_w_1a"))
         move_up(1)
         future_s.append(gather_scales(list_future, 1, "future_s_1", "future_w_1b"))
-        future_w[0].extend(gather_words(list_future, 0, 512, S, "future_w_0b", "future_s_0"))
-        future_w[1].extend(gather_words(list_future, 1, 512, S, "future_w_1c"))
-        now_w[0].extend(gather_words(list_now, 0, 512, S, "now_w_0b", "now_w_0"))
-        now_w[1].extend(gather_words(list_now, 1, 512, S, "now_w_1b"))
+        future_w[0].extend(gather_words(list_future, 0, 512, 768, "future_w_0c", "future_s_0"))
+        future_w[1].extend(gather_words(list_future, 1, 512, 768, "future_w_1c", "future_w_0"))
+        now_w[0].extend(gather_words(list_now, 0, 512, 768, "now_w_0c", "now_w_0b"))
+        now_w[1].extend(gather_words(list_now, 1, 512, 768, "now_w_1c", "now_w_1b"))
 
-        second_sizes(range(HALF, TILES))
+        second_sizes((0, 1), turned)
+        future_w[0].extend(gather_words(list_future, 0, 768, S, "future_w_0d", "c_0"))
+        future_w[1].extend(gather_words(list_future, 1, 768, S, "future_w_1d", "b_sb_0"))
+        now_w[0].extend(gather_words(list_now, 0, 768, S, "now_w_0d", "c_1"))
+        now_w[1].extend(gather_words(list_now, 1, 768, S, "now_w_1d", "b_sb_1"))
+        c_products(both_passes((4, 5)), low)
+        b_products((4, 5), high)
+        second_sizes((2, 3), spare)
+        c_products(both_passes((6, 7)), low)
+        b_products((6, 7), high)
+        second_sizes((4, 5), turned)
+
+        joint = {}
+        for i, tag in zip(REPEATED, spare):
+            joint[i] = new_bank(tag)
+            for a in range(PASSES):
+                b_pass(joint[i], i, a, a == 0, False)
+        second_sizes((6, 7), turned)
 
         def quantize(codes, scales, values):
             nc.vector.quantize_mx(out=codes.bitcast(FP8X4), scales=scales, in_=values)
@@ -213,43 +243,46 @@ def tile_list_patch_motion_acceleration_kernel(
         for a in range(PASSES):
             quantize(w1_codes[:, a, :], w1_s[:, a, :], w1_bf[a][:].rearrange("p c j -> p (c j)"))
 
-        past_s = [gather_scales(list_past, 0, "past_s_0")]
-        early = sb([P, PASSES, S // 2], U32, "past_w_early", "c_2")
+        past_s = [gather_scales(list_past, 0, "past_s_0", "c_2")]
+        early = sb([P, PASSES, S // 2], U32, "past_w_early", "c_3")
         for start in (0, 256):
             for a in range(PASSES):
                 gather(tab_w[a], U32, list_past, start, start + 256, early[:, a, start : start + 256])
-        past_s.append(gather_scales(list_past, 1, "past_s_1", "c_4"))
         past_w = [[early[:, a, P * i : P * (i + 1)] for i in range(HALF)] for a in range(PASSES)]
-        past_w[0].extend(gather_words(list_past, 0, S // 2, S, "past_w_late_0", "c_3"))
+        past_s.append(gather_scales(list_past, 1, "past_s_1", "c_4"))
+        for a in range(PASSES):
+            past_w[a].extend(gather_words(list_past, a, 512, 768, "past_w_c%d" % a, ("c_5", "c_6")[a]))
 
         wd_codes = sb([P, N], U32, "wd_codes")
         wd_s = sb([P, N], U8, "wd_s")
-        wd_bf = sb([P, N, 4], BF16, "wd_bf", "c_5")
-        nc.vector.tensor_copy(*woven(wd_bf[:], wd_raw[:]))
-        past_w[1].extend(gather_words(list_past, 1, S // 2, S, "past_w_late_1", "c_6"))
-        quantize(wd_codes[:], wd_s[:], wd_bf[:].rearrange("p c t -> p (c t)"))
+        wd_bf = sb([P, N, 4], BF16, "wd_bf")
+        for part in range(4):
+            cols = slice(P * part, P * (part + 1))
+            nc.scalar.copy(wd_bf[:, cols, :], wd_raw[:, :, cols].rearrange("p t c -> p c t"))
 
         terms = {}
 
-        def first_products(tiles):
-            for i in tiles:
-                bank = product_bank(i)
+        def first_products(tiles, tags):
+            for i, tag in zip(tiles, tags):
+                bank = joint[i] if i in REPEATED else new_bank(tag)
                 for a in range(PASSES):
-                    a_pass(bank, i, a, a == PASSES - 1)
+                    a_pass(bank, i, a, a == 0 and i not in REPEATED)
                 a_sb = dealt_tile("a", i)
-                if i in ON_VECTOR:
+                terms[i] = [a_sb]
+                if i in REPEATED:
+                    nc.scalar.activation(a_sb[:], dealt(bank), ACT.Abs)
+                elif i in ON_VECTOR:
                     nc.vector.tensor_tensor(a_sb[:], dealt(bank), b_sb[i][:], ALU.add)
-                    terms[i] = [a_sb]
                 else:
                     nc.scalar.copy(a_sb[:], dealt(bank))
-                    terms[i] = [a_sb, b_sb[i]]
+                    terms[i].append(b_sb[i])
 
         first = {}
 
-        def first_sizes(tiles):
+        def first_sizes(tiles, tags):
             first[tiles[0] // 2] = sb([P, 2, P, 4], F32, "first_%d" % tiles[0])
-            for i in tiles:
-                nc.scalar.activation(first[i // 2][:, i % 2], turned_sum(i % 2, terms[i]), ACT.Abs)
+            for i, tag in zip(tiles, tags):
+                nc.scalar.activation(first[i // 2][:, i % 2], turned_sum(tag, terms[i]), ACT.Abs)
 
         out_rows = out.rearrange("(m p) j -> p m j", p=P)
 
@@ -283,19 +316,27 @@ def tile_list_patch_motion_acceleration_kernel(
                 copies[g](o_sb[:], o_bank[:])
                 nc.sync.dma_start(out_rows[:, per_bank * g : per_bank * (g + 1), cols], o_sb[:])
 
-        first_products((0, 1, 2, 3))
-        first_sizes((0, 1))
-        first_sizes((2, 3))
-        first_products((4, 5, 6, 7))
-        ring = ("turned2", "turned3")
         on_scalar = (nc.scalar.copy, nc.scalar.copy)
-        decode((0, 1), difference((0, 1)), ring, on_scalar)
-        first_sizes((4, 5))
-        decode((2, 3), difference((2, 3)), ring, on_scalar)
-        first_sizes((6, 7))
+        first_products((0, 1), spare)
+        first_products((2, 3), low)
+        h_01 = sb([P, 2, P, 4], BF16, "h_0")
+        sizes = [turned_sum(tag, terms[i]) for i, tag in zip(REPEATED, spare)]
+        quantize(wd_codes[:], wd_s[:], wd_bf[:].rearrange("p c t -> p (c t)"))
+        for i in REPEATED:
+            nc.vector.tensor_tensor(h_01[:, i], sizes[i], second[0][:, i], ALU.subtract)
+        for a in range(PASSES):
+            past_w[a].extend(gather_words(list_past, a, 768, S, "past_w_d%d" % a, ("c_7", "a_0")[a]))
+        first_products((4, 5), high)
+        first_sizes((2, 3), turned)
+        decode((0, 1), h_01, spare, on_scalar)
+        h_23 = difference((2, 3))
+        first_products((6, 7), low)
+        first_sizes((4, 5), turned)
+        decode((2, 3), h_23, spare, on_scalar)
+        first_sizes((6, 7), turned)
         h_45 = difference((4, 5))
         h_6 = difference((6,))
-        decode((4, 5), h_45, ("product0", "product1"), on_scalar)
+        decode((4, 5), h_45, high, on_scalar)
         h_7 = difference((7,))
-        decode((6,), h_6, ("product2",), (nc.scalar.copy,))
-        decode((7,), h_7, ("product3", "turned2"), (nc.vector.tensor_copy, nc.scalar.copy))
+        decode((6,), h_6, ("product0",), (nc.scalar.copy,))
+        decode((7,), h_7, ("product1", "spare0"), (nc.vector.tensor_copy, nc.scalar.copy))

@@ -50,7 +50,7 @@ def tile_list_patch_motion_acceleration_kernel(
         w1_raw = [sb([P, 4, H], F32, "w1_raw_%d" % a) for a in range(PASSES)]
         wd_raw = sb([P, 4, N], F32, "wd_raw")
 
-        nc.vector.memset(tab_s[:].bitcast(I32), 0)
+        nc.gpsimd.memset(tab_s[:].bitcast(I32), 0)
         make_identity(nc, ident[:])
         nc.vector.memset(w8_s[:].bitcast(I32), 0)
         nc.vector.memset(w4_s[:].bitcast(I32), 0)
@@ -108,12 +108,11 @@ def tile_list_patch_motion_acceleration_kernel(
 
         future_s = [gather_scales(list_future, 0, "future_s_0")]
         future_w = [gather_words(list_future, 0, 0, 512, "future_w_0")]
-        now_w = [gather_words(list_now, 0, 0, 256, "now_w_0a")]
-        now_w[0].extend(gather_words(list_now, 0, 256, 512, "now_w_0b"))
+        now_w = [gather_words(list_now, 0, 0, 512, "now_w_0")]
+        ahead = gather_words(list_future, 0, 512, 768, "future_w_0c")
         future_w.append(gather_words(list_future, 1, 0, 256, "future_w_1a"))
         future_w[1].extend(gather_words(list_future, 1, 256, 512, "future_w_1b"))
-        now_w.append(gather_words(list_now, 1, 0, 256, "now_w_1a"))
-        now_w[1].extend(gather_words(list_now, 1, 256, 512, "now_w_1b"))
+        now_w.append(gather_words(list_now, 1, 0, 512, "now_w_1"))
 
         def mx_pass(bank, i, words, word_scales, weights, weight_scales, start, stop):
             cols = slice(P * (i % HALF), P * (i % HALF + 1))
@@ -197,36 +196,30 @@ def tile_list_patch_motion_acceleration_kernel(
         low, high = ("product0", "product1"), ("product2", "product3")
         turned, spare = ("turned0", "turned1"), ("spare0", "spare1")
 
-        c_products([(0, 0), (1, 0), (2, 0), (0, 1), (1, 1), (2, 1), (3, 0), (3, 1)], low + high)
+        c_products([(i, a) for a in range(PASSES) for i in range(HALF)], low + high)
         b_products((0, 1), low)
         b_products((2, 3), high)
+        second_sizes((0, 1), turned)
+        second_sizes((2, 3), spare)
 
         now_s.append(gather_scales(list_now, 1, "now_s_1", "future_w_1a"))
         move_up(1)
         future_s.append(gather_scales(list_future, 1, "future_s_1", "future_w_1b"))
-        future_w[0].extend(gather_words(list_future, 0, 512, 768, "future_w_0c", "future_s_0"))
-        future_w[1].extend(gather_words(list_future, 1, 512, 768, "future_w_1c", "future_w_0"))
-        now_w[0].extend(gather_words(list_now, 0, 512, 768, "now_w_0c", "now_w_0b"))
-        now_w[1].extend(gather_words(list_now, 1, 512, 768, "now_w_1c", "now_w_1b"))
+        future_w[0].extend(ahead + gather_words(list_future, 0, 768, S, "future_w_0b", "future_s_0"))
+        future_w[1].extend(gather_words(list_future, 1, 512, S, "future_w_1c"))
+        now_w[0].extend(gather_words(list_now, 0, 512, S, "now_w_0b", "c_0"))
+        now_w[1].extend(gather_words(list_now, 1, 512, S, "now_w_1b"))
 
-        second_sizes((0, 1), turned)
-        future_w[0].extend(gather_words(list_future, 0, 768, S, "future_w_0d", "c_0"))
-        future_w[1].extend(gather_words(list_future, 1, 768, S, "future_w_1d", "b_sb_0"))
-        now_w[0].extend(gather_words(list_now, 0, 768, S, "now_w_0d", "c_1"))
-        now_w[1].extend(gather_words(list_now, 1, 768, S, "now_w_1d", "b_sb_1"))
-        c_products(both_passes((4, 5)), low)
-        b_products((4, 5), high)
-        second_sizes((2, 3), spare)
-        c_products(both_passes((6, 7)), low)
+        c_products(both_passes((4, 5, 6, 7)), low + high)
+        b_products((4, 5), low)
         b_products((6, 7), high)
         second_sizes((4, 5), turned)
-
         joint = {}
         for i, tag in zip(REPEATED, spare):
             joint[i] = new_bank(tag)
             for a in range(PASSES):
                 b_pass(joint[i], i, a, a == 0, False)
-        second_sizes((6, 7), turned)
+        second_sizes((6, 7), low)
 
         def quantize(codes, scales, values):
             nc.vector.quantize_mx(out=codes.bitcast(FP8X4), scales=scales, in_=values)
@@ -250,15 +243,11 @@ def tile_list_patch_motion_acceleration_kernel(
                 gather(tab_w[a], U32, list_past, start, start + 256, early[:, a, start : start + 256])
         past_w = [[early[:, a, P * i : P * (i + 1)] for i in range(HALF)] for a in range(PASSES)]
         past_s.append(gather_scales(list_past, 1, "past_s_1", "c_4"))
-        for a in range(PASSES):
-            past_w[a].extend(gather_words(list_past, a, 512, 768, "past_w_c%d" % a, ("c_5", "c_6")[a]))
-
-        wd_codes = sb([P, N], U32, "wd_codes")
+        past_w[0].extend(gather_words(list_past, 0, S // 2, S, "past_w_late_0", "c_5"))
         wd_s = sb([P, N], U8, "wd_s")
-        wd_bf = sb([P, N, 4], BF16, "wd_bf")
-        for part in range(4):
-            cols = slice(P * part, P * (part + 1))
-            nc.scalar.copy(wd_bf[:, cols, :], wd_raw[:, :, cols].rearrange("p t c -> p c t"))
+        wd_bf = sb([P, N, 4], BF16, "wd_bf", "c_6")
+        nc.vector.tensor_copy(*woven(wd_bf[:], wd_raw[:]))
+        past_w[1].extend(gather_words(list_past, 1, S // 2, S, "past_w_late_1", "c_7"))
 
         terms = {}
 
@@ -318,25 +307,23 @@ def tile_list_patch_motion_acceleration_kernel(
 
         on_scalar = (nc.scalar.copy, nc.scalar.copy)
         first_products((0, 1), spare)
-        first_products((2, 3), low)
+        first_products((2, 3), high)
         h_01 = sb([P, 2, P, 4], BF16, "h_0")
         sizes = [turned_sum(tag, terms[i]) for i, tag in zip(REPEATED, spare)]
-        quantize(wd_codes[:], wd_s[:], wd_bf[:].rearrange("p c t -> p (c t)"))
         for i in REPEATED:
             nc.vector.tensor_tensor(h_01[:, i], sizes[i], second[0][:, i], ALU.subtract)
-        for a in range(PASSES):
-            past_w[a].extend(gather_words(list_past, a, 768, S, "past_w_d%d" % a, ("c_7", "a_0")[a]))
-        first_products((4, 5), high)
+        wd_codes = sb([P, N], U32, "wd_codes", "second_0")
+        quantize(wd_codes[:], wd_s[:], wd_bf[:].rearrange("p c t -> p (c t)"))
         first_sizes((2, 3), turned)
+        first_products((4, 5), low)
+        first_products((6, 7), high)
         decode((0, 1), h_01, spare, on_scalar)
-        h_23 = difference((2, 3))
-        first_products((6, 7), low)
         first_sizes((4, 5), turned)
-        decode((2, 3), h_23, spare, on_scalar)
+        decode((2, 3), difference((2, 3)), spare, on_scalar)
         first_sizes((6, 7), turned)
         h_45 = difference((4, 5))
         h_6 = difference((6,))
-        decode((4, 5), h_45, high, on_scalar)
+        decode((4, 5), h_45, low, on_scalar)
         h_7 = difference((7,))
-        decode((6,), h_6, ("product0",), (nc.scalar.copy,))
-        decode((7,), h_7, ("product1", "spare0"), (nc.vector.tensor_copy, nc.scalar.copy))
+        decode((6,), h_6, ("product2",), (nc.scalar.copy,))
+        decode((7,), h_7, ("product3", "spare0"), (nc.vector.tensor_copy, nc.scalar.copy))

@@ -200,7 +200,6 @@ def tile_list_patch_motion_acceleration_kernel(
         b_products((0, 1), low)
         b_products((2, 3), high)
         second_sizes((0, 1), turned)
-        second_sizes((2, 3), spare)
 
         now_s.append(gather_scales(list_now, 1, "now_s_1", "future_w_1a"))
         move_up(1)
@@ -208,9 +207,11 @@ def tile_list_patch_motion_acceleration_kernel(
         future_w[0].extend(ahead + gather_words(list_future, 0, 768, S, "future_w_0b", "future_s_0"))
         future_w[1].extend(gather_words(list_future, 1, 512, S, "future_w_1c"))
         now_w[0].extend(gather_words(list_now, 0, 512, S, "now_w_0b", "c_0"))
-        now_w[1].extend(gather_words(list_now, 1, 512, S, "now_w_1b"))
+        now_w[1].extend(gather_words(list_now, 1, 512, S, "now_w_1b", "c_1"))
 
-        c_products(both_passes((4, 5, 6, 7)), low + high)
+        c_products(both_passes((4, 5)), low)
+        second_sizes((2, 3), spare)
+        c_products(both_passes((6, 7)), high)
         b_products((4, 5), low)
         b_products((6, 7), high)
         second_sizes((4, 5), turned)
@@ -243,11 +244,11 @@ def tile_list_patch_motion_acceleration_kernel(
                 gather(tab_w[a], U32, list_past, start, start + 256, early[:, a, start : start + 256])
         past_w = [[early[:, a, P * i : P * (i + 1)] for i in range(HALF)] for a in range(PASSES)]
         past_s.append(gather_scales(list_past, 1, "past_s_1", "c_4"))
-        past_w[0].extend(gather_words(list_past, 0, S // 2, S, "past_w_late_0", "c_5"))
+        for a in range(PASSES):
+            past_w[a].extend(gather_words(list_past, a, 512, 768, "past_w_c%d" % a, "c_%d" % (5 + a)))
         wd_s = sb([P, N], U8, "wd_s")
-        wd_bf = sb([P, N, 4], BF16, "wd_bf", "c_6")
+        wd_bf = sb([P, N, 4], BF16, "wd_bf", "c_7")
         nc.vector.tensor_copy(*woven(wd_bf[:], wd_raw[:]))
-        past_w[1].extend(gather_words(list_past, 1, S // 2, S, "past_w_late_1", "c_7"))
 
         terms = {}
 
@@ -310,12 +311,14 @@ def tile_list_patch_motion_acceleration_kernel(
         first_products((2, 3), high)
         h_01 = sb([P, 2, P, 4], BF16, "h_0")
         sizes = [turned_sum(tag, terms[i]) for i, tag in zip(REPEATED, spare)]
+        for a in range(PASSES):
+            past_w[a].extend(gather_words(list_past, a, 768, S, "past_w_d%d" % a, "a_%d" % a))
         for i in REPEATED:
             nc.vector.tensor_tensor(h_01[:, i], sizes[i], second[0][:, i], ALU.subtract)
         wd_codes = sb([P, N], U32, "wd_codes", "second_0")
         quantize(wd_codes[:], wd_s[:], wd_bf[:].rearrange("p c t -> p (c t)"))
-        first_sizes((2, 3), turned)
         first_products((4, 5), low)
+        first_sizes((2, 3), turned)
         first_products((6, 7), high)
         decode((0, 1), h_01, spare, on_scalar)
         first_sizes((4, 5), turned)

@@ -19,10 +19,9 @@ ALU = mybir.AluOpType
 
 P = 128
 PASSES = K // 512
-TILES = S // P
-HALF = TILES // 2
-ON_VECTOR = (6, 7)
-REPEATED = (0, 1)
+PAIR = 2 * P
+HALF = S // 2
+LAST = 3
 
 
 def tile_list_patch_motion_acceleration_kernel(
@@ -36,62 +35,65 @@ def tile_list_patch_motion_acceleration_kernel(
         def sb(shape, dtype, name, tag=None):
             return keep.tile(shape, dtype, name=name, tag=tag or name, align_bytes=64)
 
-        list_past = keep.tile([P, S // 16], U16, name="list_past")
-        list_now = keep.tile([P, S // 16], U16, name="list_now")
-        list_future = keep.tile([P, S // 16], U16, name="list_future")
+        lists = {
+            "past": keep.tile([P, S // 16], U16, name="list_past"),
+            "now": keep.tile([P, S // 16], U16, name="list_now"),
+            "future": keep.tile([P, S // 16], U16, name="list_future"),
+        }
         tab_w = [sb([P, T], I32, "tab_w_%d" % a) for a in range(PASSES)]
         tab_s = sb([P, T], U8, "tab_s")
-        now_s1 = [sb([P, S // 2], U8, "now_s1_%d" % u) for u in range(2)]
+        moved = [sb([P, HALF], U8, "moved_%d" % u) for u in range(2)]
         w4_w = sb([P, PASSES, 2 * H], U8, "w4_w")
-        w8_w = [sb([P, H], I32, "w8_w_%d" % a) for a in range(PASSES)]
         w4_s = sb([P, PASSES, H], U8, "w4_s")
+        w8_w = [sb([P, H], I32, "w8_w_%d" % a) for a in range(PASSES)]
         w8_s = sb([P, H], U8, "w8_s")
-        ident = sb([P, P], F32, "ident")
         w1_raw = [sb([P, 4, H], F32, "w1_raw_%d" % a) for a in range(PASSES)]
         wd_raw = sb([P, 4, N], F32, "wd_raw")
+        ident = sb([P, P], F32, "ident")
 
         nc.gpsimd.memset(tab_s[:].bitcast(I32), 0)
         make_identity(nc, ident[:])
         nc.vector.memset(w8_s[:].bitcast(I32), 0)
         nc.vector.memset(w4_s[:].bitcast(I32), 0)
         for u in range(2):
-            nc.vector.memset(now_s1[u][96:P, :].bitcast(I32), 0)
+            nc.vector.memset(moved[u][96:P, :].bitcast(I32), 0)
 
         tab_rows = tab_words.rearrange("a p t i -> a p (t i)").bitcast(I32)
         w8_rows = w8_words.rearrange("a p e i -> a p (e i)").bitcast(I32)
-        nc.sync.dma_start(list_now[:], offs2)
-        for q in range(4):
-            nc.sync.dma_start(
-                tab_s[32 * q : 32 * q + 4 * PASSES, :].bitcast(I32), tab_scales[:, 4 * q : 4 * q + 4, :].bitcast(I32)
-            )
-        nc.sync.dma_start(list_future[:], offs3)
-        nc.sync.dma_start(tab_w[0][:], tab_rows[0])
+
+        def load_packed_scales(plane, scales):
+            for q in range(4):
+                nc.sync.dma_start(
+                    plane[32 * q : 32 * q + 4 * PASSES, :].bitcast(I32), scales[:, 4 * q : 4 * q + 4, :].bitcast(I32)
+                )
+
+        nc.sync.dma_start(lists["future"][:], offs3)
+        nc.sync.dma_start(lists["now"][:], offs2)
         nc.sync.dma_start(w8_w[0][:], w8_rows[0])
-        for q in range(4):
-            nc.sync.dma_start(
-                w8_s[32 * q : 32 * q + 4 * PASSES, :].bitcast(I32), w8_scales[:, 4 * q : 4 * q + 4, :].bitcast(I32)
-            )
+        load_packed_scales(tab_s, tab_scales)
+        nc.sync.dma_start(tab_w[0][:], tab_rows[0])
+        load_packed_scales(w8_s, w8_scales)
         nc.sync.dma_start(tab_w[1][:], tab_rows[1])
         nc.sync.dma_start(w8_w[1][:], w8_rows[1])
 
-        def gather(window, dtype, lst, start, end, picked):
-            nc.vector.tensor_copy(picked, window[:].bitcast(dtype).indirect(lst[:, start // 16 : end // 16]))
+        planes, words = {}, {}
 
-        def gather_scales(lst, u, name, tag=None):
-            picked = sb([P, S // 2], U8, name, tag)
-            gather(tab_s, U8, lst, (S // 2) * u, (S // 2) * (u + 1), picked[:])
-            return picked
+        def gather_scales(which, u, tag=None):
+            planes[which, u] = sb([P, HALF], U8, "%s_s_%d" % (which, u), tag)
+            offsets = lists[which][:, HALF * u // 16 : HALF * (u + 1) // 16]
+            nc.vector.tensor_copy(planes[which, u][:], tab_s[:].indirect(offsets))
 
-        def gather_words(lst, a, start, end, name, tag=None):
-            picked = sb([P, end - start], U32, name, tag)
-            gather(tab_w[a], U32, lst, start, end, picked[:])
-            return [picked[:, j : j + P] for j in range(0, end - start, P)]
+        def gather_words(which, a, pair, tag=None):
+            words[which, a, pair] = sb([P, PAIR], U32, "%s_w_%d_%d" % (which, a, pair), tag)
+            offsets = lists[which][:, PAIR * pair // 16 : PAIR * (pair + 1) // 16]
+            nc.vector.tensor_copy(words[which, a, pair][:], tab_w[a][:].bitcast(U32).indirect(offsets))
 
-        def move_up(u):
-            nc.sync.dma_start(now_s1[u][0:100, :].bitcast(I32), now_s[u][4:104, :].bitcast(I32))
+        def move_plane(u):
+            nc.sync.dma_start(moved[u][0:100, :].bitcast(I32), planes["now", u][4:104, :].bitcast(I32))
 
-        now_s = [gather_scales(list_now, 0, "now_s_0")]
-        move_up(0)
+        gather_scales("future", 0)
+        gather_scales("now", 0)
+        move_plane(0)
         nc.sync.dma_start(w4_w[:].bitcast(I32), w4_words.rearrange("a p e -> p a e").bitcast(I32))
         for q in range(4):
             nc.sync.dma_start(
@@ -101,58 +103,47 @@ def tile_list_patch_motion_acceleration_kernel(
         w1_rows = w1.rearrange("(a p j) c -> a p j c", p=P, j=4)
         for a in range(PASSES):
             nc.sync.dma_start(w1_raw[a][:], w1_rows[a])
-        nc.sync.dma_start(list_past[:], offs)
+        nc.sync.dma_start(lists["past"][:], offs)
         wd_rows = wd.rearrange("(g t i) n -> t g i n", t=4, i=8)
         for t in range(4):
             nc.sync.dma_start(wd_raw[:, t, :], wd_rows[t])
 
-        future_s = [gather_scales(list_future, 0, "future_s_0")]
-        future_w = [gather_words(list_future, 0, 0, 512, "future_w_0")]
-        now_w = [gather_words(list_now, 0, 0, 512, "now_w_0")]
-        ahead = gather_words(list_future, 0, 512, 768, "future_w_0c")
-        future_w.append(gather_words(list_future, 1, 0, 256, "future_w_1a"))
-        future_w[1].extend(gather_words(list_future, 1, 256, 512, "future_w_1b"))
-        now_w.append(gather_words(list_now, 1, 0, 512, "now_w_1"))
-
-        def mx_pass(bank, i, words, word_scales, weights, weight_scales, start, stop):
-            cols = slice(P * (i % HALF), P * (i % HALF + 1))
+        def mx_pass(bank, which, i, a, start, stop):
+            cols = slice(P * (i % 4), P * (i % 4 + 1))
+            plane = planes[which, i // 4][4 * a :, cols]
+            if which == "future":
+                weights, weight_scales = w8_w[a][:].bitcast(FP8X4), w8_s[4 * a :, :]
+            elif which == "past":
+                weights, weight_scales = w1_codes[:, a, :].bitcast(FP8X4), w1_s[:, a, :]
+            else:
+                weights, weight_scales = w4_w[:, a, :].bitcast(FP4X4), w4_s[:, a, :]
+                plane = [planes["now", i // 4], moved[i // 4]][a][:, cols]
             nc.tensor.matmul_mx(
                 out=bank[:],
-                lhsT=words.bitcast(FP8X4),
-                lhsT_scale=word_scales[:, cols],
+                lhsT=words[which, a, i // 2][:, P * (i % 2) : P * (i % 2 + 1)].bitcast(FP8X4),
+                lhsT_scale=plane,
                 rhs=weights,
                 rhs_scale=weight_scales,
                 start=start,
                 stop=stop,
             )
 
-        def c_pass(bank, i, a):
-            mx_pass(
-                bank, i, future_w[a][i], future_s[i // HALF][4 * a :, :], w8_w[a][:].bitcast(FP8X4), w8_s[4 * a :, :],
-                a == 0, a == PASSES - 1,
-            )
+        def tiles_of(pair):
+            return (2 * pair, 2 * pair + 1)
 
-        def b_pass(bank, i, a, start, stop):
-            plane = [now_s, now_s1][a][i // HALF]
-            mx_pass(bank, i, now_w[a][i], plane[:], w4_w[:, a, :].bitcast(FP4X4), w4_s[:, a, :], start, stop)
-
-        def a_pass(bank, i, a, start):
-            mx_pass(
-                bank, i, past_w[a][i], past_s[i // HALF][4 * a :, :], w1_codes[:, a, :].bitcast(FP8X4), w1_s[:, a, :],
-                start, a == PASSES - 1,
-            )
-
-        def new_bank(tag):
-            return psum.tile([P, H], F32, name="bank", tag=tag)
+        def new_banks(pair, letter):
+            return {i: psum.tile([P, H], F32, name="bank", tag="%s%d" % (letter, i % 2)) for i in tiles_of(pair)}
 
         def dealt(bank):
             return bank[:].rearrange("j (g t i) -> j t g i", t=4, i=8)
 
-        def dealt_tile(name, i):
-            return sb([P, 4, 16, 8], F32, "%s_%d" % (name, i))
+        def leave(name, i, bank, func, scale):
+            copy = sb([P, 4, 16, 8], F32, "%s_%d" % (name, i))
+            nc.scalar.activation(copy[:], dealt(bank), func, scale=scale)
+            return copy
 
-        def turned_sum(tag, terms):
-            bank = psum.tile([P, 4, P], F32, name="bank", tag=tag)
+        def turned_sum(i, letter, terms):
+            bank = psum.tile([P, 4, P], F32, name="bank", tag="%s%d" % (letter, i % 2))
             for t in range(4):
                 for n, term in enumerate(terms):
                     nc.tensor.matmul(
@@ -165,62 +156,72 @@ def tile_list_patch_motion_acceleration_kernel(
                     )
             return bank[:].rearrange("p t j -> p j t")
 
-        c_sb, b_sb = {}, {}
-        second = [sb([P, 2, P, 4], F32, "second_%d" % pair) for pair in range(HALF)]
+        held = {"past": {}, "now": {}, "future": {}}
 
-        def c_products(order, tags):
-            banks = {}
-            for i, a in order:
-                if a == 0:
-                    banks[i] = new_bank(tags[i % len(tags)])
-                c_pass(banks[i], i, a)
-                if a == PASSES - 1:
-                    c_sb[i] = dealt_tile("c", i)
-                    nc.scalar.activation(c_sb[i][:], dealt(banks[i]), ACT.Copy, scale=-1.0)
-
-        def b_products(tiles, tags):
-            for i, tag in zip(tiles, tags):
-                bank = new_bank(tag)
+        def products(which, pair, letter):
+            banks = new_banks(pair, letter)
+            for i in tiles_of(pair):
                 for a in range(PASSES):
-                    b_pass(bank, i, a, a == 0, a == PASSES - 1)
-                b_sb[i] = dealt_tile("b_sb", i)
-                nc.scalar.copy(b_sb[i][:], dealt(bank))
+                    mx_pass(banks[i], which, i, a, a == 0, a == PASSES - 1)
+                held[which][i] = leave(which, i, banks[i], ACT.Copy, -1.0 if which == "future" else 1.0)
 
-        def second_sizes(tiles, tags):
-            for i, tag in zip(tiles, tags):
-                nc.scalar.activation(second[i // 2][:, i % 2], turned_sum(tag, [b_sb[i], c_sb[i]]), ACT.Abs)
+        def sizes(other, pair, letter):
+            size = sb([P, 2, P, 4], F32, "size_%s_%d" % (other, pair))
+            for i in tiles_of(pair):
+                nc.scalar.activation(size[:, i % 2], turned_sum(i, letter, [held["now"][i], held[other][i]]), ACT.Abs)
+            return size
 
-        def both_passes(tiles):
-            return [(i, a) for i in tiles for a in range(PASSES)]
+        second, first = {}, {}
 
-        low, high = ("product0", "product1"), ("product2", "product3")
-        turned, spare = ("turned0", "turned1"), ("spare0", "spare1")
+        gather_words("future", 0, 0)
+        gather_words("future", 0, 1)
+        gather_words("now", 0, 0)
+        gather_words("future", 1, 0)
+        gather_words("now", 1, 0)
+        gather_words("future", 1, 1)
+        gather_words("now", 0, 1, "future_w_1_0")
+        gather_words("now", 1, 1)
 
-        c_products([(i, a) for a in range(PASSES) for i in range(HALF)], low + high)
-        b_products((0, 1), low)
-        b_products((2, 3), high)
-        second_sizes((0, 1), turned)
+        opened = {}
+        for pair, letter in ((0, "A"), (1, "B")):
+            opened.update(new_banks(pair, letter))
+            for i in tiles_of(pair):
+                mx_pass(opened[i], "future", i, 0, True, False)
 
-        now_s.append(gather_scales(list_now, 1, "now_s_1", "future_w_1a"))
-        move_up(1)
-        future_s.append(gather_scales(list_future, 1, "future_s_1", "future_w_1b"))
-        future_w[0].extend(ahead + gather_words(list_future, 0, 768, S, "future_w_0b", "future_s_0"))
-        future_w[1].extend(gather_words(list_future, 1, 512, S, "future_w_1c"))
-        now_w[0].extend(gather_words(list_now, 0, 512, S, "now_w_0b", "c_0"))
-        now_w[1].extend(gather_words(list_now, 1, 512, S, "now_w_1b", "c_1"))
+        def close_future(pair):
+            for i in tiles_of(pair):
+                mx_pass(opened[i], "future", i, 1, False, True)
+                held["future"][i] = leave("future", i, opened[i], ACT.Copy, -1.0)
 
-        c_products(both_passes((4, 5)), low)
-        second_sizes((2, 3), spare)
-        c_products(both_passes((6, 7)), high)
-        b_products((4, 5), low)
-        b_products((6, 7), high)
-        second_sizes((4, 5), turned)
-        joint = {}
-        for i, tag in zip(REPEATED, spare):
-            joint[i] = new_bank(tag)
+        close_future(0)
+        products("now", 0, "C")
+        close_future(1)
+        products("now", 1, "A")
+        second[0] = sizes("future", 0, "D")
+
+        gather_scales("future", 1, "future_w_1_1")
+        gather_words("future", 0, 2, "future_s_0")
+        gather_words("future", 1, 2, "now_w_1_1")
+        gather_scales("now", 1, "future_w_1_0")
+        move_plane(1)
+        for a in range(PASSES):
+            gather_words("future", a, 3, "future_%d" % a)
+
+        products("future", 2, "C")
+        second[1] = sizes("future", 1, "B")
+        for a, tag in enumerate(("future_s_0", "now_w_1_1")):
+            gather_words("now", a, 2, tag)
+        products("future", 3, "D")
+        for a in range(PASSES):
+            gather_words("now", a, 3, "future_%d" % (2 + a))
+        products("now", 2, "A")
+        products("now", 3, "B")
+        second[2] = sizes("future", 2, "C")
+        joint = new_banks(LAST, "A")
+        for i in tiles_of(LAST):
             for a in range(PASSES):
-                b_pass(joint[i], i, a, a == 0, False)
-        second_sizes((6, 7), low)
+                mx_pass(joint[i], "now", i, a, a == 0, False)
+        second[3] = sizes("future", 3, "D")
 
         def quantize(codes, scales, values):
             nc.vector.quantize_mx(out=codes.bitcast(FP8X4), scales=scales, in_=values)
@@ -232,62 +233,49 @@ def tile_list_patch_motion_acceleration_kernel(
         w1_s = sb([P, PASSES, H], U8, "w1_s")
         w1_bf = []
         for a in range(PASSES):
-            w1_bf.append(sb([P, H, 4], BF16, "w1_bf_%d" % a, "c_%d" % (2 + a)))
+            w1_bf.append(sb([P, H, 4], BF16, "w1_bf_%d" % a, "future_%d" % a))
             nc.vector.tensor_scalar_mul(*woven(w1_bf[a][:], w1_raw[a][:]), -1.0)
         for a in range(PASSES):
             quantize(w1_codes[:, a, :], w1_s[:, a, :], w1_bf[a][:].rearrange("p c j -> p (c j)"))
 
-        past_s = [gather_scales(list_past, 0, "past_s_0", "c_2")]
-        early = sb([P, PASSES, S // 2], U32, "past_w_early", "c_3")
-        for start in (0, 256):
-            for a in range(PASSES):
-                gather(tab_w[a], U32, list_past, start, start + 256, early[:, a, start : start + 256])
-        past_w = [[early[:, a, P * i : P * (i + 1)] for i in range(HALF)] for a in range(PASSES)]
-        past_s.append(gather_scales(list_past, 1, "past_s_1", "c_4"))
+        gather_scales("past", 0, "future_0")
+        gather_words("past", 0, 0, "future_1")
+        gather_words("past", 1, 0, "w1_raw_0")
+        gather_words("past", 0, 1, "w1_raw_1")
+        gather_words("past", 1, 1, "future_4")
+        gather_scales("past", 1, "future_5")
         for a in range(PASSES):
-            past_w[a].extend(gather_words(list_past, a, 512, 768, "past_w_c%d" % a, "c_%d" % (5 + a)))
+            gather_words("past", a, 2, "future_%d" % (6 + a))
+
+        products("past", 0, "C")
+        products("past", 1, "B")
         wd_s = sb([P, N], U8, "wd_s")
-        wd_bf = sb([P, N, 4], BF16, "wd_bf", "c_7")
+        wd_bf = sb([P, N, 4], BF16, "wd_bf", "future_1")
         nc.vector.tensor_copy(*woven(wd_bf[:], wd_raw[:]))
-
-        terms = {}
-
-        def first_products(tiles, tags):
-            for i, tag in zip(tiles, tags):
-                bank = joint[i] if i in REPEATED else new_bank(tag)
-                for a in range(PASSES):
-                    a_pass(bank, i, a, a == 0 and i not in REPEATED)
-                a_sb = dealt_tile("a", i)
-                terms[i] = [a_sb]
-                if i in REPEATED:
-                    nc.scalar.activation(a_sb[:], dealt(bank), ACT.Abs)
-                elif i in ON_VECTOR:
-                    nc.vector.tensor_tensor(a_sb[:], dealt(bank), b_sb[i][:], ALU.add)
-                else:
-                    nc.scalar.copy(a_sb[:], dealt(bank))
-                    terms[i].append(b_sb[i])
-
-        first = {}
-
-        def first_sizes(tiles, tags):
-            first[tiles[0] // 2] = sb([P, 2, P, 4], F32, "first_%d" % tiles[0])
-            for i, tag in zip(tiles, tags):
-                nc.scalar.activation(first[i // 2][:, i % 2], turned_sum(tag, terms[i]), ACT.Abs)
+        gather_words("past", 0, 3, "w1_raw_0")
+        gather_words("past", 1, 3, "w1_raw_1")
+        first[0] = sizes("past", 0, "D")
+        products("past", 2, "C")
+        first[1] = sizes("past", 1, "B")
+        last = {}
+        for i in tiles_of(LAST):
+            for a in range(PASSES):
+                mx_pass(joint[i], "past", i, a, False, a == PASSES - 1)
+            last[i] = leave("last", i, joint[i], ACT.Abs, 1.0)
+        first[2] = sizes("past", 2, "D")
 
         out_rows = out.rearrange("(m p) j -> p m j", p=P)
+        h = {pair: sb([P, 2, P, 4], BF16, "h_%d" % pair) for pair in range(4)}
 
-        def difference(tiles):
-            h = sb([P, len(tiles), P, 4], BF16, "h_%d" % tiles[0])
-            part = slice(tiles[0] % 2, tiles[-1] % 2 + 1)
-            nc.vector.tensor_tensor(h[:], first[tiles[0] // 2][:, part], second[tiles[0] // 2][:, part], ALU.subtract)
-            return h
+        def difference(pair, part):
+            nc.vector.tensor_tensor(h[pair][:, part], first[pair][:, part], second[pair][:, part], ALU.subtract)
 
-        def decode(tiles, h, tags, copies):
-            width = P * len(tiles)
-            cols = slice(P * tiles[0], P * tiles[0] + width)
-            h_codes = sb([P, width], U32, "h_codes_%d" % tiles[0])
-            h_s = sb([P, width], U8, "h_s_%d" % tiles[0])
-            quantize(h_codes[:], h_s[:], h[:].rearrange("p f j t -> p (f j t)"))
+        def decode(pair, part, tags, copies):
+            width = P * (part.stop - part.start)
+            start = PAIR * pair + P * part.start
+            h_codes = sb([P, width], U32, "h_codes_%d" % start)
+            h_s = sb([P, width], U8, "h_s_%d" % start)
+            quantize(h_codes[:], h_s[:], h[pair][:, part].rearrange("p f j t -> p (f j t)"))
             per_bank = 4 // len(tags)
             for g in range(len(tags)):
                 o_bank = psum.tile([P, per_bank, width], F32, name="bank", tag=tags[g])
@@ -302,31 +290,23 @@ def tile_list_patch_motion_acceleration_kernel(
                         start=True,
                         stop=True,
                     )
-                o_sb = sb([P, per_bank, width], F32, "o_sb_%d_%d" % (tiles[0], g))
+                o_sb = sb([P, per_bank, width], F32, "o_sb_%d_%d" % (start, g))
                 copies[g](o_sb[:], o_bank[:])
-                nc.sync.dma_start(out_rows[:, per_bank * g : per_bank * (g + 1), cols], o_sb[:])
+                nc.sync.dma_start(out_rows[:, per_bank * g : per_bank * (g + 1), start : start + width], o_sb[:])
 
+        both, lower, upper = slice(0, 2), slice(0, 1), slice(1, 2)
         on_scalar = (nc.scalar.copy, nc.scalar.copy)
-        first_products((0, 1), spare)
-        first_products((2, 3), high)
-        h_01 = sb([P, 2, P, 4], BF16, "h_0")
-        sizes = [turned_sum(tag, terms[i]) for i, tag in zip(REPEATED, spare)]
-        for a in range(PASSES):
-            past_w[a].extend(gather_words(list_past, a, 768, S, "past_w_d%d" % a, "a_%d" % a))
-        for i in REPEATED:
-            nc.vector.tensor_tensor(h_01[:, i], sizes[i], second[0][:, i], ALU.subtract)
-        wd_codes = sb([P, N], U32, "wd_codes", "second_0")
+        difference(0, both)
+        wd_codes = sb([P, N], U32, "wd_codes", "size_past_0")
         quantize(wd_codes[:], wd_s[:], wd_bf[:].rearrange("p c t -> p (c t)"))
-        first_products((4, 5), low)
-        first_sizes((2, 3), turned)
-        first_products((6, 7), high)
-        decode((0, 1), h_01, spare, on_scalar)
-        first_sizes((4, 5), turned)
-        decode((2, 3), difference((2, 3)), spare, on_scalar)
-        first_sizes((6, 7), turned)
-        h_45 = difference((4, 5))
-        h_6 = difference((6,))
-        decode((4, 5), h_45, low, on_scalar)
-        h_7 = difference((7,))
-        decode((6,), h_6, ("product2",), (nc.scalar.copy,))
-        decode((7,), h_7, ("product3", "spare0"), (nc.vector.tensor_copy, nc.scalar.copy))
+        decode(0, both, ("C0", "C1"), on_scalar)
+        turned = {i: turned_sum(i, "B", [last[i]]) for i in tiles_of(LAST)}
+        difference(1, both)
+        difference(2, lower)
+        decode(1, both, ("A0", "A1"), on_scalar)
+        difference(2, upper)
+        nc.vector.tensor_tensor(h[LAST][:, 0], turned[6], second[LAST][:, 0], ALU.subtract)
+        decode(2, both, ("D0", "D1"), on_scalar)
+        nc.vector.tensor_tensor(h[LAST][:, 1], turned[7], second[LAST][:, 1], ALU.subtract)
+        decode(LAST, lower, ("C0",), (nc.scalar.copy,))
+        decode(LAST, upper, ("C1", "A0"), (nc.vector.tensor_copy, nc.scalar.copy))

@@ -21,7 +21,7 @@ P = 128
 PASSES = K // 512
 PAIR = 2 * P
 HALF = S // 2
-LAST = 3
+REPEATED = 3
 
 
 def tile_list_patch_motion_acceleration_kernel(
@@ -83,10 +83,12 @@ def tile_list_patch_motion_acceleration_kernel(
             offsets = lists[which][:, HALF * u // 16 : HALF * (u + 1) // 16]
             nc.vector.tensor_copy(planes[which, u][:], tab_s[:].indirect(offsets))
 
-        def gather_words(which, a, pair, tag=None):
-            words[which, a, pair] = sb([P, PAIR], U32, "%s_w_%d_%d" % (which, a, pair), tag)
-            offsets = lists[which][:, PAIR * pair // 16 : PAIR * (pair + 1) // 16]
-            nc.vector.tensor_copy(words[which, a, pair][:], tab_w[a][:].bitcast(U32).indirect(offsets))
+        def gather_words(which, a, pair, tag=None, pairs=1):
+            picked = sb([P, PAIR * pairs], U32, "%s_w_%d_%d" % (which, a, pair), tag)
+            offsets = lists[which][:, PAIR * pair // 16 : PAIR * (pair + pairs) // 16]
+            nc.vector.tensor_copy(picked[:], tab_w[a][:].bitcast(U32).indirect(offsets))
+            for n in range(pairs):
+                words[which, a, pair + n] = picked[:, PAIR * n : PAIR * (n + 1)]
 
         def move_plane(u):
             nc.sync.dma_start(moved[u][0:100, :].bitcast(I32), planes["now", u][4:104, :].bitcast(I32))
@@ -139,7 +141,10 @@ def tile_list_patch_motion_acceleration_kernel(
 
         def leave(name, i, bank, func, scale):
             copy = sb([P, 4, 16, 8], F32, "%s_%d" % (name, i))
-            nc.scalar.activation(copy[:], dealt(bank), func, scale=scale)
+            if func is None:
+                nc.scalar.copy(copy[:], dealt(bank))
+            else:
+                nc.scalar.activation(copy[:], dealt(bank), func, scale=scale)
             return copy
 
         def turned_sum(i, letter, terms):
@@ -157,71 +162,29 @@ def tile_list_patch_motion_acceleration_kernel(
             return bank[:].rearrange("p t j -> p j t")
 
         held = {"past": {}, "now": {}, "future": {}}
+        motion = {}
 
-        def products(which, pair, letter):
+        def products(which, pair, letter, on_vector=()):
             banks = new_banks(pair, letter)
             for i in tiles_of(pair):
                 for a in range(PASSES):
                     mx_pass(banks[i], which, i, a, a == 0, a == PASSES - 1)
-                held[which][i] = leave(which, i, banks[i], ACT.Copy, -1.0 if which == "future" else 1.0)
+                if i not in on_vector:
+                    held[which][i] = leave(which, i, banks[i], ACT.Copy if which == "future" else None, -1.0)
+            return banks
+
+        def subtract_on_vector(i, bank):
+            motion[i] = sb([P, 4, 16, 8], F32, "motion_%d" % i)
+            nc.vector.tensor_tensor(motion[i][:], dealt(bank), held["now"][i][:], ALU.add)
 
         def sizes(other, pair, letter):
             size = sb([P, 2, P, 4], F32, "size_%s_%d" % (other, pair))
             for i in tiles_of(pair):
-                nc.scalar.activation(size[:, i % 2], turned_sum(i, letter, [held["now"][i], held[other][i]]), ACT.Abs)
+                terms = [held["now"][i], held[other][i]] if i in held[other] else [motion[i]]
+                nc.scalar.activation(size[:, i % 2], turned_sum(i, letter, terms), ACT.Abs)
             return size
 
         second, first = {}, {}
-
-        gather_words("future", 0, 0)
-        gather_words("future", 0, 1)
-        gather_words("now", 0, 0)
-        gather_words("future", 1, 0)
-        gather_words("now", 1, 0)
-        gather_words("future", 1, 1)
-        gather_words("now", 0, 1, "future_w_1_0")
-        gather_words("now", 1, 1)
-
-        opened = {}
-        for pair, letter in ((0, "A"), (1, "B")):
-            opened.update(new_banks(pair, letter))
-            for i in tiles_of(pair):
-                mx_pass(opened[i], "future", i, 0, True, False)
-
-        def close_future(pair):
-            for i in tiles_of(pair):
-                mx_pass(opened[i], "future", i, 1, False, True)
-                held["future"][i] = leave("future", i, opened[i], ACT.Copy, -1.0)
-
-        close_future(0)
-        products("now", 0, "C")
-        close_future(1)
-        products("now", 1, "A")
-        second[0] = sizes("future", 0, "D")
-
-        gather_scales("future", 1, "future_w_1_1")
-        gather_words("future", 0, 2, "future_s_0")
-        gather_words("future", 1, 2, "now_w_1_1")
-        gather_scales("now", 1, "future_w_1_0")
-        move_plane(1)
-        for a in range(PASSES):
-            gather_words("future", a, 3, "future_%d" % a)
-
-        products("future", 2, "C")
-        second[1] = sizes("future", 1, "B")
-        for a, tag in enumerate(("future_s_0", "now_w_1_1")):
-            gather_words("now", a, 2, tag)
-        products("future", 3, "D")
-        for a in range(PASSES):
-            gather_words("now", a, 3, "future_%d" % (2 + a))
-        products("now", 2, "A")
-        products("now", 3, "B")
-        second[2] = sizes("future", 2, "C")
-        joint = new_banks(LAST, "A")
-        for i in tiles_of(LAST):
-            for a in range(PASSES):
-                mx_pass(joint[i], "now", i, a, a == 0, False)
-        second[3] = sizes("future", 3, "D")
 
         def quantize(codes, scales, values):
             nc.vector.quantize_mx(out=codes.bitcast(FP8X4), scales=scales, in_=values)
@@ -231,51 +194,25 @@ def tile_list_patch_motion_acceleration_kernel(
 
         w1_codes = sb([P, PASSES, H], U32, "w1_codes")
         w1_s = sb([P, PASSES, H], U8, "w1_s")
-        w1_bf = []
-        for a in range(PASSES):
-            w1_bf.append(sb([P, H, 4], BF16, "w1_bf_%d" % a, "future_%d" % a))
-            nc.vector.tensor_scalar_mul(*woven(w1_bf[a][:], w1_raw[a][:]), -1.0)
-        for a in range(PASSES):
-            quantize(w1_codes[:, a, :], w1_s[:, a, :], w1_bf[a][:].rearrange("p c j -> p (c j)"))
-
-        gather_scales("past", 0, "future_0")
-        gather_words("past", 0, 0, "future_1")
-        gather_words("past", 1, 0, "w1_raw_0")
-        gather_words("past", 0, 1, "w1_raw_1")
-        gather_words("past", 1, 1, "future_4")
-        gather_scales("past", 1, "future_5")
-        for a in range(PASSES):
-            gather_words("past", a, 2, "future_%d" % (6 + a))
-
-        products("past", 0, "C")
-        products("past", 1, "B")
         wd_s = sb([P, N], U8, "wd_s")
-        wd_bf = sb([P, N, 4], BF16, "wd_bf", "future_1")
-        nc.vector.tensor_copy(*woven(wd_bf[:], wd_raw[:]))
-        gather_words("past", 0, 3, "w1_raw_0")
-        gather_words("past", 1, 3, "w1_raw_1")
-        first[0] = sizes("past", 0, "D")
-        products("past", 2, "C")
-        first[1] = sizes("past", 1, "B")
-        last = {}
-        for i in tiles_of(LAST):
-            for a in range(PASSES):
-                mx_pass(joint[i], "past", i, a, False, a == PASSES - 1)
-            last[i] = leave("last", i, joint[i], ACT.Abs, 1.0)
-        first[2] = sizes("past", 2, "D")
-
         out_rows = out.rearrange("(m p) j -> p m j", p=P)
         h = {pair: sb([P, 2, P, 4], BF16, "h_%d" % pair) for pair in range(4)}
 
         def difference(pair, part):
             nc.vector.tensor_tensor(h[pair][:, part], first[pair][:, part], second[pair][:, part], ALU.subtract)
 
+        quantized = {}
+
+        def quantize_h(pair, part):
+            width = P * (part.stop - part.start)
+            start = PAIR * pair + P * part.start
+            quantized[start] = (sb([P, width], U32, "h_codes_%d" % start), sb([P, width], U8, "h_s_%d" % start))
+            quantize(quantized[start][0][:], quantized[start][1][:], h[pair][:, part].rearrange("p f j t -> p (f j t)"))
+
         def decode(pair, part, tags, copies):
             width = P * (part.stop - part.start)
             start = PAIR * pair + P * part.start
-            h_codes = sb([P, width], U32, "h_codes_%d" % start)
-            h_s = sb([P, width], U8, "h_s_%d" % start)
-            quantize(h_codes[:], h_s[:], h[pair][:, part].rearrange("p f j t -> p (f j t)"))
+            h_codes, h_s = quantized[start]
             per_bank = 4 // len(tags)
             for g in range(len(tags)):
                 o_bank = psum.tile([P, per_bank, width], F32, name="bank", tag=tags[g])
@@ -296,17 +233,121 @@ def tile_list_patch_motion_acceleration_kernel(
 
         both, lower, upper = slice(0, 2), slice(0, 1), slice(1, 2)
         on_scalar = (nc.scalar.copy, nc.scalar.copy)
-        difference(0, both)
-        wd_codes = sb([P, N], U32, "wd_codes", "size_past_0")
+
+
+        banks, joint, joined, w1_bf = {}, {}, {}, {}
+
+        def open_group(which, pair, letter):
+            banks.update(new_banks(pair, letter))
+            for i in tiles_of(pair):
+                mx_pass(banks[i], which, i, 0, True, False)
+
+        def close_group(which, pair):
+            for i in tiles_of(pair):
+                mx_pass(banks[i], which, i, 1, False, True)
+                held[which][i] = leave(which, i, banks[i], ACT.Copy if which == "future" else None, -1.0)
+
+        def open_joint(letter):
+            joint.update(new_banks(REPEATED, letter))
+            for i in tiles_of(REPEATED):
+                for a in range(PASSES):
+                    mx_pass(joint[i], "now", i, a, a == 0, False)
+
+        def close_joint():
+            for i in tiles_of(REPEATED):
+                for a in range(PASSES):
+                    mx_pass(joint[i], "past", i, a, False, a == PASSES - 1)
+                joined[i] = leave("joined", i, joint[i], ACT.Abs, 1.0)
+
+        def difference_from_bank(i):
+            nc.vector.tensor_tensor(h[REPEATED][:, i % 2], turned[i], second[REPEATED][:, i % 2], ALU.subtract)
+
+        def round_w1(a, tag):
+            w1_bf[a] = sb([P, H, 4], BF16, "w1_bf_%d" % a, tag)
+            nc.vector.tensor_scalar_mul(*woven(w1_bf[a][:], w1_raw[a][:]), -1.0)
+
+        def round_on_scalar(rounded, raw, quarter, scale):
+            cols = slice(P * quarter, P * (quarter + 1))
+            nc.scalar.activation(*woven(rounded[:, cols], raw[:, :, cols]), ACT.Copy, scale=scale)
+
+        gather_words("future", 0, 0)
+        gather_words("future", 0, 1)
+        gather_words("now", 0, 0)
+        gather_words("future", 1, 0)
+        gather_words("now", 1, 0)
+        gather_words("future", 1, 1)
+        gather_words("now", 0, 1, "future_w_1_0")
+        gather_words("now", 1, 1)
+        open_group("future", 0, "A")
+        open_group("future", 1, "B")
+        close_group("future", 0)
+        banks.update(products("now", 0, "C"))
+        close_group("future", 1)
+        banks.update(products("now", 1, "A"))
+        second[0] = sizes("future", 0, "D")
+        gather_scales("future", 1, "future_w_1_1")
+        gather_words("future", 0, 2, "future_s_0")
+        gather_words("future", 1, 2, "now_w_1_1")
+        gather_scales("now", 1, "future_w_1_0")
+        move_plane(1)
+        gather_words("future", 0, 3, "future_0")
+        gather_words("future", 1, 3, "moved_0")
+        w1_bf[1] = sb([P, H, 4], BF16, "w1_bf_1", "future_1")
+        banks.update(products("future", 2, "C"))
+        round_on_scalar(w1_bf[1], w1_raw[1], 0, -1.0)
+        second[1] = sizes("future", 1, "B")
+        round_on_scalar(w1_bf[1], w1_raw[1], 1, -1.0)
+        gather_words("now", 0, 2, "future_s_0")
+        gather_words("now", 1, 2, "now_w_1_1")
+        banks.update(products("future", 3, "D"))
+        round_on_scalar(w1_bf[1], w1_raw[1], 2, -1.0)
+        gather_words("now", 0, 3, "future_2")
+        gather_words("now", 1, 3, "future_3")
+        banks.update(products("now", 2, "A"))
+        round_on_scalar(w1_bf[1], w1_raw[1], 3, -1.0)
+        banks.update(products("now", 3, "B"))
+        second[2] = sizes("future", 2, "C")
+        open_joint("A")
+        second[3] = sizes("future", 3, "D")
+        round_w1(0, "future_0")
+        gather_scales("past", 0, "future_s_0")
+        quantize(w1_codes[:, 0, :], w1_s[:, 0, :], w1_bf[0][:].rearrange("p c j -> p (c j)"))
+        gather_words("past", 0, 0, "now_w_1_1")
+        gather_words("past", 1, 0, "future_0")
+        quantize(w1_codes[:, 1, :], w1_s[:, 1, :], w1_bf[1][:].rearrange("p c j -> p (c j)"))
+        gather_words("past", 0, 1, "future_4")
+        gather_words("past", 1, 1, "future_1")
+        gather_scales("past", 1, "future_6")
+        gather_words("past", 0, 2, "future_7")
+        banks.update(products("past", 0, "C"))
+        gather_words("past", 1, 2, "future_0")
+        banks.update(products("past", 1, "B"))
+        wd_bf = sb([P, N, 4], BF16, "wd_bf", "future_5")
+        nc.vector.tensor_copy(*woven(wd_bf[:], wd_raw[:]))
+        gather_words("past", 0, 3, "future_4")
+        gather_words("past", 1, 3, "future_1")
+        first[0] = sizes("past", 0, "D")
+        wd_codes = sb([P, N], U32, "wd_codes", "past_1")
         quantize(wd_codes[:], wd_s[:], wd_bf[:].rearrange("p c t -> p (c t)"))
-        decode(0, both, ("C0", "C1"), on_scalar)
-        turned = {i: turned_sum(i, "B", [last[i]]) for i in tiles_of(LAST)}
-        difference(1, both)
+        banks.update(products("past", 2, "C"))
+        first[1] = sizes("past", 1, "B")
+        close_joint()
+        first[2] = sizes("past", 2, "D")
+        difference(0, both)
+        difference(1, lower)
+        quantize_h(0, both)
+        decode(0, both, ("C0", "C1",), (nc.scalar.copy, nc.scalar.copy,))
+        turned = {i: turned_sum(i, "B", [joined[i]]) for i in tiles_of(REPEATED)}
+        difference(1, upper)
         difference(2, lower)
-        decode(1, both, ("A0", "A1"), on_scalar)
+        quantize_h(1, both)
+        decode(1, both, ("A0", "A1",), (nc.scalar.copy, nc.scalar.copy,))
         difference(2, upper)
-        nc.vector.tensor_tensor(h[LAST][:, 0], turned[6], second[LAST][:, 0], ALU.subtract)
-        decode(2, both, ("D0", "D1"), on_scalar)
-        nc.vector.tensor_tensor(h[LAST][:, 1], turned[7], second[LAST][:, 1], ALU.subtract)
-        decode(LAST, lower, ("C0",), (nc.scalar.copy,))
-        decode(LAST, upper, ("C1", "A0"), (nc.vector.tensor_copy, nc.scalar.copy))
+        difference_from_bank(6)
+        quantize_h(2, both)
+        decode(2, both, ("D0", "D1",), (nc.scalar.copy, nc.scalar.copy,))
+        difference_from_bank(7)
+        quantize_h(3, lower)
+        decode(3, lower, ("C0",), (nc.scalar.copy,))
+        quantize_h(3, upper)
+        decode(3, upper, ("C1", "A0",), (nc.vector.tensor_copy, nc.scalar.copy,))

@@ -285,9 +285,9 @@ def tile_list_patch_motion_acceleration_kernel(
         close_group("future", 1)
         banks.update(products("now", 1, "A"))
         second[0] = sizes("future", 0, "D")
-        gather_scales("future", 1, "future_w_1_1")
+        gather_scales("future", 1, "now_w_1_0")
         gather_words("future", 0, 2, "future_s_0")
-        gather_words("future", 1, 2, "now_w_1_1")
+        gather_words("future", 1, 2, "future_w_1_1")
         gather_scales("now", 1, "future_w_1_0")
         move_plane(1)
         gather_words("future", 0, 3, "future_0")
@@ -297,12 +297,10 @@ def tile_list_patch_motion_acceleration_kernel(
         round_on_scalar(w1_bf[1], w1_raw[1], 0, -1.0)
         second[1] = sizes("future", 1, "B")
         round_on_scalar(w1_bf[1], w1_raw[1], 1, -1.0)
-        gather_words("now", 0, 2, "future_s_0")
-        gather_words("now", 1, 2, "now_w_1_1")
+        gather_words("now", 0, 2, "future_s_0", 2)
+        gather_words("now", 1, 2, "future_w_1_1", 2)
         banks.update(products("future", 3, "D"))
         round_on_scalar(w1_bf[1], w1_raw[1], 2, -1.0)
-        gather_words("now", 0, 3, "future_2")
-        gather_words("now", 1, 3, "future_3")
         banks.update(products("now", 2, "A"))
         round_on_scalar(w1_bf[1], w1_raw[1], 3, -1.0)
         banks.update(products("now", 3, "B"))
@@ -310,22 +308,19 @@ def tile_list_patch_motion_acceleration_kernel(
         open_joint("A")
         second[3] = sizes("future", 3, "D")
         round_w1(0, "future_0")
-        gather_scales("past", 0, "future_s_0")
+        gather_scales("past", 0, "future_2")
         quantize(w1_codes[:, 0, :], w1_s[:, 0, :], w1_bf[0][:].rearrange("p c j -> p (c j)"))
-        gather_words("past", 0, 0, "now_w_1_1")
-        gather_words("past", 1, 0, "future_0")
-        quantize(w1_codes[:, 1, :], w1_s[:, 1, :], w1_bf[1][:].rearrange("p c j -> p (c j)"))
-        gather_words("past", 0, 1, "future_4")
-        gather_words("past", 1, 1, "future_1")
-        gather_scales("past", 1, "future_6")
-        gather_words("past", 0, 2, "future_7")
-        banks.update(products("past", 0, "C"))
-        gather_words("past", 1, 2, "future_0")
-        banks.update(products("past", 1, "B"))
-        wd_bf = sb([P, N, 4], BF16, "wd_bf", "future_5")
+        gather_words("past", 0, 0, "future_3", 2)
+        gather_words("past", 1, 0, "w8_w_0")
+        wd_bf = sb([P, N, 4], BF16, "wd_bf", "w1_raw_0")
         nc.vector.tensor_copy(*woven(wd_bf[:], wd_raw[:]))
-        gather_words("past", 0, 3, "future_4")
-        gather_words("past", 1, 3, "future_1")
+        quantize(w1_codes[:, 1, :], w1_s[:, 1, :], w1_bf[1][:].rearrange("p c j -> p (c j)"))
+        gather_words("past", 1, 1, "w1_raw_1")
+        gather_scales("past", 1, "future_1")
+        gather_words("past", 0, 2, "future_4", 2)
+        gather_words("past", 1, 2, "future_5", 2)
+        banks.update(products("past", 0, "C"))
+        banks.update(products("past", 1, "B"))
         first[0] = sizes("past", 0, "D")
         wd_codes = sb([P, N], U32, "wd_codes", "past_1")
         quantize(wd_codes[:], wd_s[:], wd_bf[:].rearrange("p c t -> p (c t)"))

@@ -260,7 +260,62 @@ def tile_list_patch_motion_acceleration_kernel(
                 joined[i] = leave("joined", i, joint[i], ACT.Abs, 1.0)
 
         def difference_from_bank(i):
-            nc.vector.tensor_tensor(h[REPEATED][:, i % 2], turned[i], second[REPEATED][:, i % 2], ALU.subtract)
+            turned = turning["joined", i][:].rearrange("p t j -> p j t")
+            nc.vector.tensor_tensor(h[REPEATED][:, i % 2], turned, second[REPEATED][:, i % 2], ALU.subtract)
+
+        turning, decoded = {}, {}
+
+        def turn(kind, i, tag, slices):
+            if slices[0] == 0:
+                turning[kind, i] = psum.tile([P, 4, P], F32, name="bank", tag=tag)
+            if kind == "joined":
+                terms = [joined[i]]
+            elif i in held[kind]:
+                terms = [held["now"][i], held[kind][i]]
+            else:
+                terms = [motion[i]]
+            for t in slices:
+                for n, term in enumerate(terms):
+                    nc.tensor.matmul(
+                        turning[kind, i][:, t, :],
+                        lhsT=term[:, t].rearrange("j g i -> j (g i)"),
+                        rhs=ident[:],
+                        is_transpose=True,
+                        start=(n == 0),
+                        stop=(n == len(terms) - 1),
+                    )
+
+        def take_size(kind, i):
+            sizes_of = second if kind == "future" else first
+            if i % 2 == 0:
+                sizes_of[i // 2] = sb([P, 2, P, 4], F32, "size_%s_%d" % (kind, i // 2))
+            nc.scalar.activation(sizes_of[i // 2][:, i % 2], turning[kind, i][:].rearrange("p t j -> p j t"), ACT.Abs)
+
+        def decode_products(pair, part, tags):
+            width = P * (part.stop - part.start)
+            start = PAIR * pair + P * part.start
+            h_codes, h_s = quantized[start]
+            per_bank = 4 // len(tags)
+            for g in range(len(tags)):
+                decoded[start, g] = psum.tile([P, per_bank, width], F32, name="bank", tag=tags[g])
+                for m in range(per_bank):
+                    rows = slice(P * (per_bank * g + m), P * (per_bank * g + m + 1))
+                    nc.tensor.matmul_mx(
+                        out=decoded[start, g][:, m, :],
+                        lhsT=wd_codes[:, rows].bitcast(FP8X4),
+                        lhsT_scale=wd_s[:, rows],
+                        rhs=h_codes[:].bitcast(FP8X4),
+                        rhs_scale=h_s[:],
+                        start=True,
+                        stop=True,
+                    )
+
+        def store(pair, part, g, copy):
+            start = PAIR * pair + P * part.start
+            per_bank, width = decoded[start, g].shape[1:]
+            o_sb = sb([P, per_bank, width], F32, "o_sb_%d_%d" % (start, g))
+            copy(o_sb[:], decoded[start, g][:])
+            nc.sync.dma_start(out_rows[:, per_bank * g : per_bank * (g + 1), start : start + width], o_sb[:])
 
         def round_w1(a, tag):
             w1_bf[a] = sb([P, H, 4], BF16, "w1_bf_%d" % a, tag)
@@ -296,15 +351,18 @@ def tile_list_patch_motion_acceleration_kernel(
         banks.update(products("future", 2, "C"))
         round_on_scalar(w1_bf[1], w1_raw[1], 0, -1.0)
         second[1] = sizes("future", 1, "B")
-        round_on_scalar(w1_bf[1], w1_raw[1], 1, -1.0)
         gather_words("now", 0, 2, "future_s_0", 2)
         gather_words("now", 1, 2, "future_w_1_1", 2)
         banks.update(products("future", 3, "D"))
-        round_on_scalar(w1_bf[1], w1_raw[1], 2, -1.0)
         banks.update(products("now", 2, "A"))
-        round_on_scalar(w1_bf[1], w1_raw[1], 3, -1.0)
         banks.update(products("now", 3, "B"))
-        second[2] = sizes("future", 2, "C")
+        round_on_scalar(w1_bf[1], w1_raw[1], 1, -1.0)
+        round_on_scalar(w1_bf[1], w1_raw[1], 2, -1.0)
+        turn("future", 4, "C0", (0, 1, 2, 3))
+        take_size("future", 4)
+        round_on_scalar(w1_bf[1], w1_raw[1], 3, -1.0)
+        turn("future", 5, "C1", (0, 1, 2, 3))
+        take_size("future", 5)
         open_joint("A")
         second[3] = sizes("future", 3, "D")
         round_w1(0, "future_0")
@@ -312,14 +370,17 @@ def tile_list_patch_motion_acceleration_kernel(
         quantize(w1_codes[:, 0, :], w1_s[:, 0, :], w1_bf[0][:].rearrange("p c j -> p (c j)"))
         gather_words("past", 0, 0, "future_3", 2)
         gather_words("past", 1, 0, "w8_w_0")
-        wd_bf = sb([P, N, 4], BF16, "wd_bf", "w1_raw_0")
-        nc.vector.tensor_copy(*woven(wd_bf[:], wd_raw[:]))
+        gather_words("past", 1, 1, "w8_w_1")
+        gather_words("past", 0, 2, "w8_s")
         quantize(w1_codes[:, 1, :], w1_s[:, 1, :], w1_bf[1][:].rearrange("p c j -> p (c j)"))
-        gather_words("past", 1, 1, "w1_raw_1")
-        gather_scales("past", 1, "future_1")
-        gather_words("past", 0, 2, "future_4", 2)
-        gather_words("past", 1, 2, "future_5", 2)
-        banks.update(products("past", 0, "C"))
+        gather_scales("past", 1, "w1_raw_1")
+        gather_words("past", 1, 2, "future_6")
+        gather_words("past", 0, 3, "future_7")
+        gather_words("past", 1, 3, "future_1")
+        open_group("past", 0, "C")
+        close_group("past", 0)
+        wd_bf = sb([P, N, 4], BF16, "wd_bf", "w8_w_0")
+        nc.vector.tensor_copy(*woven(wd_bf[:], wd_raw[:]))
         banks.update(products("past", 1, "B"))
         first[0] = sizes("past", 0, "D")
         wd_codes = sb([P, N], U32, "wd_codes", "past_1")
@@ -332,7 +393,8 @@ def tile_list_patch_motion_acceleration_kernel(
         difference(1, lower)
         quantize_h(0, both)
         decode(0, both, ("C0", "C1",), (nc.scalar.copy, nc.scalar.copy,))
-        turned = {i: turned_sum(i, "B", [joined[i]]) for i in tiles_of(REPEATED)}
+        turn("joined", 6, "B0", (0, 1, 2, 3))
+        turn("joined", 7, "B1", (0, 1, 2, 3))
         difference(1, upper)
         difference(2, lower)
         quantize_h(1, both)

@@ -317,6 +317,26 @@ def tile_list_patch_motion_acceleration_kernel(
             copy(o_sb[:], decoded[start, g][:])
             nc.sync.dma_start(out_rows[:, per_bank * g : per_bank * (g + 1), start : start + width], o_sb[:])
 
+        def round_on_vector(rounded, raw, quarter, scale):
+            cols = slice(P * quarter, P * (quarter + 1))
+            nc.vector.tensor_scalar_mul(*woven(rounded[:, cols], raw[:, :, cols]), scale)
+
+        def product(which, i, tag):
+            bank = psum.tile([P, H], F32, name="bank", tag=tag)
+            for a in range(PASSES):
+                mx_pass(bank, which, i, a, a == 0, a == PASSES - 1)
+            held[which][i] = leave(which, i, bank, ACT.Copy if which == "future" else None, -1.0)
+
+        def repeat_now(i, tag):
+            joint[i] = psum.tile([P, H], F32, name="bank", tag=tag)
+            for a in range(PASSES):
+                mx_pass(joint[i], "now", i, a, a == 0, False)
+
+        def join_past(i):
+            for a in range(PASSES):
+                mx_pass(joint[i], "past", i, a, False, a == PASSES - 1)
+            joined[i] = leave("joined", i, joint[i], ACT.Abs, 1.0)
+
         def round_w1(a, tag):
             w1_bf[a] = sb([P, H, 4], BF16, "w1_bf_%d" % a, tag)
             nc.vector.tensor_scalar_mul(*woven(w1_bf[a][:], w1_raw[a][:]), -1.0)
@@ -347,55 +367,48 @@ def tile_list_patch_motion_acceleration_kernel(
         move_plane(1)
         gather_words("future", 0, 3, "future_0")
         gather_words("future", 1, 3, "moved_0")
-        w1_bf[1] = sb([P, H, 4], BF16, "w1_bf_1", "future_1")
         banks.update(products("future", 2, "C"))
-        round_on_scalar(w1_bf[1], w1_raw[1], 0, -1.0)
         second[1] = sizes("future", 1, "B")
         gather_words("now", 0, 2, "future_s_0", 2)
         gather_words("now", 1, 2, "future_w_1_1", 2)
         banks.update(products("future", 3, "D"))
         banks.update(products("now", 2, "A"))
         banks.update(products("now", 3, "B"))
-        round_on_scalar(w1_bf[1], w1_raw[1], 1, -1.0)
-        round_on_scalar(w1_bf[1], w1_raw[1], 2, -1.0)
-        turn("future", 4, "C0", (0, 1, 2, 3))
-        take_size("future", 4)
-        round_on_scalar(w1_bf[1], w1_raw[1], 3, -1.0)
-        turn("future", 5, "C1", (0, 1, 2, 3))
-        take_size("future", 5)
+        second[2] = sizes("future", 2, "C")
         open_joint("A")
         second[3] = sizes("future", 3, "D")
-        round_w1(0, "future_0")
         gather_scales("past", 0, "future_2")
+        gather_words("past", 0, 0, "future_3")
+        round_w1(0, "future_0")
+        round_w1(1, "moved_0")
         quantize(w1_codes[:, 0, :], w1_s[:, 0, :], w1_bf[0][:].rearrange("p c j -> p (c j)"))
-        gather_words("past", 0, 0, "future_3", 2)
-        gather_words("past", 1, 0, "w8_w_0")
-        gather_words("past", 1, 1, "w8_w_1")
-        gather_words("past", 0, 2, "w8_s")
         quantize(w1_codes[:, 1, :], w1_s[:, 1, :], w1_bf[1][:].rearrange("p c j -> p (c j)"))
-        gather_scales("past", 1, "w1_raw_1")
-        gather_words("past", 1, 2, "future_6")
-        gather_words("past", 0, 3, "future_7")
-        gather_words("past", 1, 3, "future_1")
+        gather_words("past", 1, 0, "w8_w_0")
+        gather_words("past", 0, 1, "w8_w_1")
+        gather_words("past", 1, 1, "w8_s")
+        gather_scales("past", 1, "now_w_1_0")
+        gather_words("past", 0, 2, "w1_raw_0")
+        gather_words("past", 1, 2, "w1_raw_1")
+        gather_words("past", 0, 3, "future_0")
+        gather_words("past", 1, 3, "moved_0")
+        wd_bf = sb([P, N, 4], BF16, "wd_bf", "future_4")
+        nc.vector.tensor_copy(*woven(wd_bf[:], wd_raw[:]))
         open_group("past", 0, "C")
         close_group("past", 0)
-        wd_bf = sb([P, N, 4], BF16, "wd_bf", "w8_w_0")
-        nc.vector.tensor_copy(*woven(wd_bf[:], wd_raw[:]))
         banks.update(products("past", 1, "B"))
         first[0] = sizes("past", 0, "D")
-        wd_codes = sb([P, N], U32, "wd_codes", "past_1")
-        quantize(wd_codes[:], wd_s[:], wd_bf[:].rearrange("p c t -> p (c t)"))
         banks.update(products("past", 2, "C"))
+        difference(0, both)
         first[1] = sizes("past", 1, "B")
+        wd_codes = sb([P, N], U32, "wd_codes", "past_2")
+        quantize(wd_codes[:], wd_s[:], wd_bf[:].rearrange("p c t -> p (c t)"))
+        quantize_h(0, both)
         close_joint()
         first[2] = sizes("past", 2, "D")
-        difference(0, both)
-        difference(1, lower)
-        quantize_h(0, both)
         decode(0, both, ("C0", "C1",), (nc.scalar.copy, nc.scalar.copy,))
         turn("joined", 6, "B0", (0, 1, 2, 3))
         turn("joined", 7, "B1", (0, 1, 2, 3))
-        difference(1, upper)
+        difference(1, both)
         difference(2, lower)
         quantize_h(1, both)
         decode(1, both, ("A0", "A1",), (nc.scalar.copy, nc.scalar.copy,))

from contextlib import ExitStack

import concourse.mybir as mybir
from concourse.masks import make_identity

K, T, S, H, N = 1024, 2048, 1024, 512, 512
FLOPS = 2 * S * (3 * K * H + H * N)

F32 = mybir.dt.float32
BF16 = mybir.dt.bfloat16
I32 = mybir.dt.int32
U32 = mybir.dt.uint32
U16 = mybir.dt.uint16
U8 = mybir.dt.uint8
FP8X4 = mybir.dt.float8_e4m3fn_x4
FP4X4 = mybir.dt.float4_e2m1fn_x4
ACT = mybir.ActivationFunctionType
ALU = mybir.AluOpType

P = 128
PASSES = K // 512
PAIR = 2 * P
HALF = S // 2
REPEATED = 3


def tile_list_patch_motion_acceleration_kernel(
    tc, tab_words, tab_scales, offs, offs2, offs3, w1, w4_words, w4_scales, w8_words, w8_scales, wd, out
):
    nc = tc.nc
    with ExitStack() as ctx:
        keep = ctx.enter_context(tc.tile_pool(name="keep", bufs=1))
        psum = ctx.enter_context(tc.psum_pool(name="psum", bufs=1))

        def sb(shape, dtype, name, tag=None):
            return keep.tile(shape, dtype, name=name, tag=tag or name, align_bytes=64)

        lists = {
            "past": keep.tile([P, S // 16], U16, name="list_past"),
            "now": keep.tile([P, S // 16], U16, name="list_now"),
            "future": keep.tile([P, S // 16], U16, name="list_future"),
        }
        tab_w = [sb([P, T], I32, "tab_w_%d" % a) for a in range(PASSES)]
        tab_s = sb([P, T], U8, "tab_s")
        moved = [sb([P, HALF], U8, "moved_%d" % u) for u in range(2)]
        w4_w = sb([P, PASSES, 2 * H], U8, "w4_w")
        w4_s = sb([P, PASSES, H], U8, "w4_s")
        w8_w = [sb([P, H], I32, "w8_w_%d" % a) for a in range(PASSES)]
        w8_s = sb([P, H], U8, "w8_s")
        w1_raw = [sb([P, 4, H], F32, "w1_raw_%d" % a) for a in range(PASSES)]
        wd_raw = sb([P, 4, N], F32, "wd_raw")
        ident = sb([P, P], F32, "ident")

        nc.gpsimd.memset(tab_s[:].bitcast(I32), 0)
        make_identity(nc, ident[:])
        nc.vector.memset(w8_s[:].bitcast(I32), 0)
        nc.vector.memset(w4_s[:].bitcast(I32), 0)
        for u in range(2):
            nc.vector.memset(moved[u][96:P, :].bitcast(I32), 0)

        tab_rows = tab_words.rearrange("a p t i -> a p (t i)").bitcast(I32)
        w8_rows = w8_words.rearrange("a p e i -> a p (e i)").bitcast(I32)

        def load_packed_scales(plane, scales):
            for q in range(4):
                nc.sync.dma_start(
                    plane[32 * q : 32 * q + 4 * PASSES, :].bitcast(I32), scales[:, 4 * q : 4 * q + 4, :].bitcast(I32)
                )

        nc.sync.dma_start(lists["future"][:], offs3)
        nc.sync.dma_start(lists["now"][:], offs2)
        nc.sync.dma_start(w8_w[0][:], w8_rows[0])
        load_packed_scales(tab_s, tab_scales)
        nc.sync.dma_start(tab_w[0][:], tab_rows[0])
        load_packed_scales(w8_s, w8_scales)
        nc.sync.dma_start(tab_w[1][:], tab_rows[1])
        nc.sync.dma_start(w8_w[1][:], w8_rows[1])

        planes, words = {}, {}

        def gather_scales(which, u, tag=None):
            planes[which, u] = sb([P, HALF], U8, "%s_s_%d" % (which, u), tag)
            offsets = lists[which][:, HALF * u // 16 : HALF * (u + 1) // 16]
            nc.vector.tensor_copy(planes[which, u][:], tab_s[:].indirect(offsets))

        def gather_words(which, a, pair, tag=None, pairs=1):
            picked = sb([P, PAIR * pairs], U32, "%s_w_%d_%d" % (which, a, pair), tag)
            offsets = lists[which][:, PAIR * pair // 16 : PAIR * (pair + pairs) // 16]
            nc.vector.tensor_copy(picked[:], tab_w[a][:].bitcast(U32).indirect(offsets))
            for n in range(pairs):
                words[which, a, pair + n] = picked[:, PAIR * n : PAIR * (n + 1)]

        def move_plane(u):
            nc.sync.dma_start(moved[u][0:100, :].bitcast(I32), planes["now", u][4:104, :].bitcast(I32))

        gather_scales("future", 0)
        gather_scales("now", 0)
        move_plane(0)
        nc.sync.dma_start(w4_w[:].bitcast(I32), w4_words.rearrange("a p e -> p a e").bitcast(I32))
        for q in range(4):
            nc.sync.dma_start(
                w4_s[32 * q : 32 * q + 4, :, :].bitcast(I32),
                w4_scales[:, 4 * q : 4 * q + 4, :].rearrange("a r e -> r a e").bitcast(I32),
            )
        w1_rows = w1.rearrange("(a p j) c -> a p j c", p=P, j=4)
        for a in range(PASSES):
            nc.sync.dma_start(w1_raw[a][:], w1_rows[a])
        nc.sync.dma_start(lists["past"][:], offs)
        wd_rows = wd.rearrange("(g t i) n -> t g i n", t=4, i=8)
        for t in range(4):
            nc.sync.dma_start(wd_raw[:, t, :], wd_rows[t])

        def mx_pass(bank, which, i, a, start, stop):
            cols = slice(P * (i % 4), P * (i % 4 + 1))
            plane = planes[which, i // 4][4 * a :, cols]
            if which == "future":
                weights, weight_scales = w8_w[a][:].bitcast(FP8X4), w8_s[4 * a :, :]
            elif which == "past":
                weights, weight_scales = w1_codes[:, a, :].bitcast(FP8X4), w1_s[:, a, :]
            else:
                weights, weight_scales = w4_w[:, a, :].bitcast(FP4X4), w4_s[:, a, :]
                plane = [planes["now", i // 4], moved[i // 4]][a][:, cols]
            nc.tensor.matmul_mx(
                out=bank[:],
                lhsT=words[which, a, i // 2][:, P * (i % 2) : P * (i % 2 + 1)].bitcast(FP8X4),
                lhsT_scale=plane,
                rhs=weights,
                rhs_scale=weight_scales,
                start=start,
                stop=stop,
            )

        def tiles_of(pair):
            return (2 * pair, 2 * pair + 1)

        def new_banks(pair, letter):
            return {i: psum.tile([P, H], F32, name="bank", tag="%s%d" % (letter, i % 2)) for i in tiles_of(pair)}

        def dealt(bank):
            return bank[:].rearrange("j (g t i) -> j t g i", t=4, i=8)

        def leave(name, i, bank, func, scale):
            copy = sb([P, 4, 16, 8], F32, "%s_%d" % (name, i))
            if func is None:
                nc.scalar.copy(copy[:], dealt(bank))
            else:
                nc.scalar.activation(copy[:], dealt(bank), func, scale=scale)
            return copy

        def turned_sum(i, letter, terms):
            bank = psum.tile([P, 4, P], F32, name="bank", tag="%s%d" % (letter, i % 2))
            for t in range(4):
                for n, term in enumerate(terms):
                    nc.tensor.matmul(
                        bank[:, t, :],
                        lhsT=term[:, t].rearrange("j g i -> j (g i)"),
                        rhs=ident[:],
                        is_transpose=True,
                        start=(n == 0),
                        stop=(n == len(terms) - 1),
                    )
            return bank[:].rearrange("p t j -> p j t")

        held = {"past": {}, "now": {}, "future": {}}
        motion = {}

        def products(which, pair, letter, on_vector=()):
            banks = new_banks(pair, letter)
            for i in tiles_of(pair):
                for a in range(PASSES):
                    mx_pass(banks[i], which, i, a, a == 0, a == PASSES - 1)
                if i not in on_vector:
                    held[which][i] = leave(which, i, banks[i], ACT.Copy if which == "future" else None, -1.0)
            return banks

        def subtract_on_vector(i, bank):
            motion[i] = sb([P, 4, 16, 8], F32, "motion_%d" % i)
            nc.vector.tensor_tensor(motion[i][:], dealt(bank), held["now"][i][:], ALU.add)

        def sizes(other, pair, letter):
            size = sb([P, 2, P, 4], F32, "size_%s_%d" % (other, pair))
            for i in tiles_of(pair):
                terms = [held["now"][i], held[other][i]] if i in held[other] else [motion[i]]
                nc.scalar.activation(size[:, i % 2], turned_sum(i, letter, terms), ACT.Abs)
            return size

        second, first = {}, {}

        def quantize(codes, scales, values):
            nc.vector.quantize_mx(out=codes.bitcast(FP8X4), scales=scales, in_=values)

        def woven(grouped, raw):
            return grouped.rearrange("p (c i) t -> p c t i", i=4), raw.rearrange("p t (c i) -> p c t i", i=4)

        w1_codes = sb([P, PASSES, H], U32, "w1_codes")
        w1_s = sb([P, PASSES, H], U8, "w1_s")
        wd_s = sb([P, N], U8, "wd_s")
        out_rows = out.rearrange("(m p) j -> p m j", p=P)
        h = {pair: sb([P, 2, P, 4], BF16, "h_%d" % pair) for pair in range(4)}

        def difference(pair, part):
            nc.vector.tensor_tensor(h[pair][:, part], first[pair][:, part], second[pair][:, part], ALU.subtract)

        quantized = {}

        def quantize_h(pair, part):
            width = P * (part.stop - part.start)
            start = PAIR * pair + P * part.start
            quantized[start] = (sb([P, width], U32, "h_codes_%d" % start), sb([P, width], U8, "h_s_%d" % start))
            quantize(quantized[start][0][:], quantized[start][1][:], h[pair][:, part].rearrange("p f j t -> p (f j t)"))

        def decode(pair, part, tags, copies):
            width = P * (part.stop - part.start)
            start = PAIR * pair + P * part.start
            h_codes, h_s = quantized[start]
            per_bank = 4 // len(tags)
            for g in range(len(tags)):
                o_bank = psum.tile([P, per_bank, width], F32, name="bank", tag=tags[g])
                for m in range(per_bank):
                    rows = slice(P * (per_bank * g + m), P * (per_bank * g + m + 1))
                    nc.tensor.matmul_mx(
                        out=o_bank[:, m, :],
                        lhsT=wd_codes[:, rows].bitcast(FP8X4),
                        lhsT_scale=wd_s[:, rows],
                        rhs=h_codes[:].bitcast(FP8X4),
                        rhs_scale=h_s[:],
                        start=True,
                        stop=True,
                    )
                o_sb = sb([P, per_bank, width], F32, "o_sb_%d_%d" % (start, g))
                copies[g](o_sb[:], o_bank[:])
                nc.sync.dma_start(out_rows[:, per_bank * g : per_bank * (g + 1), start : start + width], o_sb[:])

        both, lower, upper = slice(0, 2), slice(0, 1), slice(1, 2)
        on_scalar = (nc.scalar.copy, nc.scalar.copy)


        banks, joint, joined, w1_bf = {}, {}, {}, {}

        def open_group(which, pair, letter):
            banks.update(new_banks(pair, letter))
            for i in tiles_of(pair):
                mx_pass(banks[i], which, i, 0, True, False)

        def close_group(which, pair):
            for i in tiles_of(pair):
                mx_pass(banks[i], which, i, 1, False, True)
                held[which][i] = leave(which, i, banks[i], ACT.Copy if which == "future" else None, -1.0)

        def open_joint(letter):
            joint.update(new_banks(REPEATED, letter))
            for i in tiles_of(REPEATED):
                for a in range(PASSES):
                    mx_pass(joint[i], "now", i, a, a == 0, False)

        def close_joint():
            for i in tiles_of(REPEATED):
                for a in range(PASSES):
                    mx_pass(joint[i], "past", i, a, False, a == PASSES - 1)
                joined[i] = leave("joined", i, joint[i], ACT.Abs, 1.0)

        def difference_from_bank(i):
            turned = turning["joined", i][:].rearrange("p t j -> p j t")
            nc.vector.tensor_tensor(h[REPEATED][:, i % 2], turned, second[REPEATED][:, i % 2], ALU.subtract)

        turning, decoded = {}, {}

        def turn(kind, i, tag, slices):
            if slices[0] == 0:
                turning[kind, i] = psum.tile([P, 4, P], F32, name="bank", tag=tag)
            if kind == "joined":
                terms = [joined[i]]
            elif i in held[kind]:
                terms = [held["now"][i], held[kind][i]]
            else:
                terms = [motion[i]]
            for t in slices:
                for n, term in enumerate(terms):
                    nc.tensor.matmul(
                        turning[kind, i][:, t, :],
                        lhsT=term[:, t].rearrange("j g i -> j (g i)"),
                        rhs=ident[:],
                        is_transpose=True,
                        start=(n == 0),
                        stop=(n == len(terms) - 1),
                    )

        def take_size(kind, i):
            sizes_of = second if kind == "future" else first
            if i % 2 == 0:
                sizes_of[i // 2] = sb([P, 2, P, 4], F32, "size_%s_%d" % (kind, i // 2))
            nc.scalar.activation(sizes_of[i // 2][:, i % 2], turning[kind, i][:].rearrange("p t j -> p j t"), ACT.Abs)

        def decode_products(pair, part, tags):
            width = P * (part.stop - part.start)
            start = PAIR * pair + P * part.start
            h_codes, h_s = quantized[start]
            per_bank = 4 // len(tags)
            for g in range(len(tags)):
                decoded[start, g] = psum.tile([P, per_bank, width], F32, name="bank", tag=tags[g])
                for m in range(per_bank):
                    rows = slice(P * (per_bank * g + m), P * (per_bank * g + m + 1))
                    nc.tensor.matmul_mx(
                        out=decoded[start, g][:, m, :],
                        lhsT=wd_codes[:, rows].bitcast(FP8X4),
                        lhsT_scale=wd_s[:, rows],
                        rhs=h_codes[:].bitcast(FP8X4),
                        rhs_scale=h_s[:],
                        start=True,
                        stop=True,
                    )

        def store(pair, part, g, copy):
            start = PAIR * pair + P * part.start
            per_bank, width = decoded[start, g].shape[1:]
            o_sb = sb([P, per_bank, width], F32, "o_sb_%d_%d" % (start, g))
            copy(o_sb[:], decoded[start, g][:])
            nc.sync.dma_start(out_rows[:, per_bank * g : per_bank * (g + 1), start : start + width], o_sb[:])

        def round_on_vector(rounded, raw, quarter, scale):
            cols = slice(P * quarter, P * (quarter + 1))
            nc.vector.tensor_scalar_mul(*woven(rounded[:, cols], raw[:, :, cols]), scale)

        def product(which, i, tag):
            bank = psum.tile([P, H], F32, name="bank", tag=tag)
            for a in range(PASSES):
                mx_pass(bank, which, i, a, a == 0, a == PASSES - 1)
            held[which][i] = leave(which, i, bank, ACT.Copy if which == "future" else None, -1.0)

        def repeat_now(i, tag):
            joint[i] = psum.tile([P, H], F32, name="bank", tag=tag)
            for a in range(PASSES):
                mx_pass(joint[i], "now", i, a, a == 0, False)

        def join_past(i):
            for a in range(PASSES):
                mx_pass(joint[i], "past", i, a, False, a == PASSES - 1)
            joined[i] = leave("joined", i, joint[i], ACT.Abs, 1.0)

        def round_w1(a, tag):
            w1_bf[a] = sb([P, H, 4], BF16, "w1_bf_%d" % a, tag)
            nc.vector.tensor_scalar_mul(*woven(w1_bf[a][:], w1_raw[a][:]), -1.0)

        def round_on_scalar(rounded, raw, quarter, scale):
            cols = slice(P * quarter, P * (quarter + 1))
            nc.scalar.activation(*woven(rounded[:, cols], raw[:, :, cols]), ACT.Copy, scale=scale)

        gather_words("future", 0, 0)
        gather_words("future", 0, 1)
        gather_words("now", 0, 0)
        gather_words("future", 1, 0)
        gather_words("now", 1, 0)
        gather_words("future", 1, 1)
        gather_words("now", 0, 1, "future_w_1_0")
        gather_words("now", 1, 1)
        open_group("future", 0, "A")
        open_group("future", 1, "B")
        close_group("future", 0)
        banks.update(products("now", 0, "C"))
        close_group("future", 1)
        banks.update(products("now", 1, "A"))
        second[0] = sizes("future", 0, "D")
        gather_scales("future", 1, "now_w_1_0")
        gather_words("future", 0, 2, "future_s_0")
        gather_words("future", 1, 2, "future_w_1_1")
        gather_scales("now", 1, "future_w_1_0")
        move_plane(1)
        gather_words("future", 0, 3, "future_0")
        gather_words("future", 1, 3, "moved_0")
        banks.update(products("future", 2, "C"))
        second[1] = sizes("future", 1, "B")
        gather_words("now", 0, 2, "future_s_0", 2)
        gather_words("now", 1, 2, "future_w_1_1", 2)
        banks.update(products("future", 3, "D"))
        banks.update(products("now", 2, "A"))
        banks.update(products("now", 3, "B"))
        second[2] = sizes("future", 2, "C")
        open_joint("A")
        second[3] = sizes("future", 3, "D")
        gather_scales("past", 0, "future_2")
        gather_words("past", 0, 0, "future_3")
        round_w1(0, "future_0")
        round_w1(1, "moved_0")
        quantize(w1_codes[:, 0, :], w1_s[:, 0, :], w1_bf[0][:].rearrange("p c j -> p (c j)"))
        quantize(w1_codes[:, 1, :], w1_s[:, 1, :], w1_bf[1][:].rearrange("p c j -> p (c j)"))
        gather_words("past", 1, 0, "w8_w_0")
        gather_words("past", 0, 1, "w8_w_1")
        gather_words("past", 1, 1, "w8_s")
        gather_scales("past", 1, "now_w_1_0")
        gather_words("past", 0, 2, "w1_raw_0")
        gather_words("past", 1, 2, "w1_raw_1")
        gather_words("past", 0, 3, "future_0")
        gather_words("past", 1, 3, "moved_0")
        wd_bf = sb([P, N, 4], BF16, "wd_bf", "future_4")
        nc.vector.tensor_copy(*woven(wd_bf[:], wd_raw[:]))
        open_group("past", 0, "C")
        close_group("past", 0)
        banks.update(products("past", 1, "B"))
        first[0] = sizes("past", 0, "D")
        banks.update(products("past", 2, "C"))
        difference(0, both)
        first[1] = sizes("past", 1, "B")
        wd_codes = sb([P, N], U32, "wd_codes", "past_2")
        quantize(wd_codes[:], wd_s[:], wd_bf[:].rearrange("p c t -> p (c t)"))
        quantize_h(0, both)
        close_joint()
        first[2] = sizes("past", 2, "D")
        decode(0, both, ("C0", "C1",), (nc.scalar.copy, nc.scalar.copy,))
        turn("joined", 6, "B0", (0, 1, 2, 3))
        turn("joined", 7, "B1", (0, 1, 2, 3))
        difference(1, both)
        difference(2, lower)
        quantize_h(1, both)
        decode(1, both, ("A0", "A1",), (nc.scalar.copy, nc.scalar.copy,))
        difference(2, upper)
        difference_from_bank(6)
        quantize_h(2, both)
        decode(2, both, ("D0", "D1",), (nc.scalar.copy, nc.scalar.copy,))
        difference_from_bank(7)
        quantize_h(3, lower)
        decode(3, lower, ("C0",), (nc.scalar.copy,))
        quantize_h(3, upper)
        decode(3, upper, ("C1", "A0",), (nc.vector.tensor_copy, nc.scalar.copy,))
